import numpy as np, ml_dtypes
CORES = [40,64,80,88,96,104,120,144]
N = 8
BF = ml_dtypes.bfloat16
def gentries(a):
    return np.ascontiguousarray(a.reshape(8, 16, -1).transpose(0, 2, 1)).reshape(8, -1)
def gtable(e):
    e = np.asarray(e); return np.ascontiguousarray(e.reshape(8, -1, 16).transpose(0, 2, 1)).reshape(128, -1).astype(np.int32)
V, TL, FM, LM = 2048, 4, 15, 768
NT = 8 // TL
def pick(a, i):
    return np.take_along_axis(a, i, -1)
def turn(x):
    return np.argsort(x, axis=-1)
def put(P, a, b, g, p):
    P[min(a, b), max(a, b), g] = p if a < b else turn(p)
def setw(W, a, b, t, w):
    W[min(a, b), max(a, b), t] = w
def same():
    P = np.empty((N, N, 8, V), np.int64); P[...] = np.arange(V)
    return P
def noise(rng, part):
    p = np.tile(np.arange(V), (len(part), 1))
    for i in range(len(part)):
        x = rng.permutation(V)[:max(2, int(part[i] * V))]; p[i, x] = np.roll(x, 1)
    return p
def twins(rng, share, n):
    return np.arange(V)[None, :] ^ np.repeat((rng.random((n, V // 2)) < share).astype(np.int64), 2, axis=1)
def swaps(n):
    p = np.arange(V); p[n] = n.reshape(-1, 2)[:, ::-1].reshape(-1)
    return p
def paired(rng, b):
    c = np.where(rng.random(b.shape) < 0.4, np.where(b < FM, b + 1, b - 1), b)
    f = np.tile(np.stack([b, c], -1).reshape(8, 16, V), (N, 1, 1, 1))
    return np.clip(f + (rng.random(f.shape) < 0.05) * rng.integers(-1, 2, f.shape), 0, FM)
def scene(rng, P, W, lo, hi):
    def good():
        return noise(rng, lo * (0.25 + 0.75 * rng.random(TL)))
    def bad():
        return noise(rng, hi + 0.2 * rng.random(TL))
    kinds = min(3, NT * (N // 4)); s = int(rng.integers(0, kinds))
    for t in range(NT):
        g = slice(t * TL, t * TL + TL)
        for a in range(N):
            for b in range(a + 1, N): put(P, a, b, g, bad())
        for q in range(N // 4):
            m = int(rng.integers(0, 4)); L = [4 * q + (i ^ m) for i in range(4)]; kind = (t * (N // 4) + q + s) % kinds
            if kind < 2:
                for i, k in (((0, 3), (3, 1), (1, 2)), ((0, 2), (2, 1), (1, 3)))[kind]: put(P, L[i], L[k], g, good())
            else:
                for i in range(4):
                    for k in range(i): put(P, L[i], L[k], g, good())
                x = twins(rng, 0.5, TL); put(P, L[0], L[2], g, x); put(P, L[1], L[3], g, x)
                setw(W, L[0], L[1], t, LM); setw(W, L[2], L[3], t, 0)
        if N == 8:
            for d in (4, 6):
                h = int(rng.integers(0, 2)); b = (2 * h) ^ int(rng.integers(0, 2)); put(P, b, b ^ (d + 1), g, good())
                a = 2 - 2 * h; x = twins(rng, 0.5, TL)
                put(P, a, a ^ d, g, good()); put(P, a ^ 1, a ^ 1 ^ d, g, good()); put(P, a, a ^ d ^ 1, g, x); put(P, a ^ 1, a ^ d, g, x)
                setw(W, a, a ^ d, t, LM); setw(W, a ^ 1, a ^ 1 ^ d, t, 0)
def pack(Q, f, P, W):
    ft = pick(f, Q[:, :, None, :]); back = turn(Q); X = np.empty((N, 8, N - 1, V), np.int64); lam = np.empty((N, NT, N - 1), np.int32)
    for a in range(N):
        for b in range(a + 1, N):
            x = pick(back[b], pick(P[a, b], Q[a])); d = a ^ b
            X[a, :, d - 1] = x; X[b, :, d - 1] = turn(x); lam[a, :, d - 1] = W[a, b]; lam[b, :, d - 1] = W[a, b]
    return {"ft": np.ascontiguousarray(ft.reshape(N, 128, V)).astype(np.float32).astype(BF), "mp": np.stack([gtable(x.reshape(8, -1)) for x in X]), "lam": lam}
def setup_inputs(rng):
    Q = np.argsort(rng.random((N, 8, V)), axis=-1); f = paired(rng, rng.integers(0, FM + 1, (8, 16, V // 2)))
    P = same(); W = rng.integers(0, LM + 1, (N, N, NT)); scene(rng, P, W, 0.04, 0.7)
    return pack(Q, f, P, W)
def setup_inputs_spread(rng):
    Q = np.argsort(rng.random((N, 8, V)), axis=-1)
    b = np.minimum(((FM + 1) * rng.random((8, 16, V // 2)) ** np.exp2(rng.integers(-2, 4, (8, 16, 1)))).astype(np.int64), FM); f = paired(rng, b)
    P = same(); W = np.clip(np.exp2(rng.random((N, N, NT)) * np.log2(LM + 2.0)).astype(np.int64) - 1, 0, LM); scene(rng, P, W, 0.06, 0.55)
    return pack(Q, f, P, W)
def setup_inputs_ends(rng):
    h = V // 2; x = np.arange(V)
    f = np.tile(FM * ((x & 1) ^ rng.integers(0, 2, (8, 16, 1))), (N, 1, 1, 1))
    Q = np.empty((N, 8, V), np.int64); Q[..., 0::2] = 2 * np.argsort(rng.random((N, 8, h)), axis=-1); Q[..., 1::2] = 2 * np.argsort(rng.random((N, 8, h)), axis=-1) + 1
    P = same(); W = LM * rng.integers(0, 2, (N, N, NT))
    for a in range(N):
        for b in range(a + 1, N):
            k = (a ^ b) & 1
            P[a, b, :, 0::2] = 2 * np.argsort(rng.random((8, h)), axis=-1) + k; P[a, b, :, 1::2] = 2 * np.argsort(rng.random((8, h)), axis=-1) + 1 - k
            for g in range(8):
                m = int(rng.choice(np.array([0, 0, 1, 3, V // 16]))); i = 2 * rng.permutation(h)[:m]; o = 2 * rng.permutation(h)[:m] + 1
                u = P[a, b, g, i].copy(); P[a, b, g, i] = P[a, b, g, o]; P[a, b, g, o] = u
    for r in range(N): setw(W, r, r ^ 1, slice(0, NT), LM); setw(W, r, r ^ 2, slice(0, NT), 0)
    L = N - 4
    for g in range(8 - TL, 8):
        o = 2 * int(rng.integers(0, h)) + 1; y = 2 * int(rng.integers(1, V // 8)); z = h + 2 * int(rng.integers(0, V // 8))
        t02 = 2 * int(rng.integers(0, h)); t12 = 2 * int(rng.integers(0, h)) + 1; t23 = o; t03 = o + y + t02; t13 = o + z + t12
        t01 = t03 - t23 - t12 + (0 if g == 8 - TL else y)
        for i, k, s in ((0, 1, t01), (0, 2, t02), (0, 3, t03), (1, 2, t12), (1, 3, t13), (2, 3, t23)): P[L + i, L + k, g] = (x + s) % V
    for i, k, w in ((0, 1, LM), (0, 2, LM), (0, 3, 0), (1, 2, 0), (1, 3, 0), (2, 3, LM)): setw(W, L + i, L + k, NT - 1, w)
    return pack(Q, f, P, W)
def plain(rng):
    x = np.arange(V); e = x.copy(); e[0] = V - 1; e[V - 1] = 0
    S = [x, x[::-1], (x + 1) % V, (x - 1) % V, x ^ 1, e]
    Q = np.tile(x, (N, 8, 1)); P = same(); W = rng.choice(np.array([0, 1, LM - 1, LM]), (N, N, NT))
    for a in range(N):
        for b in range(a + 1, N):
            for g in range(8):
                i = int(rng.integers(0, 8)); P[a, b, g] = S[i] if i < 6 else rng.permutation(V)
    f = rng.integers(0, FM + 1, (N, 8, 16, V)); k = rng.permutation(8)
    f[:, k[0]] = FM * rng.integers(0, 2, (N, 16, 1)); f[:, k[1]] = FM * (x == V - 1); f[:, k[2]] = x * (FM + 1) // V; f[:, k[3]] = FM * rng.integers(0, 2, (N, 16, V)); f[:, k[4]] = f[:1, k[4]]
    return Q, f, P, W
def late(rng, f, P, W):
    x = np.arange(V); S = [x, x[::-1], (x + 1) % V, (x - 1) % V, x ^ 1]; k = int(rng.integers(0, TL)); ramp = x * (FM + 1) // V
    for g in range(TL):
        if g == k:
            p, q, a, y, o = [rng.permutation(V) for i in range(5)]; s = np.empty(V, np.int64); s[o] = np.roll(o, -1)
            b = a[p[swaps(o[[0, 2]])[turn(q)]]]; M = (p, q, a[p[s]], y, a, b)
            e = np.where(rng.random((16, 1)) < 0.5, ramp, FM - ramp)
            f[0, g] = e[:, q]; f[1, g] = e[:, q[turn(p)]]; f[2:4, g] = FM * rng.integers(0, 2, (2, 16, 1))
        else:
            c = [S[int(rng.integers(0, 5))] for i in range(4)]; M = [c[j][turn(c[i])] for i, j in ((0, 1), (0, 2), (0, 3), (1, 2), (1, 3), (2, 3))]
        for n, (i, j) in enumerate(((0, 1), (0, 2), (0, 3), (1, 2), (1, 3), (2, 3))): put(P, i, j, g, M[n])
    for i, j in ((0, 1), (0, 2), (1, 2), (1, 3), (2, 3)): setw(W, i, j, 0, 0)
    setw(W, 0, 3, 0, int(rng.choice(np.array([1, LM]))))
def edge(rng, f, P, W):
    x = np.arange(V); S = [x, x[::-1], (x + 1) % V, (x - 1) % V, x ^ 1]; L = N - 4; k = 8 - TL + int(rng.integers(0, TL))
    for g in range(8 - TL, 8):
        a = S[int(rng.integers(0, 5))]; h = S[int(rng.integers(0, 5))]; s = S[int(rng.integers(1, 5))]; t = x; u = x
        if g == k:
            c = 4 * (1 + rng.permutation(V // 4 - 1)[:14]); n = np.concatenate([np.array([0]), c[:7]]); m = c[7:]
            rest = rng.permutation(np.setdiff1d(x, np.concatenate([n, m])))
            o = np.concatenate([n[[1, 0, 2, 4, 6]], rest[:V // 2], n[[3, 5, 7]], m[[0, 1, 2, 4]], rest[V // 2:], m[[3, 5, 6]]])
            s = np.empty(V, np.int64); s[o] = np.roll(o, -1)
            m = np.concatenate([m[:6], np.array([0]), m[6:]]); t = swaps(n); u = swaps(m); a = rng.permutation(V); h = rng.permutation(V)
            for r, q, w in ((L, a, n), (L + 2, h, m)):
                y = rng.integers(0, FM + 1, (16, V))
                for i in range(4):
                    z = (LM // 64 + i) // 4; lo = rng.integers(0, FM + 1 - z, 16); y[:, w[2 * i]] = lo; y[:, w[2 * i + 1]] = lo + z
                f[r, g] = y; f[r + 1, g] = y[:, turn(q)]
        for i, j, p in ((0, 1, a[t]), (0, 2, x), (0, 3, h), (1, 2, turn(a)), (1, 3, h[s[turn(a)]]), (2, 3, h[u])): put(P, L + i, L + j, g, p)
    setw(W, L, L + 1, NT - 1, LM); setw(W, L + 2, L + 3, NT - 1, LM - 1)
def setup_inputs_shapes(rng):
    Q, f, P, W = plain(rng); late(rng, f, P, W); edge(rng, f, P, W)
    return pack(Q, f, P, W)
def setup_inputs_corners(rng):
    Q, f, P, W = plain(rng); x = np.arange(V); e = x.copy(); e[0] = V - 1; e[V - 1] = 0
    for a in range(4):
        for b in range(a + 1, 4): P[a, b, :TL] = x
    n = rng.permutation(V // 2)[:2]; P[0, 1, :TL] = x[::-1]; P[1, 3, :TL] = swaps(n); f[:4, :TL] = FM; setw(W, 0, 1, 0, 1)
    m = 3 * V // 4 - 2; k = int(rng.integers(0, TL)); rest = np.setdiff1d(x, n)
    for g in range(TL):
        o = rng.permutation(rest)
        o = np.concatenate([n[:1], o[:m - 1]]) if g == k else np.concatenate([n[:1], o[:m // 2], n[1:], o[m // 2:m - 2]])
        p = x.copy(); p[o] = np.roll(o, -1); P[2, 3, g] = p
    setw(W, 2, 3, 0, 0); setw(W, 1, 3, 0, int(rng.choice(np.array([1, LM]))))
    L = N - 4
    for a in range(L, N):
        for b in range(a + 1, N): P[a, b, 8 - TL:] = x
    f[L:, 8 - TL:] = rng.integers(0, FM + 1, (TL, 16, V)); f[L:, 7, :, 0] = 0; f[L:, 7, :, V - 1] = FM
    P[N - 2, N - 1, 7] = e; setw(W, N - 2, N - 1, NT - 1, 0)
    return pack(Q, f, P, W)
def setup_inputs_calm(rng):
    Q = np.empty((N, 8, V), np.int64); Q[..., :V - 1] = np.argsort(rng.random((N, 8, V - 1)), axis=-1); Q[..., V - 1] = V - 1
    f = np.tile(rng.integers(0, FM + 1, (8, 16, V)), (N, 1, 1, 1)); f[:, :, 8:] = rng.integers(0, FM + 1, (N, 8, 8, V))
    P = same(); W = rng.integers(0, LM + 1, (N, N, NT))
    fours = [(4 * q, 2) for q in range(N // 4)] + ([(0, 4), (2, 4), (0, 6), (2, 6)] if N == 8 else [])
    for t in range(NT):
        ids = rng.permutation(V - 1)[:8 * len(fours)]
        for n in range(len(fours)):
            r, d = fours[n]; L = [r, r ^ 1, r ^ d, r ^ d ^ 1]; g = t * TL + int(rng.integers(0, TL)); z = int(rng.integers(1, FM + 1))
            u = ids[8 * n:8 * n + 4].copy(); w = ids[8 * n + 4:8 * n + 8].copy()
            if n == 0: u[0] = V - 1
            p = np.arange(V); p[u] = w; p[w] = u; P[min(L[0], L[3]), max(L[0], L[3]), g] = p; P[min(L[1], L[2]), max(L[1], L[2]), g] = p
            for i in range(4):
                a, b = int(u[i]), int(w[i]); lo = int(rng.integers(0, FM + 1 - z))
                f[:, g, :, b] = f[:, g, :, a]; f[:, g, i, a] = lo; f[:, g, i, b] = lo + z
            if d == 2: setw(W, L[0], L[1], t, 2 * z - int(rng.integers(0, 2))); setw(W, L[2], L[3], t, 2 * z - int(rng.integers(0, 2)))
            k = int(rng.integers(0, 2)); setw(W, L[0], L[2], t, 2 * z + k); setw(W, L[1], L[3], t, 2 * z + 1 - k)
            k = int(rng.integers(0, 2)); setw(W, L[0], L[3], t, 2 * z - k); setw(W, L[1], L[2], t, 2 * z - 1 + k)
    return pack(Q, f, P, W)
def check_inputs(d):
    bad = []
    f = np.asarray(d["ft"]).astype(np.float64)
    if not np.all((f >= 0) & (f <= FM) & (f == np.floor(f))): bad.append("range of ft")
    m = np.asarray(d["mp"]).astype(np.int64); w = np.asarray(d["lam"]).astype(np.int64)
    if np.min(w) < 0 or np.max(w) > LM: bad.append("range of lam")
    if any(np.any(w[r, :, k - 1] != w[r ^ k, :, k - 1]) for r in range(N) for k in range(1, N)): bad.append("lam differs between the two ranks of a pair")
    if np.min(m) < 0 or np.max(m) > V - 1: bad.append("range of mp")
    else:
        X = [gentries(a).astype(np.int64).reshape(8, N - 1, V) for a in m]
        if any(np.any(pick(X[r ^ k][:, k - 1], X[r][:, k - 1]) != np.arange(V)) for r in range(N) for k in range(1, N)): bad.append("mp: a map is not the inverse of its partner's")
    return bad
def reference(ft, mp, lam):
    F = ft.astype(np.float32).astype(np.int32).reshape(N, 8, 16, V); S = F - np.roll(F, -1, axis=3)
    X = {}
    for r in range(N):
        x = gentries(mp[r]).astype(np.int64).reshape(8, N - 1, V)
        for d in range(1, N): X[r, r ^ d] = x[:, d - 1]
    for d in range(1, N):
        e = 2 if d == 1 else 1
        for r in range(N):
            j = r ^ d
            if r > j: continue
            C = [X[r, j]] + [pick(X[k, j], X[r, k]) for k in (r ^ e, j ^ e)]
            score = []
            for c in range(3):
                G = pick(F[j], C[c][:, None, :]); A = np.abs(S[r] - (G - np.roll(G, -1, axis=2)))
                A = np.add.reduce(A.reshape(NT, -1), axis=1, dtype=np.int64); D = np.zeros(NT, np.int64)
                for o in range(3): D = D + np.add.reduce((C[c] != C[o]).reshape(NT, -1), axis=1, dtype=np.int64)
                score.append(A + lam[r][:, d - 1].astype(np.int64) * D)
            win = np.argmin(np.stack(score), axis=0)
            X[r, j] = np.stack(C)[np.repeat(win, TL), np.arange(8)]; X[j, r] = turn(X[r, j])
    ym = np.stack([gtable(np.stack([X[r, r ^ d] for d in range(1, N)], axis=1).reshape(8, -1)) for r in range(N)])
    return {"ym": ym.astype(np.float32)}

@@ -1,0 +1,706 @@
+from concourse.bass import DstId, RemoteDMATransfer
+from concourse.mybir import AluOpType as A, AxisListType, ActivationFunctionType as AF
+
+V, H, N = 2048, 1024, 8
+POS = {1: 0, 2: 1, 4: 2, 6: 3, 3: 4, 5: 5, 7: 6}
+HB = 1536
+NG = 5
+CYCLE, GATHER, WAKE, HOP, LOOK = 0.00104, 1.56, 0.06, 4.0, 0.8
+SHY, IDLE, SMALL, TRIES, SEED, MEMO = 5.0, 2.0, 8.0, 1500, 1, {}
+SUB = ((3, 2), (5, 2), (7, 2), (6, 2), (7, 1))
+HALF = {6: 0, 3: 1, 5: 2, 7: 3}
+
+SCRATCH = {
+    "stF": ("dram", [8, 128, 256], "bfloat16"), "ldF": ("dram", [8, 128, 256], "bfloat16"),
+    "stM": ("dram", [8, 128, 128], "int32"), "ldM": ("dram", [8, 128, 128], "int32"),
+    "stO": ("dram", [8, 128, 160], "float16"), "ldO": ("dram", [8, 128, 160], "float16"),
+    "Fall": ("sbuf", [128, 8 * V + 16], "bfloat16"), "OF": ("sbuf", [128, 7 * 66], "float16"),
+    "SH": ("sbuf", [128, 3 * H], "bfloat16"), "GB": ("sbuf", [128, NG * 1056], "bfloat16"),
+    "FH": ("sbuf", [128, 4 * 1040], "bfloat16"),
+    "Wall": ("sbuf", [128, 896], "int32"), "W16": ("sbuf", [128, 896], "float16"), "H16": ("sbuf", [128, 896], "float16"),
+    "OWi": ("sbuf", [128, 896], "int32"), "OW": ("sbuf", [128, 896], "float16"),
+    "TB": ("sbuf", [128, V], "int32"), "TP": ("sbuf", [128, V], "float32"),
+    "RA": ("sbuf", [128, V], "float16"), "RB": ("sbuf", [128, V], "float16"), "RU": ("sbuf", [128, V], "float16"),
+    "RS": ("sbuf", [128, V], "float32"), "RT": ("sbuf", [128, V], "float32"),
+    "PW": ("sbuf", [128, 256], "float16"), "UW": ("sbuf", [128, 768], "float16"), "TW": ("sbuf", [128, 768], "float16"),
+    "EW": ("sbuf", [128, 384], "float16"), "OM": ("sbuf", [128, 1280], "float16"), "OI": ("sbuf", [128, 1280], "float16"),
+    "W32": ("sbuf", [128, 128], "float32"), "WI": ("sbuf", [128, 384], "int32"), "PH": ("sbuf", [128, 128], "float16"),
+    "SL": ("sbuf", [128, 9 * 128], "uint16"), "FL": ("sbuf", [128, 21 * 66], "uint16"),
+    "CT": ("sbuf", [128, 768], "float16"), "ZH": ("sbuf", [128, 128], "float16"), "ZF": ("sbuf", [128, 32], "float32"),
+    "NE": ("sbuf", [128, 768], "bfloat16"), "DG": ("sbuf", [128, 18 * 128], "float16"),
+    "MH": ("sbuf", [128, 25 * 128], "float16"), "MB": ("sbuf", [128, 18 * 128], "bfloat16"), "MF": ("sbuf", [128, 22 * 128], "float32"),
+    "IR": ("sbuf", [128, 128], "bfloat16"), "GM": ("sbuf", [128, 128], "bfloat16"),
+    "CI": ("sbuf", [128, 8], "int32"), "CF": ("sbuf", [128, 96], "float32"),
+    "LMi": ("sbuf", [128, 8], "int32"), "LMf": ("sbuf", [128, 8], "float32"),
+    "ACC": ("sbuf", [128, 24], "float32"), "PR": ("sbuf", [128, 24], "float32"), "SM": ("sbuf", [128, 128], "float32"),
+    "X1": ("sbuf", [128, 16], "float32"), "X2": ("sbuf", [128, 48], "float32"), "X3": ("sbuf", [128, 96], "float32"),
+    "YO": ("sbuf", [128, 896], "float32"),
+    "PF0": ("psum", [128, H], "float32"), "PF1": ("psum", [128, H], "float32"),
+    "PA": ("psum", [128, 512], "float32"), "PB": ("psum", [128, 512], "float32"),
+    "PC": ("psum", [128, 512], "float32"), "PD": ("psum", [128, 512], "float32"),
+}
+SEMAPHORES = ["cv", "cs", "cp", "cg", "out", "aF", "aM", "aO", "a1", "a2", "a3", "rF", "rM", "rO", "r3",
+              "sF", "sM", "sN", "ownF", "ownM", "ow", "wall", "tb1", "tb2", "fall", "lm", "pi", "tu2", "tu4", "tu6",
+              "sO", "ownO", "oi", "y1", "y2", "y3"] + ["ft%d" % d for d in range(1, 8)] + ["fh%d" % d for d in HALF]
+
+
+def top(d):
+    return 1 << (d.bit_length() - 1)
+
+
+def bits(engines):
+    return sum(1 << e for e in engines)
+
+
+def plan(T, topo):
+    cores = list(T.cores)
+    teams = [[r for r in range(N) if r == 0 or topo.may_write(cores[0], cores[r])]]
+    teams.append([r for r in range(N) if r not in teams[0]])
+    layer = {r: 4 * t + i for t in range(2) for i, r in enumerate(teams[t])}
+    relay = {}
+    for r in range(N):
+        far = teams[1 - layer[r] // 4]
+        ports = [c for c in topo.cores_of(cores[r]) if c != cores[r] and all(topo.may_write(c, cores[x]) for x in far)]
+        ports.sort(key=lambda c: topo.die(c) != topo.die(cores[r]))
+        for i, x in enumerate(far):
+            relay[r, x] = ports[i]
+    return cores, teams, layer, relay
+
+
+def dst(topo, to, frm):
+    rid, pid = topo.addr(to, frm)
+    return DstId(rid=rid, pnc=pid)
+
+
+def relay_program(g, core, T, topo, cores, layer, a, x):
+    to = cores[x]
+    en = topo.engines(core, to)
+    wide = len(topo.engines(cores[a], core))
+    s = 12 * layer[a]
+    steps = (("rM", wide // 4, "aM", T.ldM[0], T.ldM[a]), ("rF", wide // 4, "aF", T.ldF[0], T.ldF[a]),
+             ("rO", wide // 4, "aO", T.ldO[0], T.ldO[layer[a]]), ("r3", wide, "a3", T.X3[:, 0:9], T.X3[:, s:s + 9]))
+    for here, n, there, src, out in steps:
+        g.wait_ge(T.sem[here], n)
+        g.remote_dma_fused([RemoteDMATransfer(dst_ids=[dst(topo, to, core)], dma_engine_mask=bits(en), remote_sem=T.sem[there],
+                                              src=src, dst=out)], local_sem=T.sem.out)
+    g.wait_ge(T.sem.out, len(steps) * len(en))
+
+
+def rank_program(g, core, T, topo):
+    cores, teams, layer, relay = plan(T, topo)
+    me = T.rank_of(core)
+    if me is None:
+        for (a, x), c in relay.items():
+            if c == core:
+                relay_program(g, core, T, topo, cores, layer, a, x)
+        return
+    lay = layer[me]
+    team = lay // 4
+    near = [r for r in teams[team] if r != me]
+    far = teams[1 - team]
+    Q = {"v": g.vector, "s": g.scalar, "p": g.tensor, "g": g, "y": g.sync}
+    ops, wr, rd, users, phys = [], {}, {}, {}, {}
+    pools = {"b": [(T[x], 0) for x in ("PA", "PB", "PC", "PD")], "f": [(T.PF0, 0), (T.PF1, 0)],
+             "G": [(T.GB, 1056 * i) for i in range(NG)], "c": [(T.CT, 0), (T.CT, 384)],
+             "r": [(T.RA, 0), (T.RB, 0), (T.RU, 0)], "R": [(T.RS, 0), (T.RT, 0)]}
+
+    def new(pool):
+        k = "%s#%d" % (pool, len(users)); users[k] = []
+        return k
+
+    def step(e, R, W, busy, late, issue, sem=None):
+        deps = set(wr[k] for k in R + W if k in wr)
+        for k in W:
+            deps |= set(rd.get(k, []))
+        i = len(ops)
+        ops.append(dict(e=e, deps=deps, busy=busy, late=late, issue=issue, sem=sem, takes=[k for k in W if users.get(k) == []]))
+        for k in R:
+            rd.setdefault(k, []).append(i)
+        for k in W:
+            wr[k] = i; rd[k] = []
+        for k in set(R + W):
+            if k in users:
+                users[k].append(i)
+
+    def part(k, a, b, s=1):
+        return (k, a, b, s)
+
+    def ap(x):
+        if isinstance(x, tuple):
+            t, o = phys[x[0]]
+            return t[:, o + x[1]:o + x[2]:x[3]] if x[3] > 1 else t[:, o + x[1]:o + x[2]]
+        return x
+
+    def do(e, R, W, n, call):
+        step(e, R, W, max(64, n) * CYCLE, 0.0, lambda q: [call(q)])
+
+    def dma(e, s, R, W, pairs, kb, rows):
+        step(e, R, W, 0.1 * len(pairs), (kb, rows), lambda q: [Q[q].dma_start(o, i) for o, i in pairs], s)
+
+    sent = [0]
+
+    def send(R, W, items, busy=0.3):
+        def issue(q):
+            g.remote_dma_fused([RemoteDMATransfer(dst_ids=[dst(topo, c, core) for c in cs], dma_engine_mask=bits(en), remote_sem=T.sem[s],
+                                                  src=src, dsts=[out for c in cs]) for cs, en, s, src, out in items], local_sem=T.sem.out)
+            return []
+        sent[0] += sum(len(it[1]) for it in items)
+        step("g", R, W + ["gq"], busy, 0.0, issue, "out")
+
+    def arrive(s, n, R, W, late):
+        step("net", R, W, 0.0, late, n, s)
+
+    vv, sc, pe = g.vector, g.scalar, g.tensor
+
+    def ts(R, W, o, i, s1, s2, op0, op1=None, n=64):
+        if op1 is None:
+            do("v", R, W, n, lambda q: vv.tensor_scalar(ap(o), ap(i), s1, None, op0))
+        else:
+            do("v", R, W, n, lambda q: vv.tensor_scalar(ap(o), ap(i), s1, s2, op0, op1))
+
+    def tt(R, W, o, a, b, op, n=64):
+        do("v", R, W, n, lambda q: vv.tensor_tensor(ap(o), ap(a), ap(b), op))
+
+    def cp(R, W, o, i, e="v", n=64):
+        do(e, R, W, n, lambda q: vv.tensor_copy(ap(o), ap(i)) if q == "v" else sc.activation(ap(o), ap(i), AF.Copy))
+
+    def mm(R, W, items, n):
+        step("p", R, W, n * CYCLE / 2, 0.0, lambda q: [pe.matmul(ap(o), ap(l), ap(r), a, z) for o, l, r, a, z in items])
+
+    def blk(t, i, n=1, w=128):
+        return part(t, i * w, (i + n) * w) if isinstance(t, str) else t[:, i * w:(i + n) * w]
+
+    def best_order():
+        if "bias" not in MEMO:
+            bias = [SMALL if o["busy"] < 0.6 else 0.0 for o in ops]
+            best, seed = order(bias)[0], SEED
+            for _ in range(TRIES):
+                new_ = list(bias)
+                for i, o in enumerate(ops):
+                    seed = (seed * 1103515245 + 12345) % 2147483648
+                    if (seed >> 4) % 1000 < (40 if o["busy"] > 0.6 else 6):
+                        new_[i] += ((seed >> 14) % 1000) / 1000.0 * 20.0 - 10.0
+                t = order(new_)[0]
+                if t is not None and t <= best:
+                    best, bias = t, new_
+            MEMO["bias"] = bias; MEMO["time"] = best
+        _, seq, extra, where = order(MEMO["bias"])
+        phys.update(where)
+        for i, more in extra.items():
+            ops[i]["deps"] = ops[i]["deps"] | more
+        return seq
+
+    def order(bias):
+        n = len(ops); extra, where, since = {}, {}, {}
+        after = [[] for _ in ops]
+        for i, o in enumerate(ops):
+            for d in o["deps"]:
+                after[d].append(i)
+        span = lambda o: o["busy"] + (2.0 + o["late"][0] / 250.0 if isinstance(o["late"], tuple) else o["late"]) + WAKE
+        rank = [0.0] * n
+        for i in range(n - 1, -1, -1):
+            rank[i] = span(ops[i]) + max([rank[j] for j in after[i]] + [0.0])
+        left = [len(o["deps"]) for o in ops]
+        ready = [i for i in range(n) if not left[i]]
+        end, free, pipe, seq = {}, {}, [0.0], []
+        slots = {p: [None] * len(v) for p, v in pools.items()}
+        open_ = {k: len(v) for k, v in users.items()}
+        uses = {}
+        for k, v in users.items():
+            for i in v:
+                uses.setdefault(i, []).append(k)
+        while ready:
+            cand = []
+            for i in ready:
+                o = ops[i]; got = []
+                if i not in since:
+                    since[i] = max([end[d] + WAKE for d in o["deps"]] + [0.0])
+                t = since[i]
+                for k in o["takes"]:
+                    fr = [(max(end[u] for u in users[h]) if h else 0.0, x) for x, h in enumerate(slots[k[0]]) if h is None or not open_[h]]
+                    if not fr:
+                        break
+                    got.append((k, min(fr)[1])); t = max(t, min(fr)[0] + WAKE)
+                else:
+                    for q in (o["e"] if o["e"] == "vs" else [o["e"]]):
+                        cand.append((max(t, free.get(q, 0.0)) if q != "net" else t, q, i, got))
+            if not cand:
+                return None, None, None, None
+            t0, q0 = min((c[0], c[1]) for c in cand)
+            t, q, i, got = max([c for c in cand if c[1] == q0 and c[0] <= t0 + LOOK],
+                               key=lambda c: rank[c[2]] + bias[c[2]] - IDLE * (c[0] - t0) - (SHY if c[1] == "v" and ops[c[2]]["e"] == "vs" else 0.0))
+            o = ops[i]; ready.remove(i)
+            for k, x in got:
+                h = slots[k[0]][x]
+                if h:
+                    extra[i] = extra.get(i, set()) | set(users[h])
+                slots[k[0]][x] = k; where[k] = pools[k[0]][x]
+            free[q] = t + o["busy"]
+            if isinstance(o["late"], tuple):
+                pipe[0] = max(pipe[0], t + 1.8) + o["late"][0] / 320.0 + o["late"][1] * 0.0025
+                end[i] = pipe[0]
+            else:
+                end[i] = free[q] + o["late"]
+            for k in uses.get(i, []):
+                open_[k] -= 1
+            seq.append((i, q))
+            for j in after[i]:
+                left[j] -= 1
+                if not left[j]:
+                    ready.append(j)
+        return max(end.values()), seq, extra, where
+
+    def emit(seq):
+        count, seen, tok = {}, {}, {}
+        total = {}
+        for o in ops:
+            if isinstance(o["late"], tuple):
+                total[o["sem"]] = total.get(o["sem"], 0) + 16 * int(round(o["busy"] * 10))
+        for i, q in seq:
+            o = ops[i]
+            if q == "net":
+                tok[i] = (o["sem"], o["issue"]); count[o["sem"]] = o["issue"]
+                continue
+            want = {}
+            for d in o["deps"]:
+                if tok[d]:
+                    want[tok[d][0]] = max(want.get(tok[d][0], 0), tok[d][1])
+            for s, k in want.items():
+                if seen.get((q, s), 0) < k:
+                    Q[q].wait_ge(T.sem[s], k); seen[q, s] = k
+            s = o["sem"] or "c" + q
+            for ins in o["issue"](q):
+                ins.then_inc(T.sem[s], 16 if o["sem"] else 1); count[s] = count.get(s, 0) + (16 if o["sem"] else 1)
+            tok[i] = None if s == "out" else (s, total.get(s, count[s]))
+        count["out"] = sent[0]
+        for s, k in count.items():
+            g.wait_ge(T.sem[s], k)
+
+    for t, sm, sf in ((1 - team, "sM", "sF"), (team, "sN", "sN")):
+        l = 4 * t
+        dma("y", sm, [], [sm + "a", "yq"], [(T.stM[l:l + 4, 0:112, :], T.mp[16 * l:16 * l + 64, :])], 0, 0)
+        dma("s", sm, [], [sm + "b"],
+            [(T.stM[k, 112, 0:7], T.lam[t]) for k in range(l, l + 4) if k != lay]
+            + [(T.stM[l:l + 4, 112, 7:128], T.mp[0:4, 0:121]), (T.stM[l:l + 4, 113:128, :], T.mp[0:60, 0:128])], 224, 64)
+        dma("y", sf, [], [sf + "c"], [(T.stF[l:l + 4], T.ft[16 * l:16 * l + 64, :])], 256, 16)
+    dma("y", "ownM", [], ["ownM"], [(T.ldM[me, 0:112, :], T.mp[16 * lay:16 * lay + 16, :]), (T.ldM[me, 112, 0:7], T.lam[team])], 56, 16)
+    dma("y", "ownF", [], ["ownF"], [(T.ldF[me], T.ft[16 * lay:16 * lay + 16, :])], 64, 16)
+    do("g", [], ["pi0", "gq"], 130, lambda q: g.iota(T.CI[:, 0:1], [[0, 1]], 0, 1))
+    do("g", [], ["IR"], 400, lambda q: g.iota(T.IR[:], [[1, 128]], 0, 0, allow_small_or_imprecise_dtypes=True))
+    do("g", [], ["GM"], 400, lambda q: g.iota(T.GM[:], [[16, 8], [0, 16]], 0, 0, allow_small_or_imprecise_dtypes=True))
+    on = topo.engines(core, relay[me, far[0]])
+    off = topo.engines(core, cores[near[0]])
+    nof, q4 = len(off), len(on) // 4
+    for keys, sem, st, ld in ((["sMa", "sMb"], "rM", T.stM, T.ldM), (["sFc"], "rF", T.stF, T.ldF)):
+        send(keys, [sem], [([relay[me, x]], on[q4 * i:q4 * i + q4], sem, st[layer[x]], ld[0]) for i, x in enumerate(far)], 3.0 if sem == "rM" else 0.3)
+    send(["sNa", "sNb", "sNc"], ["sent"], [([cores[x]], off[2 * i + k:2 * i + k + 1], sem, st[layer[x]], ld[me])
+                                           for i, x in enumerate(near) for k, (sem, st, ld) in enumerate((("aM", T.stM, T.ldM), ("aF", T.stF, T.ldF)))])
+    do("g", ["sent"], ["TB"], 4200, lambda q: g.iota(T.TB[:], [[0, V]], 0, 0))
+    do("g", ["sent"], ["TP"], 4200, lambda q: g.iota(T.TP[:], [[0, V]], 0, 0, allow_small_or_imprecise_dtypes=True))
+    arrive("aM", 3 + 4 * nof, ["rM"], ["ldM"], 8.0)
+    arrive("aF", 3 + 4 * nof, ["rF"], ["ldF"], 9.0)
+
+    CF = T.CF
+    for j in range(3):
+        ts(["pi0"], ["ci%d" % j], T.CI[:, 1 + j:2 + j], T.CI[:, 0:1], 4 + j, 1, A.logical_shift_right, A.bitwise_and)
+    ts(["pi0"], ["ci3"], T.CI[:, 4:5], T.CI[:, 0:1], 15, None, A.bitwise_and)
+    cp(["pi0", "ci0", "ci1", "ci2", "ci3"], ["c0"], CF[:, 0:5], T.CI[:, 0:5])
+    XO, PX, GX, QM, IS, IN, QT, NI, I2 = 8, 16, 32, 40, 56, 64, 72, 80, 88
+    col = lambda base, i: CF[:, base + i:base + i + 1]
+    ts(["c0"], ["xo0"], col(XO, 0), col(0, 0), 0.0, None, A.mult)
+    for j in range(3):
+        ts(["c0"], ["xo%d" % (1 << j)], col(XO, 1 << j), col(1, j), -32.0 * (1 << j), 16.0 * (1 << j), A.mult, A.add)
+    ts(["c0"], ["isr"], CF[:, 5:8], CF[:, 1:4], -1.0, 1.0, A.mult, A.add)
+    ts(["c0"], ["nisr"], CF[:, NI:NI + 3], CF[:, 1:4], 1.0, None, A.subtract)
+    ts(["c0", "IR"], ["qm"], CF[:, QM:QM + 16], T.IR[:, 0:16], col(0, 4), None, A.is_equal)
+    ts(["c0"], ["p16"], col(QT, 4), col(0, 0), 16.0, None, A.mult)
+    tt(["xo1", "xo2"], ["xo3"], col(XO, 3), col(XO, 1), col(XO, 2), A.add)
+    ts(["xo1", "xo2", "xo3", "xo4"], ["xo5"], CF[:, XO + 5:XO + 8], CF[:, XO + 1:XO + 4], col(XO, 4), None, A.add)
+    xo = ["xo%d" % i for i in range(6)]
+    ts(xo + ["c0"], ["px"], CF[:, PX:PX + 8], CF[:, XO:XO + 8], col(0, 0), None, A.add)
+    ts(["px"], ["gx"], CF[:, GX:GX + 8], CF[:, PX:PX + 8], col(0, 4), None, A.subtract)
+    tb = {1: 0, 2: 1, 4: 2}
+    isr = lambda d: col(5, tb[top(d)])
+    nisr = lambda d: col(NI, tb[top(d)])
+    for i, d in enumerate((3, 5, 6, 7)):
+        ts(["c0"] + xo, ["qt%d" % d], col(QT, i), col(XO, d ^ top(d)), col(1, tb[top(d)]), col(0, 0), A.mult, A.add)
+    ts(["gx"], ["ind0"], CF[:, IN:IN + 8], CF[:, GX:GX + 8], 16.0 * me, None, A.is_equal)
+    mats, used = {}, {"MH": 0, "MB": 0, "MF": 0, "ZH": 0, "ZF": 0}
+    cols = ["px", "gx", "qm", "isr", "nisr", "IR", "GM", "p16", "qt3", "qt5", "qt6", "qt7", "ind"]
+
+    def mat(name, buf, row, s1, s2, op0=A.is_equal, parts=128):
+        o = 128 * used[buf]; used[buf] += 1
+        mats[name] = (buf, o)
+        ts(cols, [name], T[buf][0:parts, o:o + 128], row[0:parts, :], s1, s2, op0, A.mult)
+
+    def M(name, parts=128):
+        buf, o = mats[name]
+        return T[buf][0:parts, o:o + 128]
+
+    def smat(x):
+        mat("A%d" % x, "MH", IR, col(PX, x), 128.0)
+        mat("B%d" % x, "MH", IR, col(PX, x), -2047.0)
+
+    def zmat(q, x, buf="ZH"):
+        name = "Z%d_%d" % (q, x); o = 8 * used[buf]; used[buf] += 1
+        mats[name] = (buf, o)
+        ts(cols, [name], T[buf][:, o:o + 8], GM[:, 0:128:16], col(GX, x), col(QM, q), A.is_equal, A.mult)
+
+    IR, GM = T.IR, T.GM
+    smat(2); smat(3)
+    for t in (1, 2, 4):
+        mat("D%d" % t, "MH", IR, col(PX, 0), isr(t))
+    for d in range(1, 8):
+        mat("P%d" % d, "MH", IR, col(PX, d), isr(d))
+    mat("I", "MB", IR, col(PX, 0), 1.0)
+    mat("nI", "MB", IR, col(PX, 0), -1.0)
+    for t in (1, 2, 4):
+        mat("bD%d" % t, "MB", IR, col(PX, 0), isr(t)); mat("nD%d" % t, "MB", IR, col(PX, 0), nisr(t))
+        mat("bP%d" % t, "MB", IR, col(PX, t), isr(t)); mat("nP%d" % t, "MB", IR, col(PX, t), nisr(t))
+    zmat(2, 2); zmat(1, 3)
+    mat("I16", "MH", IR, col(PX, 0), 1.0)
+    mat("ET", "MF", GM, CF[0:8, QT + 4:QT + 5], 1.0, parts=8)
+    for d, p in POS.items():
+        cp(["isr"], ["is%d" % d], col(IS, p), isr(d))
+    for i, d in enumerate((3, 5, 6, 7)):
+        mat("Q%d" % d, "MB", IR, col(QT, i), 1.0)
+    for x in (1, 4, 5, 6, 7):
+        smat(x)
+    for q in (2, 4, 6, 1, 3, 5, 7, 8, 9):
+        zmat(q, 1)
+    ONS = (7, 4, 6)
+    for x in range(2, 8):
+        zmat(0, x, "ZF" if x in ONS else "ZH")
+    for x in range(8):
+        mat("S%d" % x, "MF", GM, col(GX, x), 1.0)
+    for x, y in ((0, 1), (0, 2), (0, 4), (0, 6), (1, 3), (1, 5), (1, 7)):
+        mats["S%d_%d" % (x, y)] = ("MF", 128 * used["MF"]); used["MF"] += 1
+        tt(["S%d" % x, "S%d" % y], ["S%d_%d" % (x, y)], M("S%d_%d" % (x, y)), M("S%d" % x), M("S%d" % y), A.add, n=256)
+    ts(["ind0"], ["ind"], CF[:, I2:I2 + 8], CF[:, IN:IN + 8], col(IN, 0), None, A.add)
+    for d in (3, 5, 7):
+        mat("O%d_0" % d, "MF", GM, 64.0, col(I2, d), op0=A.is_lt)
+        mat("O%d_1" % d, "MF", GM, 64.0, col(I2, d), op0=A.is_ge)
+
+    LM, LF = ["ldM", "ownM"], ["ldF", "ownF"]
+    dma("y", "wall", LM, ["Wall"], [(T.Wall[:], T.ldM[:, 0:112, :])], 448, 128)
+    dma("s", "tb1", LM, ["TB"], [(T.TB[q:128:16, :], T.ldM[:, q:112:7, :]) for q in (2, 1)], 128, 256)
+    dma("s", "lm", LM, ["LMi"], [(T.LMi[0:8, 0:7], T.ldM[:, 112, 0:7])], 0, 16)
+    dma("y", "fall", LF, ["Fall"], [(T.Fall[:, 0:V], T.ldF[:])], 512, 128)
+
+    def load_ft(d):
+        at = V + 16 + V * POS[d]
+        do("v", [], ["FT%d" % d], H, lambda q: vv.memset(T.Fall[:, at:at + V], 0.0))
+        ts(["IR"], ["of%d" % d], blk(T.OF, POS[d], 1, 66), IR[:, 0:66], 0.0, float(at), A.mult, A.add)
+        pairs, a = [], 0
+        while a < N:
+            b = a + 1
+            if not a & top(d):
+                while b < N and not b & top(d) and b ^ d == (b - 1 ^ d) + 1:
+                    b += 1
+                pairs.append((T.Fall[16 * a:16 * b, at:at + V], T.ldF[a ^ d:(a ^ d) + b - a]))
+            a = b
+        dma("y", "ft%d" % d, LF, ["FT%d" % d], pairs, 256, 64)
+
+    turn = {"d": 0}
+
+    def lists(c, items):
+        b = new("b"); its = []; R = []
+        first = POS[items[0][0]] + 7 * c
+        for i, (d, buf, k, key) in enumerate(items):
+            o, s = i * 66, k * 128
+            its += [(part(b, o, o + 66), M("D%d" % top(d)), blk(T.OF, POS[d], 1, 66), True, False),
+                    (part(b, o, o + 66), M("D%d" % top(d)), buf[:, s:s + 66], False, False),
+                    (part(b, o, o + 64), M("P%d" % d), buf[:, s + 64:s + 128], False, False),
+                    (part(b, o + 64, o + 66), M("P%d" % d), buf[:, s:s + 2], False, True)]
+            R += [key, "D%d" % top(d), "P%d" % d, "of%d" % d]
+        n = len(items) * 66
+        mm(R, [b], its, 4 * n)
+        cp([], [b] + ["FL%d_%d" % (it[0], c) for it in items], T.FL[:, first * 66:first * 66 + n], part(b, 0, n), n=n)
+
+    def slists(slot, items):
+        b = new("b"); its = []; R = []
+        for i, (x, u, h, keys) in enumerate(items):
+            its += [(blk(b, i), M("A%d" % x), u, True, False), (blk(b, i), M("B%d" % x), h, False, True)]
+            R += keys + ["A%d" % x, "B%d" % x]
+        n = len(items)
+        mm(R, [b], its, 256 * n)
+        ts([], [b] + ["SL%d" % (slot + i) for i in range(n)], blk(T.SL, slot, n), blk(b, 0, n), float(2047 * HB), None, A.add, n=128 * n)
+
+    def compose(e, win, slot, keys):
+        row = new("r" if e == "v" else "R")
+        cp(keys + ["SL%d" % slot], [row], part(row, 0, V), T[win][:, 0:V].indirect(blk(T.SL, slot)), e, n=V * GATHER)
+        return row
+
+    def extract(row, zs):
+        b = new("b"); n = len(zs)
+        buf, o = mats[zs[0]]
+        mm([row] + list(zs), [b], [(part(b, s, 128 * n, 16), part(row, s, V, 16), T[buf][:, o:o + 8 * n], True, True) for s in range(16)],
+           1024 if row[0] == "r" else 4096)
+        c = new("c")
+        cp([], [b, c], blk(c, 0, n), blk(b, 0, n), n=128 * n)
+        b = new("b")
+        mm([c, "I16"], [b], [(blk(b, i), blk(c, i), M("I16"), True, True) for i in range(n)], 128 * n)
+        return b
+
+    def take(b, i, n, out, keys):
+        cp([], [b] + keys, out, blk(b, i, n), n=128 * n)
+
+    def judge(d, c):
+        G = new("G")
+        o = (POS[d] + 7 * c) * 66
+        src = T.Fall[:, 0:2 * V + 16 + V * POS[d]].indirect(T.FL[:, o:o + 65])
+        R = ["Fall", "Fw", "FL%d_%d" % (d, c)] + ["FT%d" % x for x in POS if POS[x] <= POS[d]]
+        sub = (d, c) in SUB
+        if sub:
+            tt(R + ["FH%d" % d], [G], part(G, 0, 1040), src, blk(T.FH, HALF[d], 1, 1040), A.subtract, n=1040 * GATHER)
+        else:
+            cp(R, [G], part(G, 0, 1040), src, "vs", n=1040 * GATHER)
+        pf = new("f")
+        m = "I" if d == top(d) else "Q%d" % d
+        t = tb[top(d)]; its = []
+        for k in (0, 512):
+            o = part(pf, k, k + 512)
+            its += [] if sub else [(o, M(m), T.SH[:, t * H + k:t * H + k + 512], True, False)]
+            its += [(o, M("I"), part(G, k, k + 512), sub, False), (o, M("nI"), part(G, k + 1, k + 513), False, True)]
+        mm([G, "I", "nI"] + ([] if sub else ["SH%d" % t, m]), [pf], its, 512 * len(its))
+        acc = T.ACC[:, 3 * POS[d] + c:3 * POS[d] + c + 1]; src = part(pf, 0, H)
+        do("vs", [], [pf, G, "ACC%d_%d" % (d, c)], H,
+           lambda q: vv.tensor_reduce(acc, ap(src), AxisListType.X, A.add, apply_absolute_value=True) if q == "v"
+           else sc.activation(ap(part(G, 0, H)), ap(src), AF.Abs, accum_out=acc))
+
+    def steps_of_r(t):
+        pf = new("f")
+        its = []; F = T.Fall
+        for k in (0, 512):
+            o = part(pf, k, k + 512)
+            its += [(o, M("bD%d" % t), F[:, k + 1:k + 513], True, False), (o, M("nD%d" % t), F[:, k:k + 512], False, False),
+                    (o, M("bP%d" % t), F[:, H + k + 1:H + k + 513], False, False), (o, M("nP%d" % t), F[:, H + k:H + k + 512], False, True)]
+        mm(["Fall", "Fw", "bD%d" % t, "nD%d" % t, "bP%d" % t, "nP%d" % t], [pf], its, 4 * H)
+        cp([], [pf, "SH%d" % tb[t]], T.SH[:, tb[t] * H:(tb[t] + 1) * H], part(pf, 0, H), "vs", n=H)
+
+    SM = T.SM
+    WW, WR, CU, CT, T1, T2 = 0, 8, 16, 20, 24, 28
+
+    def differ(b, i, k, other, keys, n=1):
+        tt(keys, [b] + ["ne%d" % (k + j) for j in range(n)], blk(T.NE, k, n), blk(b, i, n), other, A.not_equal, n=128 * n)
+        for j in range(k, k + n):
+            o = CU + j if j < 3 else CT + j - 3
+            o = SM[:, o:o + 1]
+            do("vs", [], ["ne%d" % j, "cn%d" % j], 128,
+               lambda q, j=j, o=o: vv.tensor_reduce(o, blk(T.NE, j), AxisListType.X, A.add) if q == "v"
+               else sc.activation(blk(T.NE, j), blk(T.NE, j), AF.Copy, accum_out=o))
+
+    def counts(ds):
+        n = len(ds); p = POS[ds[0]]
+        cn = ["cn%d" % k for k in range(6)]
+        cu, ct = SM[:, CU:CU + n], SM[:, CT:CT + n]
+        pr = lambda c: T.PR[:, 3 * p + c:3 * (p + n):3]
+        tt(cn, ["t2"], SM[:, T2:T2 + n], ct, cu, A.subtract)
+        tt(cn + ["W"], ["pr0"], pr(0), cu, SM[:, WW + p:WW + p + n], A.mult)
+        tt(cn, ["t1"], SM[:, T1:T1 + n], cu, ct, A.add)
+        tt(["WR"], ["t2"], SM[:, T2:T2 + n], SM[:, T2:T2 + n], SM[:, WR + p:WR + p + n], A.mult)
+        tt(["t1", "WR"], ["pr1"], pr(1), SM[:, T1:T1 + n], SM[:, WR + p:WR + p + n], A.mult)
+        tt(["t2", "pr0"], ["pr2"], pr(2), SM[:, T2:T2 + n], pr(0), A.add)
+
+    def partial(ds, out, key):
+        p, n = POS[ds[0]], len(ds)
+        tt(["pr0", "pr1", "pr2"] + ["ACC%d_%d" % (d, c) for d in ds for c in range(3)], [key], out,
+           T.ACC[:, 3 * p:3 * (p + n)], T.PR[:, 3 * p:3 * (p + n)], A.add)
+
+    def team_send(ds, buf, w, sem, key):
+        s, n = w * (lay % 4), 3 * len(ds)
+        partial(ds, buf[:, s:s + n], key)
+        send([key], [sem], [([cores[x] for x in near], off, sem, buf[:, s:s + n], buf[:, s:s + n])])
+        arrive(sem, 3 * nof, [sem], [key + "in"], HOP)
+
+    SA, SB, SC, FA, FM, F0, F1, F2, FU, FTT = 32, 44, 56, 76, 82, 88, 94, 100, 106, 112
+
+    def team_sum(buf, w, n, key):
+        tt([key, key + "in"], ["sa"], SM[:, SA:SA + n], buf[:, 0:n], buf[:, w:w + n], A.add)
+        tt([key, key + "in"], ["sb"], SM[:, SB:SB + n], buf[:, 2 * w:2 * w + n], buf[:, 3 * w:3 * w + n], A.add)
+        tt(["sb"], ["sa"], SM[:, SA:SA + n], SM[:, SA:SA + n], SM[:, SB:SB + n], A.add)
+
+    def decide(b, n):
+        cp([], [b, "sc"], SM[:, SC:SC + 3 * n], part(b, 0, 3 * n))
+        s = lambda c: SM[:, SC + c:SC + 3 * n:3]
+        f = lambda x: SM[:, x:x + n]
+        tt(["sc"], ["fm"], f(FM), s(1), s(0), A.min)
+        tt(["sc"], ["fa", "fa0", "fa3"], f(FA), s(1), s(0), A.is_lt)
+        tt(["sc", "fm"], ["f2"], f(F2), s(2), f(FM), A.is_lt)
+        tt(["fa", "f2"], ["f1"], f(F1), f(FA), f(F2), A.is_gt)
+        tt(["fa", "f2"], ["fm"], f(FM), f(FA), f(F2), A.max)
+        ts(["fm"], ["f0"], f(F0), f(FM), -1.0, 1.0, A.mult, A.add)
+
+    def swap(lo, n, ds):
+        p = POS[ds[0]]
+        f = lambda x: SM[:, x + lo:x + lo + n]
+        k = str(lo)
+        tt(["f1", "f2"], ["fa" + k, "fa"], f(FA), f(F1), f(F2), A.subtract)
+        tt(["is%d" % d for d in ds], ["fa" + k], f(FA), f(FA), CF[:, IS + p:IS + p + n], A.mult)
+        tt(["fa" + k, "f2"], ["fu" + k], f(FU), f(FA), f(F2), A.add)
+        tt(["fa" + k, "f1"], ["ft" + k], f(FTT), f(F1), f(FA), A.subtract)
+
+    def diag(flag, i, keys):
+        k = turn["d"] % 18; turn["d"] += 1
+        ts(keys + ["I16"], ["dg%d" % k], blk(T.DG, k), M("I16"), SM[:, flag + i:flag + i + 1], None, A.mult)
+        return k
+
+    def select(sets):
+        b = new("b")
+        mm(["dg%d" % k for t in sets for k, _, _ in t] + [key for t in sets for _, _, key in t], [b],
+           [(blk(b, i), blk(T.DG, k), src, j == 0, j == 2) for i, t in enumerate(sets) for j, (k, src, _) in enumerate(t)], 384 * len(sets))
+        return b
+
+    def scores(R, terms):
+        b = new("b")
+        its = [(part(b, c, c + 3), M(m), SM[:, o:o + 3], j == 0, j == len(t) - 1) for c, t in terms for j, (m, o) in enumerate(t)]
+        mm(R + [m for c, t in terms for m, o in t], [b], its, 256 * len(its))
+        return b
+
+    W = lambda d: blk(T.W16, d - 1)
+    Hh = lambda d: blk(T.H16, d - 1)
+    UP = {2: 0, 4: 1, 6: 2, 3: 3, 5: 4, 7: 5}
+    U = lambda d: blk(T.UW, UP[d])
+    TT = lambda d: blk(T.TW, UP[d])
+    SLOT = {3: 2, 5: 3, 7: 4, 2: 5, 4: 6, 6: 7}
+    EV, OD = (2, 4, 6), (3, 5, 7)
+
+    WA, WH = ["W16", "W16a"], ["W16", "W16a", "H16", "H16a"]
+
+    for d in (1, 2, 4, 6, 3, 5, 7):
+        load_ft(d)
+    cp(["Wall"], ["W16a"], blk(T.W16, 0, 4), blk(T.Wall, 0, 4), n=512)
+    ts(["W16a"], ["H16a"], blk(T.H16, 1, 2), blk(T.W16, 1, 2), 0.0625, HB - 0.46875, A.mult, A.add, n=128)
+    slists(0, [(2, W(2), Hh(2), ["W16a", "H16a"]), (3, W(3), Hh(3), ["W16a", "H16a"])])
+    cp(["Fall"], ["Fw"], T.Fall[:, V:V + 16], T.Fall[:, 0:16], "vs")
+    halves = []
+    for d, k in HALF.items():
+        rs = [a ^ d if a & top(d) else a for a in range(N)]
+        pairs, a = [], 0
+        while a < N:
+            b = a + 1
+            while b < N and rs[b] == rs[b - 1] + 1 and b & top(d) == a & top(d):
+                b += 1
+            h = H if a & top(d) else 0
+            pairs.append((T.FH[16 * a:16 * b, 1040 * k:1040 * (k + 1)], T.Fall[16 * rs[a]:16 * (rs[a] + b - a), h:h + 1040]))
+            a = b
+        halves.append(("y", "fh%d" % d, ["Fall", "Fw", "TP"], ["FH%d" % d], pairs, 260, 128))
+    for t in (1, 2, 4):
+        steps_of_r(t)
+    lists(0, [(d, T.W16, d - 1, "W16a") for d in (1, 2, 4)])
+    cp(["Wall"], ["W16"], blk(T.W16, 4, 3), blk(T.Wall, 4, 3), n=384)
+    lists(0, [(d, T.W16, d - 1, "W16") for d in (6, 3, 5, 7)])
+    ts(WA, ["H16"], blk(T.H16, 3, 4), blk(T.W16, 3, 4), 0.0625, HB - 0.46875, A.mult, A.add, n=256)
+    slists(2, [(x, W(x), Hh(x), WH) for x in OD])
+    slists(5, [(x, W(x), Hh(x), WH) for x in EV])
+    cp(["LMi"], ["LMf"], T.LMf[0:8, 0:7], T.LMi[0:8, 0:7])
+    bw = new("b")
+    mm(["ET", "LMf"], [bw], [(part(bw, 0, 7), M("ET", parts=8), T.LMf[0:8, 0:7], True, True)], 256)
+    cp([], [bw, "Wa"], SM[:, WW:WW + 1], part(bw, 0, 1))
+    cp([], [bw, "Wb"], SM[:, WW + 1:WW + 4], part(bw, 1, 7, 2))
+    cp(["Wa", "Wb"], [bw, "W"], SM[:, WW + 4:WW + 7], part(bw, 2, 7, 2))
+    tt(["W"] + ["is%d" % d for d in POS], ["WR"], SM[:, WR:WR + 7], SM[:, WW:WW + 7], CF[:, IS:IS + 7], A.mult)
+    b2 = extract(compose("v", "TB", 0, ["TB"]), ["Z2_2"])
+    take(b2, 0, 1, blk(T.PW, 0), ["P2"])
+    lists(1, [(1, T.PW, 0, "P2")])
+    differ(b2, 0, 0, W(1), ["W16a"])
+    b3 = extract(compose("v", "TB", 1, ["TB"]), ["Z1_3"])
+    take(b3, 0, 1, blk(T.PW, 1), ["P3"])
+    lists(2, [(1, T.PW, 1, "P3")])
+    differ(b3, 0, 3, blk(T.PW, 0), ["P2"])
+    dma("y", "tb2", LM, ["TB"], [(T.TB[q:128:16, :], T.ldM[:, q:112:7, :]) for q in (3, 4, 5, 6)], 256, 512)
+    for d in POS:
+        judge(d, 0)
+    judge(1, 1); judge(1, 2)
+    counts([1])
+    team_send([1], T.X1, 4, "a1", "X1")
+    team_sum(T.X1, 4, 3, "X1")
+    decide(scores(["sa"], [(0, [("S0_1", SA)])]), 1)
+    swap(0, 1, [1])
+    k0, kU, kT = diag(F0, 0, ["f0"]), diag(FU, 0, ["fu0"]), diag(FTT, 0, ["ft0"])
+    b = select([[(k0, W(1), "W16a"), (kU, blk(T.PW, 0), "P2"), (kT, blk(T.PW, 1), "P3")]])
+    take(b, 0, 1, T.W32[:], ["pi32"])
+    dma("y", "pi", ["pi32"], ["TP"], [(T.TP[0:128:16, :], T.W32[:])], 64, 128)
+    for x in halves:
+        dma(*x)
+    dma("y", "ow", ["FH7"], ["OWi"], [(blk(T.OWi, 2, 5), blk(T.mp, 2, 5))], 320, 128)
+    take(b, 0, 1, blk(T.OM, 0), ["pi16"])
+    ts([], [b, "PH"], T.PH[:], blk(b, 0), 0.0625, HB - 0.46875, A.mult, A.add, n=128)
+    slists(8, [(1, blk(T.OM, 0), T.PH[:], ["pi16", "PH"])])
+
+    row = compose("v", "TB", 8, ["TB"])
+    b = extract(row, ["Z2_1", "Z4_1", "Z6_1"])
+    take(b, 0, 3, blk(T.UW, 0, 3), ["UE"])
+    lists(1, [(d, T.UW, UP[d], "UE") for d in EV])
+    for i, d in enumerate(EV):
+        differ(b, i, i, W(d), WA)
+    take(extract(row, ["Z1_1", "Z3_1", "Z5_1"]), 0, 3, blk(T.UW, 3, 3), ["UO"])
+    for d in EV + OD:
+        x, i = d ^ 1, UP[d]
+        b = extract(compose("s" if x in ONS else "v", "TP", SLOT[x], ["TP"]), ["Z0_%d" % x])
+        take(b, 0, 1, TT(d), ["T%d" % d])
+        if d in EV:
+            lists(2, [(d, T.TW, i, "T%d" % d)])
+            take(b, 0, 1, blk(T.WI, i), ["wi%d" % d])
+            differ(b, 0, 3 + i, U(d), ["UE"])
+            dma("y", "tu%d" % d, ["wi%d" % d, "UE"], ["TE%d" % d], [(T.TB[7 + i:128:16, :], blk(T.WI, i))], 64, 128)
+    take(extract(compose("v", "TB", 8, ["TB", "TE2", "TE4", "TE6"]), ["Z7_1", "Z8_1", "Z9_1"]), 0, 3, T.EW[:], ["EW"])
+    for c in (1, 2):
+        for d in EV:
+            judge(d, c)
+    counts(EV)
+    team_send(EV, T.X2, 12, "a2", "X2")
+    team_sum(T.X2, 12, 9, "X2")
+    decide(scores(["sa"], [(9 * k + 3 * i, [("S%d_%d" % (k, d ^ k), SA + 3 * i)]) for k in (0, 1) for i, d in enumerate(EV)]), 6)
+    swap(3, 3, EV); swap(0, 3, EV)
+
+    ks = [(diag(F0, 3 + i, ["f0"]), diag(FU, 3 + i, ["fu3"]), diag(FTT, 3 + i, ["ft3"])) for i in range(3)]
+    b = select([[(ks[i][0], U(d), "UO"), (ks[i][1], W(d), "W16"), (ks[i][2], blk(T.EW, i), "EW")] for i, d in enumerate(OD)])
+    take(b, 0, 3, blk(T.OM, 4, 3), ["U3"])
+    lists(1, [(d, T.OM, 4 + i, "U3") for i, d in enumerate(OD)])
+    for i, d in enumerate(OD):
+        differ(b, i, i, W(d), WA)
+    ks = [(diag(F0, i, ["f0"]), diag(FU, i, ["fu0"]), diag(FTT, i, ["ft0"])) for i in range(3)]
+    b = select([[(ks[i][0], TT(d), "T%d" % d), (ks[i][1], blk(T.EW, i), "EW"), (ks[i][2], W(d), "W16")] for i, d in enumerate(OD)])
+    take(b, 0, 3, blk(T.OM, 7, 3), ["T3n"])
+    lists(2, [(d, T.OM, 7 + i, "T3n") for i, d in enumerate(OD)])
+    differ(b, 0, 3, blk(T.OM, 4, 3), ["U3"], 3)
+    b = select([[(ks[i][0], W(d), "W16"), (ks[i][1], U(d), "UE"), (ks[i][2], TT(d), "T%d" % d)] for i, d in enumerate(EV)])
+    take(b, 0, 3, blk(T.OM, 1, 3), ["fin"])
+    om = ["pi16", "fin", "U3", "T3n"]
+    dma("y", "sO", om, ["stO"], [(T.stO[:], T.OM[:])], 320, 128)
+    dma("y", "ownO", om, ["ownO"], [(T.ldO[lay], T.OM[16 * me:16 * me + 16, :])], 40, 16)
+    send(["stO"], ["rO"], [([relay[me, x]], on[q4 * i:q4 * i + q4], "rO", T.stO[x], T.ldO[0]) for i, x in enumerate(far)])
+    send([], [], [([cores[x]], off[2 * i:2 * i + 2], "aO", T.stO[x], T.ldO[lay]) for i, x in enumerate(near)])
+    arrive("aO", 6 + 4 * nof, ["rO"], ["ldO"], 1.5 * HOP)
+    dma("y", "oi", ["ldO", "ownO"], ["OI"], [(T.OI[:], T.ldO[:])], 320, 128)
+    for c in (1, 2):
+        for d in OD:
+            judge(d, c)
+    counts(OD)
+    s = 12 * lay
+    partial(OD, T.X3[:, s:s + 9], "X3")
+    send(["X3"], ["r3"], [([relay[me, x] for x in far], on, "r3", T.X3[:, s:s + 9], T.X3[:, 0:9])])
+    send([], [], [([cores[x] for x in near], off, "a3", T.X3[:, s:s + 9], T.X3[:, s:s + 9])])
+    arrive("a3", 7 * nof, ["r3"], ["X3in"], 1.5 * HOP)
+
+    cp(["OWi"], ["OW"], blk(T.OW, 2, 5), blk(T.OWi, 2, 5), n=640)
+    cp(["OI"], ["ya"], blk(T.YO, 0, 2), blk(T.OI, 0, 2), n=256)
+    cp(["OI"], ["yb"], blk(T.YO, 3), blk(T.OI, 2), n=128)
+    cp(["OI"], ["yc"], blk(T.YO, 5), blk(T.OI, 3), n=128)
+    dma("y", "y1", ["ya", "yb", "yc"], [], [(blk(T.ym, 0, 2), blk(T.YO, 0, 2)), (blk(T.ym, 3), blk(T.YO, 3)), (blk(T.ym, 5), blk(T.YO, 5))], 256, 384)
+    X = ["X3", "X3in"]
+    for t, (o, k) in enumerate(((SA, "sa"), (SB, "sb"))):
+        c = 48 * t
+        tt(X, [k], SM[:, o:o + 9], T.X3[:, c:c + 9], T.X3[:, c + 12:c + 21], A.add)
+        tt(X, ["pr%d" % t], T.PR[:, 12 * t:12 * t + 9], T.X3[:, c + 24:c + 33], T.X3[:, c + 36:c + 45], A.add)
+    for t, (o, k) in enumerate(((SA, "sa"), (SB, "sb"))):
+        tt(["pr%d" % t], [k], SM[:, o:o + 9], SM[:, o:o + 9], T.PR[:, 12 * t:12 * t + 9], A.add)
+    decide(scores(["sa", "sb"], [(3 * i, [("O%d_0" % d, SA + 3 * i), ("O%d_1" % d, SB + 3 * i)]) for i, d in enumerate(OD)]), 3)
+    for i, d in enumerate(OD):
+        low = me < me ^ d
+        ks = diag(F1 if low else F2, i, ["f1", "f2"]), diag(F2 if low else F1, i, ["f1", "f2"]), diag(F0, i, ["f0"])
+        b = select([[(ks[0], blk(T.OI, 4 + i), "OI"), (ks[1], blk(T.OI, 7 + i), "OI"), (ks[2], blk(T.OW, d - 1), "OW")]])
+        cp([], [b, "y%d" % d], blk(T.YO, d - 1), blk(b, 0), "s", n=128)
+        dma("s" if d == 7 else "y", "y3" if d == 7 else "y2", ["y%d" % d], [], [(blk(T.ym, d - 1), blk(T.YO, d - 1))], 64, 128)
+    emit(best_order())

@@ -5,10 +5,14 @@ V, H, N = 2048, 1024, 8
 POS = {1: 0, 2: 1, 4: 2, 6: 3, 3: 4, 5: 5, 7: 6}
 HB = 1536
 NG = 5
-CYCLE, GATHER, WAKE, HOP, LOOK = 0.00104, 1.56, 0.06, 4.0, 0.8
-SHY, IDLE, SMALL, TRIES, SEED, MEMO = 5.0, 2.0, 8.0, 1500, 1, {}
-SUB = ((3, 2), (5, 2), (7, 2), (6, 2), (7, 1))
-HALF = {6: 0, 3: 1, 5: 2, 7: 3}
+CYCLE, GATHER, WAKE, HOP, LOOK = 0.00091, 1.56, 0.06, 4.0, 0.4
+SHY, IDLE, SMALL, TRIES, SEED, MEMO = 5.0, 6.0, 4.0, 4000, 1, {}
+SLACK, EARLY = 0.2, 0.3
+FORCE = {(1, 2): "v", (1, 1): "s", (1, 0): "s"}
+HOLD = {2: ["ACC1_1"], 4: ["X1"], 6: ["X1"], 3: ["X1"], 5: ["X1"], 7: ["X1"], "back": ["X1"], "T5": ["FL6_2"], "T7": ["ACC2_2"], "T3": ["FL6_2"]}
+ONS = (7, 4, 6)
+SUB = ((3, 2), (5, 2), (7, 2))
+HALF = {3: 0, 5: 1, 7: 2}
 
 SCRATCH = {
     "stF": ("dram", [8, 128, 256], "bfloat16"), "ldF": ("dram", [8, 128, 256], "bfloat16"),
@@ -19,29 +23,29 @@ SCRATCH = {
     "FH": ("sbuf", [128, 4 * 1040], "bfloat16"),
     "Wall": ("sbuf", [128, 896], "int32"), "W16": ("sbuf", [128, 896], "float16"), "H16": ("sbuf", [128, 896], "float16"),
     "OWi": ("sbuf", [128, 896], "int32"), "OW": ("sbuf", [128, 896], "float16"),
-    "TB": ("sbuf", [128, V], "int32"), "TP": ("sbuf", [128, V], "float32"),
+    "TB": ("sbuf", [128, V], "int32"), "TC": ("sbuf", [128, V], "int32"), "TP": ("sbuf", [128, V], "float32"),
     "RA": ("sbuf", [128, V], "float16"), "RB": ("sbuf", [128, V], "float16"), "RU": ("sbuf", [128, V], "float16"),
     "RS": ("sbuf", [128, V], "float32"), "RT": ("sbuf", [128, V], "float32"),
-    "PW": ("sbuf", [128, 256], "float16"), "UW": ("sbuf", [128, 768], "float16"), "TW": ("sbuf", [128, 768], "float16"),
+    "PW": ("sbuf", [128, 512], "float16"), "UW": ("sbuf", [128, 768], "float16"), "TW": ("sbuf", [128, 768], "float16"),
     "EW": ("sbuf", [128, 384], "float16"), "OM": ("sbuf", [128, 1280], "float16"), "OI": ("sbuf", [128, 1280], "float16"),
     "W32": ("sbuf", [128, 128], "float32"), "WI": ("sbuf", [128, 384], "int32"), "PH": ("sbuf", [128, 128], "float16"),
     "SL": ("sbuf", [128, 9 * 128], "uint16"), "FL": ("sbuf", [128, 21 * 66], "uint16"),
     "CT": ("sbuf", [128, 768], "float16"), "ZH": ("sbuf", [128, 128], "float16"), "ZF": ("sbuf", [128, 32], "float32"),
     "NE": ("sbuf", [128, 768], "bfloat16"), "DG": ("sbuf", [128, 18 * 128], "float16"),
-    "MH": ("sbuf", [128, 25 * 128], "float16"), "MB": ("sbuf", [128, 18 * 128], "bfloat16"), "MF": ("sbuf", [128, 22 * 128], "float32"),
+    "MH": ("sbuf", [128, 34 * 128], "float16"), "MB": ("sbuf", [128, 18 * 128], "bfloat16"), "MF": ("sbuf", [128, 22 * 128], "float32"),
     "IR": ("sbuf", [128, 128], "bfloat16"), "GM": ("sbuf", [128, 128], "bfloat16"),
     "CI": ("sbuf", [128, 8], "int32"), "CF": ("sbuf", [128, 96], "float32"),
     "LMi": ("sbuf", [128, 8], "int32"), "LMf": ("sbuf", [128, 8], "float32"),
     "ACC": ("sbuf", [128, 24], "float32"), "PR": ("sbuf", [128, 24], "float32"), "SM": ("sbuf", [128, 128], "float32"),
     "X1": ("sbuf", [128, 16], "float32"), "X2": ("sbuf", [128, 48], "float32"), "X3": ("sbuf", [128, 96], "float32"),
-    "YO": ("sbuf", [128, 896], "float32"),
+    "XS": ("sbuf", [128, 96], "float32"), "YO": ("sbuf", [128, 896], "float32"),
     "PF0": ("psum", [128, H], "float32"), "PF1": ("psum", [128, H], "float32"),
     "PA": ("psum", [128, 512], "float32"), "PB": ("psum", [128, 512], "float32"),
     "PC": ("psum", [128, 512], "float32"), "PD": ("psum", [128, 512], "float32"),
 }
 SEMAPHORES = ["cv", "cs", "cp", "cg", "out", "aF", "aM", "aO", "a1", "a2", "a3", "rF", "rM", "rO", "r3",
               "sF", "sM", "sN", "ownF", "ownM", "ow", "wall", "tb1", "tb2", "fall", "lm", "pi", "tu2", "tu4", "tu6",
-              "sO", "ownO", "oi", "y1", "y2", "y3"] + ["ft%d" % d for d in range(1, 8)] + ["fh%d" % d for d in HALF]
+              "sO", "ownO", "oi", "y1", "y2"] + ["ft%d" % d for d in range(1, 8)] + ["fh%d" % d for d in HALF]
 
 
 def top(d):
@@ -50,6 +54,10 @@ def top(d):
 
 def bits(engines):
     return sum(1 << e for e in engines)
+
+
+def slot3(lay):
+    return 24 * (lay % 4) + 12 * (lay // 4)
 
 
 def plan(T, topo):
@@ -76,9 +84,9 @@ def relay_program(g, core, T, topo, cores, layer, a, x):
     to = cores[x]
     en = topo.engines(core, to)
     wide = len(topo.engines(cores[a], core))
-    s = 12 * layer[a]
+    s = slot3(layer[a])
     steps = (("rM", wide // 4, "aM", T.ldM[0], T.ldM[a]), ("rF", wide // 4, "aF", T.ldF[0], T.ldF[a]),
-             ("rO", wide // 4, "aO", T.ldO[0], T.ldO[layer[a]]), ("r3", wide, "a3", T.X3[:, 0:9], T.X3[:, s:s + 9]))
+             ("rO", wide // 4, "aO", T.ldO[0], T.ldO[layer[a]]), ("r3", wide, "a3", T.X3[:, 0:12], T.X3[:, s:s + 12]))
     for here, n, there, src, out in steps:
         g.wait_ge(T.sem[here], n)
         g.remote_dma_fused([RemoteDMATransfer(dst_ids=[dst(topo, to, core)], dma_engine_mask=bits(en), remote_sem=T.sem[there],
@@ -100,6 +108,7 @@ def rank_program(g, core, T, topo):
     far = teams[1 - team]
     Q = {"v": g.vector, "s": g.scalar, "p": g.tensor, "g": g, "y": g.sync}
     ops, wr, rd, users, phys = [], {}, {}, {}, {}
+    hold = []
     pools = {"b": [(T[x], 0) for x in ("PA", "PB", "PC", "PD")], "f": [(T.PF0, 0), (T.PF1, 0)],
              "G": [(T.GB, 1056 * i) for i in range(NG)], "c": [(T.CT, 0), (T.CT, 384)],
              "r": [(T.RA, 0), (T.RB, 0), (T.RU, 0)], "R": [(T.RS, 0), (T.RT, 0)]}
@@ -113,7 +122,10 @@ def rank_program(g, core, T, topo):
         for k in W:
             deps |= set(rd.get(k, []))
         i = len(ops)
-        ops.append(dict(e=e, deps=deps, busy=busy, late=late, issue=issue, sem=sem, takes=[k for k in W if users.get(k) == []]))
+        hard = set(deps)
+        deps |= set(wr[k] for k in hold)
+        del hold[:]
+        ops.append(dict(e=e, deps=deps, hard=hard, busy=busy, late=late, issue=issue, sem=sem, takes=[k for k in W if users.get(k) == []]))
         for k in R:
             rd.setdefault(k, []).append(i)
         for k in W:
@@ -164,8 +176,11 @@ def rank_program(g, core, T, topo):
     def cp(R, W, o, i, e="v", n=64):
         do(e, R, W, n, lambda q: vv.tensor_copy(ap(o), ap(i)) if q == "v" else sc.activation(ap(o), ap(i), AF.Copy))
 
-    def mm(R, W, items, n):
+    def mm(R, W, items, n, beside=False):
+        first = wr.get(W[0])
         step("p", R, W, n * CYCLE / 2, 0.0, lambda q: [pe.matmul(ap(o), ap(l), ap(r), a, z) for o, l, r, a, z in items])
+        if beside:
+            ops[-1]["hard"].discard(first); ops[-1]["like"] = first
 
     def blk(t, i, n=1, w=128):
         return part(t, i * w, (i + n) * w) if isinstance(t, str) else t[:, i * w:(i + n) * w]
@@ -173,21 +188,26 @@ def rank_program(g, core, T, topo):
     def best_order():
         if "bias" not in MEMO:
             bias = [SMALL if o["busy"] < 0.6 else 0.0 for o in ops]
+            for i, o in enumerate(ops):
+                bias[i] += 100.0 - i if o["sem"] in ("sM", "sF", "sN") else 50.0 if o["sem"] in ("wall", "tb1") else 0.0
+            big = [i for i, o in enumerate(ops) if o["busy"] > 0.5 and o["e"] in "vsp" and o["deps"]]
             best, seed = order(bias)[0], SEED
-            for _ in range(TRIES):
+            now, top_ = best, bias
+            for k in range(TRIES):
                 new_ = list(bias)
-                for i, o in enumerate(ops):
+                for _ in range(3):
                     seed = (seed * 1103515245 + 12345) % 2147483648
-                    if (seed >> 4) % 1000 < (40 if o["busy"] > 0.6 else 6):
-                        new_[i] += ((seed >> 14) % 1000) / 1000.0 * 20.0 - 10.0
+                    new_[big[(seed >> 3) % len(big)]] += ((seed >> 14) % 1000) / 1000.0 * 24.0 - 12.0
                 t = order(new_)[0]
-                if t is not None and t <= best:
-                    best, bias = t, new_
-            MEMO["bias"] = bias; MEMO["time"] = best
+                if t is not None and t <= now + SLACK * (1.0 - k / TRIES):
+                    now, bias = t, new_
+                    if t < best:
+                        best, top_ = t, new_
+            MEMO["bias"] = top_; MEMO["time"] = best
         _, seq, extra, where = order(MEMO["bias"])
         phys.update(where)
         for i, more in extra.items():
-            ops[i]["deps"] = ops[i]["deps"] | more
+            ops[i]["hard"] = ops[i]["hard"] | more
         return seq
 
     def order(bias):
@@ -248,7 +268,8 @@ def rank_program(g, core, T, topo):
                 left[j] -= 1
                 if not left[j]:
                     ready.append(j)
-        return max(end.values()), seq, extra, where
+        MEMO["end"] = max(end.values())
+        return max(end.values()) + EARLY * sum(end[i] for i in range(n) if ops[i]["e"] == "net"), seq, extra, where
 
     def emit(seq):
         count, seen, tok = {}, {}, {}
@@ -262,7 +283,7 @@ def rank_program(g, core, T, topo):
                 tok[i] = (o["sem"], o["issue"]); count[o["sem"]] = o["issue"]
                 continue
             want = {}
-            for d in o["deps"]:
+            for d in o["hard"]:
                 if tok[d]:
                     want[tok[d][0]] = max(want.get(tok[d][0], 0), tok[d][1])
             for s, k in want.items():
@@ -278,13 +299,13 @@ def rank_program(g, core, T, topo):
 
     for t, sm, sf in ((1 - team, "sM", "sF"), (team, "sN", "sN")):
         l = 4 * t
-        dma("y", sm, [], [sm + "a", "yq"], [(T.stM[l:l + 4, 0:112, :], T.mp[16 * l:16 * l + 64, :])], 0, 0)
-        dma("s", sm, [], [sm + "b"],
-            [(T.stM[k, 112, 0:7], T.lam[t]) for k in range(l, l + 4) if k != lay]
-            + [(T.stM[l:l + 4, 112, 7:128], T.mp[0:4, 0:121]), (T.stM[l:l + 4, 113:128, :], T.mp[0:60, 0:128])], 224, 64)
+        dma("s", sm, ["yq"], [sm + "b"], [(T.stM[k, 112, 0:7], T.lam[t]) for k in range(l, l + 4) if k != lay], 0, 16)
+        dma("y", sm, [], [sm + "a"],
+            [(T.stM[l:l + 4, 0:112, :], T.mp[16 * l:16 * l + 64, :]), (T.stM[l:l + 4, 113:128, :], T.mp[0:60, 0:128]),
+             (T.stM[l:l + 4, 112, 7:128], T.mp[0:4, 0:121])], 256, 96)
         dma("y", sf, [], [sf + "c"], [(T.stF[l:l + 4], T.ft[16 * l:16 * l + 64, :])], 256, 16)
-    dma("y", "ownM", [], ["ownM"], [(T.ldM[me, 0:112, :], T.mp[16 * lay:16 * lay + 16, :]), (T.ldM[me, 112, 0:7], T.lam[team])], 56, 16)
-    dma("y", "ownF", [], ["ownF"], [(T.ldF[me], T.ft[16 * lay:16 * lay + 16, :])], 64, 16)
+    dma("s", "ownM", ["sMa"], ["ownM"], [(T.ldM[me, 0:112, :], T.mp[16 * lay:16 * lay + 16, :]), (T.ldM[me, 112, 0:7], T.lam[team])], 56, 16)
+    dma("s", "ownF", ["sMa"], ["ownF"], [(T.ldF[me], T.ft[16 * lay:16 * lay + 16, :])], 64, 16)
     do("g", [], ["pi0", "gq"], 130, lambda q: g.iota(T.CI[:, 0:1], [[0, 1]], 0, 1))
     do("g", [], ["IR"], 400, lambda q: g.iota(T.IR[:], [[1, 128]], 0, 0, allow_small_or_imprecise_dtypes=True))
     do("g", [], ["GM"], 400, lambda q: g.iota(T.GM[:], [[16, 8], [0, 16]], 0, 0, allow_small_or_imprecise_dtypes=True))
@@ -296,9 +317,10 @@ def rank_program(g, core, T, topo):
     send(["sNa", "sNb", "sNc"], ["sent"], [([cores[x]], off[2 * i + k:2 * i + k + 1], sem, st[layer[x]], ld[me])
                                            for i, x in enumerate(near) for k, (sem, st, ld) in enumerate((("aM", T.stM, T.ldM), ("aF", T.stF, T.ldF)))])
     do("g", ["sent"], ["TB"], 4200, lambda q: g.iota(T.TB[:], [[0, V]], 0, 0))
-    do("g", ["sent"], ["TP"], 4200, lambda q: g.iota(T.TP[:], [[0, V]], 0, 0, allow_small_or_imprecise_dtypes=True))
+    do("g", ["TB"], ["TC"], 4200, lambda q: g.iota(T.TC[:], [[0, V]], 0, 0))
+    do("g", ["TC"], ["TP"], 4200, lambda q: g.iota(T.TP[:], [[0, V]], 0, 0, allow_small_or_imprecise_dtypes=True))
     arrive("aM", 3 + 4 * nof, ["rM"], ["ldM"], 8.0)
-    arrive("aF", 3 + 4 * nof, ["rF"], ["ldF"], 9.0)
+    arrive("aF", 3 + 4 * nof, ["rF"], ["ldF"], 8.3)
 
     CF = T.CF
     for j in range(3):
@@ -347,6 +369,14 @@ def rank_program(g, core, T, topo):
         ts(cols, [name], T[buf][:, o:o + 8], GM[:, 0:128:16], col(GX, x), col(QM, q), A.is_equal, A.mult)
 
     IR, GM = T.IR, T.GM
+    for i, (src, k) in enumerate(((col(5, 0), 128.0), (col(5, 0), -2047.0), (col(1, 0), 128.0), (col(1, 0), -2047.0))):
+        ts(["isr", "c0"], ["sc%d" % i], col(24, i), src, k, None, A.mult)
+    cols += ["sc0", "sc1", "sc2", "sc3"]
+    for i, side in enumerate("rj"):
+        for x in (2, 3):
+            mat("A%d%s" % (x, side), "MH", IR, col(PX, x), col(24, 2 * i))
+            mat("B%d%s" % (x, side), "MH", IR, col(PX, x), col(24, 2 * i + 1))
+    mat("E1", "MH", IR, col(PX, 0), col(1, 0))
     smat(2); smat(3)
     for t in (1, 2, 4):
         mat("D%d" % t, "MH", IR, col(PX, 0), isr(t))
@@ -368,7 +398,6 @@ def rank_program(g, core, T, topo):
         smat(x)
     for q in (2, 4, 6, 1, 3, 5, 7, 8, 9):
         zmat(q, 1)
-    ONS = (7, 4, 6)
     for x in range(2, 8):
         zmat(0, x, "ZF" if x in ONS else "ZH")
     for x in range(8):
@@ -377,19 +406,26 @@ def rank_program(g, core, T, topo):
         mats["S%d_%d" % (x, y)] = ("MF", 128 * used["MF"]); used["MF"] += 1
         tt(["S%d" % x, "S%d" % y], ["S%d_%d" % (x, y)], M("S%d_%d" % (x, y)), M("S%d" % x), M("S%d" % y), A.add, n=256)
     ts(["ind0"], ["ind"], CF[:, I2:I2 + 8], CF[:, IN:IN + 8], col(IN, 0), None, A.add)
-    for d in (3, 5, 7):
-        mat("O%d_0" % d, "MF", GM, 64.0, col(I2, d), op0=A.is_lt)
-        mat("O%d_1" % d, "MF", GM, 64.0, col(I2, d), op0=A.is_ge)
+    mat("O0", "MF", GM, 64.0, 1.0, op0=A.is_lt)
+    mat("O1", "MF", GM, 64.0, 1.0, op0=A.is_ge)
+    for i, d in enumerate((3, 5, 7, 0)):
+        ts(["ind", "IR"], ["im%d" % d], T.XS[:, 72 + 3 * i:75 + 3 * i], IR[:, 0:3], 0.0, col(I2, d), A.mult, A.add)
+    cp(["im3", "im5", "im7", "im0"], ["im"], T.XS[:, 84:96], T.XS[:, 72:84])
+    s3 = slot3(lay)
+    ts(["IR"], ["X3"], T.X3[:, s3:s3 + 12], IR[:, 0:12], 0.0, None, A.mult)
 
     LM, LF = ["ldM", "ownM"], ["ldF", "ownF"]
     dma("y", "wall", LM, ["Wall"], [(T.Wall[:], T.ldM[:, 0:112, :])], 448, 128)
-    dma("s", "tb1", LM, ["TB"], [(T.TB[q:128:16, :], T.ldM[:, q:112:7, :]) for q in (2, 1)], 128, 256)
-    dma("s", "lm", LM, ["LMi"], [(T.LMi[0:8, 0:7], T.ldM[:, 112, 0:7])], 0, 16)
+    dma("y", "tb1", LM, ["TB"], [(T.TB[q:128:16, :], T.ldM[:, q:112:7, :]) for q in (2, 1)], 128, 256)
     dma("y", "fall", LF, ["Fall"], [(T.Fall[:, 0:V], T.ldF[:])], 512, 128)
+    dma("y", "lm", LM + LF, ["LMi"], [(T.LMi[0:8, 0:7], T.ldM[:, 112, 0:7])], 0, 16)
 
     def load_ft(d):
         at = V + 16 + V * POS[d]
-        do("v", [], ["FT%d" % d], H, lambda q: vv.memset(T.Fall[:, at:at + V], 0.0))
+        if d in (1, 2, 4):
+            do("v", [], ["FT%d" % d], H, lambda q: vv.memset(T.Fall[:, at:at + V], 0.0))
+        else:
+            cp(["FH3", "FH5"], ["FT%d" % d], T.Fall[:, at:at + V], T.FH[:, 0:V], "s", n=V)
         ts(["IR"], ["of%d" % d], blk(T.OF, POS[d], 1, 66), IR[:, 0:66], 0.0, float(at), A.mult, A.add)
         pairs, a = [], 0
         while a < N:
@@ -434,8 +470,10 @@ def rank_program(g, core, T, topo):
     def extract(row, zs):
         b = new("b"); n = len(zs)
         buf, o = mats[zs[0]]
-        mm([row] + list(zs), [b], [(part(b, s, 128 * n, 16), part(row, s, V, 16), T[buf][:, o:o + 8 * n], True, True) for s in range(16)],
-           1024 if row[0] == "r" else 4096)
+        k = 16 if row[0] == "r" else 4
+        for s0 in range(0, 16, k):
+            mm([row] + list(zs), [b], [(part(b, s, 128 * n, 16), part(row, s, V, 16), T[buf][:, o:o + 8 * n], True, True) for s in range(s0, s0 + k)],
+               1024, s0 > 0)
         c = new("c")
         cp([], [b, c], blk(c, 0, n), blk(b, 0, n), n=128 * n)
         b = new("b")
@@ -454,15 +492,15 @@ def rank_program(g, core, T, topo):
         if sub:
             tt(R + ["FH%d" % d], [G], part(G, 0, 1040), src, blk(T.FH, HALF[d], 1, 1040), A.subtract, n=1040 * GATHER)
         else:
-            cp(R, [G], part(G, 0, 1040), src, "vs", n=1040 * GATHER)
+            cp(R, [G], part(G, 0, 1040), src, FORCE.get((d, c), "vs"), n=1040 * GATHER)
         pf = new("f")
         m = "I" if d == top(d) else "Q%d" % d
-        t = tb[top(d)]; its = []
+        t = tb[top(d)]
         for k in (0, 512):
             o = part(pf, k, k + 512)
-            its += [] if sub else [(o, M(m), T.SH[:, t * H + k:t * H + k + 512], True, False)]
+            its = [] if sub else [(o, M(m), T.SH[:, t * H + k:t * H + k + 512], True, False)]
             its += [(o, M("I"), part(G, k, k + 512), sub, False), (o, M("nI"), part(G, k + 1, k + 513), False, True)]
-        mm([G, "I", "nI"] + ([] if sub else ["SH%d" % t, m]), [pf], its, 512 * len(its))
+            mm([G, "I", "nI"] + ([] if sub else ["SH%d" % t, m]), [pf], its, 512 * len(its), k > 0)
         acc = T.ACC[:, 3 * POS[d] + c:3 * POS[d] + c + 1]; src = part(pf, 0, H)
         do("vs", [], [pf, G, "ACC%d_%d" % (d, c)], H,
            lambda q: vv.tensor_reduce(acc, ap(src), AxisListType.X, A.add, apply_absolute_value=True) if q == "v"
@@ -470,12 +508,12 @@ def rank_program(g, core, T, topo):
 
     def steps_of_r(t):
         pf = new("f")
-        its = []; F = T.Fall
+        F = T.Fall
         for k in (0, 512):
             o = part(pf, k, k + 512)
-            its += [(o, M("bD%d" % t), F[:, k + 1:k + 513], True, False), (o, M("nD%d" % t), F[:, k:k + 512], False, False),
-                    (o, M("bP%d" % t), F[:, H + k + 1:H + k + 513], False, False), (o, M("nP%d" % t), F[:, H + k:H + k + 512], False, True)]
-        mm(["Fall", "Fw", "bD%d" % t, "nD%d" % t, "bP%d" % t, "nP%d" % t], [pf], its, 4 * H)
+            its = [(o, M("bD%d" % t), F[:, k + 1:k + 513], True, False), (o, M("nD%d" % t), F[:, k:k + 512], False, False),
+                   (o, M("bP%d" % t), F[:, H + k + 1:H + k + 513], False, False), (o, M("nP%d" % t), F[:, H + k:H + k + 512], False, True)]
+            mm(["Fall", "Fw", "bD%d" % t, "nD%d" % t, "bP%d" % t, "nP%d" % t], [pf], its, 2 * H, k > 0)
         cp([], [pf, "SH%d" % tb[t]], T.SH[:, tb[t] * H:(tb[t] + 1) * H], part(pf, 0, H), "vs", n=H)
 
     SM = T.SM
@@ -540,20 +578,21 @@ def rank_program(g, core, T, topo):
         tt(["fa" + k, "f2"], ["fu" + k], f(FU), f(FA), f(F2), A.add)
         tt(["fa" + k, "f1"], ["ft" + k], f(FTT), f(F1), f(FA), A.subtract)
 
-    def diag(flag, i, keys):
+    def diag(flag, i, keys, m="I16"):
         k = turn["d"] % 18; turn["d"] += 1
-        ts(keys + ["I16"], ["dg%d" % k], blk(T.DG, k), M("I16"), SM[:, flag + i:flag + i + 1], None, A.mult)
+        ts(keys + [m], ["dg%d" % k], blk(T.DG, k), M(m), SM[:, flag + i:flag + i + 1], None, A.mult)
         return k
 
     def select(sets):
         b = new("b")
         mm(["dg%d" % k for t in sets for k, _, _ in t] + [key for t in sets for _, _, key in t], [b],
-           [(blk(b, i), blk(T.DG, k), src, j == 0, j == 2) for i, t in enumerate(sets) for j, (k, src, _) in enumerate(t)], 384 * len(sets))
+           [(blk(b, i), blk(T.DG, k), src, j == 0, j == len(t) - 1) for i, t in enumerate(sets) for j, (k, src, _) in enumerate(t)],
+           128 * sum(len(t) for t in sets))
         return b
 
-    def scores(R, terms):
+    def scores(R, terms, w=3):
         b = new("b")
-        its = [(part(b, c, c + 3), M(m), SM[:, o:o + 3], j == 0, j == len(t) - 1) for c, t in terms for j, (m, o) in enumerate(t)]
+        its = [(part(b, c, c + w), M(m), SM[:, o:o + w], j == 0, j == len(t) - 1) for c, t in terms for j, (m, o) in enumerate(t)]
         mm(R + [m for c, t in terms for m, o in t], [b], its, 256 * len(its))
         return b
 
@@ -567,11 +606,16 @@ def rank_program(g, core, T, topo):
 
     WA, WH = ["W16", "W16a"], ["W16", "W16a", "H16", "H16a"]
 
+    do("v", [], ["FH3", "FH5"], H, lambda q: vv.memset(T.FH[:, 0:V], 0.0))
     for d in (1, 2, 4, 6, 3, 5, 7):
         load_ft(d)
     cp(["Wall"], ["W16a"], blk(T.W16, 0, 4), blk(T.Wall, 0, 4), n=512)
     ts(["W16a"], ["H16a"], blk(T.H16, 1, 2), blk(T.W16, 1, 2), 0.0625, HB - 0.46875, A.mult, A.add, n=128)
-    slists(0, [(2, W(2), Hh(2), ["W16a", "H16a"]), (3, W(3), Hh(3), ["W16a", "H16a"])])
+    for k, side in enumerate("rj"):
+        b = new("b")
+        mm(["W16a", "H16a"] + [m + side for m in ("A2", "B2", "A3", "B3")], [b],
+           [(blk(b, 0), M(m + side), src, m == "A2", m == "B3") for m, src in (("A2", W(2)), ("B2", Hh(2)), ("A3", W(3)), ("B3", Hh(3)))], 512)
+        ts([], [b, "SL%d" % k], blk(T.SL, k), blk(b, 0), float(2047 * HB), None, A.add, n=128)
     cp(["Fall"], ["Fw"], T.Fall[:, V:V + 16], T.Fall[:, 0:16], "vs")
     halves = []
     for d, k in HALF.items():
@@ -600,25 +644,29 @@ def rank_program(g, core, T, topo):
     cp([], [bw, "Wb"], SM[:, WW + 1:WW + 4], part(bw, 1, 7, 2))
     cp(["Wa", "Wb"], [bw, "W"], SM[:, WW + 4:WW + 7], part(bw, 2, 7, 2))
     tt(["W"] + ["is%d" % d for d in POS], ["WR"], SM[:, WR:WR + 7], SM[:, WW:WW + 7], CF[:, IS:IS + 7], A.mult)
-    b2 = extract(compose("v", "TB", 0, ["TB"]), ["Z2_2"])
-    take(b2, 0, 1, blk(T.PW, 0), ["P2"])
-    lists(1, [(1, T.PW, 0, "P2")])
-    differ(b2, 0, 0, W(1), ["W16a"])
-    b3 = extract(compose("v", "TB", 1, ["TB"]), ["Z1_3"])
-    take(b3, 0, 1, blk(T.PW, 1), ["P3"])
-    lists(2, [(1, T.PW, 1, "P3")])
-    differ(b3, 0, 3, blk(T.PW, 0), ["P2"])
-    dma("y", "tb2", LM, ["TB"], [(T.TB[q:128:16, :], T.ldM[:, q:112:7, :]) for q in (3, 4, 5, 6)], 256, 512)
-    for d in POS:
-        judge(d, 0)
-    judge(1, 1); judge(1, 2)
-    counts([1])
+    b = extract(compose("v", "TB", 0, ["TB"]), ["Z2_2", "Z1_3"])
+    take(b, 0, 2, blk(T.PW, 0, 2), ["PR"])
+    lists(1, [(1, T.PW, 0, "PR")])
+    lists(2, [(1, T.PW, 1, "PR")])
+    differ(b, 0, 0, W(1), ["W16a"])
+    differ(b, 1, 1, W(1), ["W16a"])
+    differ(b, 1, 3, blk(T.PW, 0), ["PR"])
+    dma("y", "tb2", LM + ["FT7"], ["TC"], [(T.TC[q:128:16, :], T.ldM[:, q:112:7, :]) for q in range(1, 7)], 384, 768)
+    for c in range(3):
+        judge(1, c)
+    for c, (x, y) in enumerate(((CU, CU + 1), (CU, CT), (CU + 1, CT))):
+        ts(["cn0", "cn1", "cn3", "WR"], ["pr%d" % c], T.PR[:, c:c + 1], SM[:, x:x + 1], SM[:, y:y + 1], SM[:, WR:WR + 1], A.add, A.mult)
     team_send([1], T.X1, 4, "a1", "X1")
+    hold.extend(HOLD.get("back", []))
+    take(extract(compose("v", "TB", 1, ["TB"]), ["Z2_2", "Z1_3"]), 0, 2, blk(T.PW, 2, 2), ["PJ"])
+    for d in EV + OD:
+        hold.extend(HOLD.get(d, []))
+        judge(d, 0)
     team_sum(T.X1, 4, 3, "X1")
     decide(scores(["sa"], [(0, [("S0_1", SA)])]), 1)
-    swap(0, 1, [1])
-    k0, kU, kT = diag(F0, 0, ["f0"]), diag(FU, 0, ["fu0"]), diag(FTT, 0, ["ft0"])
-    b = select([[(k0, W(1), "W16a"), (kU, blk(T.PW, 0), "P2"), (kT, blk(T.PW, 1), "P3")]])
+    b = select([[(diag(F1, 0, ["f1"], "D1"), blk(T.PW, 0), "PR"), (diag(F2, 0, ["f2"], "D1"), blk(T.PW, 1), "PR"),
+                 (diag(F2, 0, ["f2"], "E1"), blk(T.PW, 2), "PJ"), (diag(F1, 0, ["f1"], "E1"), blk(T.PW, 3), "PJ"),
+                 (diag(F0, 0, ["f0"]), W(1), "W16a")]])
     take(b, 0, 1, T.W32[:], ["pi32"])
     dma("y", "pi", ["pi32"], ["TP"], [(T.TP[0:128:16, :], T.W32[:])], 64, 128)
     for x in halves:
@@ -628,46 +676,53 @@ def rank_program(g, core, T, topo):
     ts([], [b, "PH"], T.PH[:], blk(b, 0), 0.0625, HB - 0.46875, A.mult, A.add, n=128)
     slists(8, [(1, blk(T.OM, 0), T.PH[:], ["pi16", "PH"])])
 
-    row = compose("v", "TB", 8, ["TB"])
+    row = compose("v", "TC", 8, ["TC"])
     b = extract(row, ["Z2_1", "Z4_1", "Z6_1"])
     take(b, 0, 3, blk(T.UW, 0, 3), ["UE"])
     lists(1, [(d, T.UW, UP[d], "UE") for d in EV])
     for i, d in enumerate(EV):
         differ(b, i, i, W(d), WA)
     take(extract(row, ["Z1_1", "Z3_1", "Z5_1"]), 0, 3, blk(T.UW, 3, 3), ["UO"])
-    for d in EV + OD:
+    def by_b1(d):
         x, i = d ^ 1, UP[d]
+        hold.extend(HOLD.get("T%d" % d, []))
         b = extract(compose("s" if x in ONS else "v", "TP", SLOT[x], ["TP"]), ["Z0_%d" % x])
         take(b, 0, 1, TT(d), ["T%d" % d])
         if d in EV:
             lists(2, [(d, T.TW, i, "T%d" % d)])
             take(b, 0, 1, blk(T.WI, i), ["wi%d" % d])
             differ(b, 0, 3 + i, U(d), ["UE"])
-            dma("y", "tu%d" % d, ["wi%d" % d, "UE"], ["TE%d" % d], [(T.TB[7 + i:128:16, :], blk(T.WI, i))], 64, 128)
-    take(extract(compose("v", "TB", 8, ["TB", "TE2", "TE4", "TE6"]), ["Z7_1", "Z8_1", "Z9_1"]), 0, 3, T.EW[:], ["EW"])
+            dma("y", "tu%d" % d, ["wi%d" % d, "UE"], ["TE%d" % d], [(T.TC[7 + i:128:16, :], blk(T.WI, i))], 64, 128)
+    for d in EV:
+        by_b1(d)
+    take(extract(compose("v", "TC", 8, ["TC", "TE2", "TE4", "TE6"]), ["Z7_1", "Z8_1", "Z9_1"]), 0, 3, T.EW[:], ["EW"])
     for c in (1, 2):
         for d in EV:
             judge(d, c)
+    for d in OD:
+        by_b1(d)
     counts(EV)
     team_send(EV, T.X2, 12, "a2", "X2")
     team_sum(T.X2, 12, 9, "X2")
     decide(scores(["sa"], [(9 * k + 3 * i, [("S%d_%d" % (k, d ^ k), SA + 3 * i)]) for k in (0, 1) for i, d in enumerate(EV)]), 6)
     swap(3, 3, EV); swap(0, 3, EV)
 
-    ks = [(diag(F0, 3 + i, ["f0"]), diag(FU, 3 + i, ["fu3"]), diag(FTT, 3 + i, ["ft3"])) for i in range(3)]
-    b = select([[(ks[i][0], U(d), "UO"), (ks[i][1], W(d), "W16"), (ks[i][2], blk(T.EW, i), "EW")] for i, d in enumerate(OD)])
-    take(b, 0, 3, blk(T.OM, 4, 3), ["U3"])
-    lists(1, [(d, T.OM, 4 + i, "U3") for i, d in enumerate(OD)])
+    ks = []
     for i, d in enumerate(OD):
-        differ(b, i, i, W(d), WA)
-    ks = [(diag(F0, i, ["f0"]), diag(FU, i, ["fu0"]), diag(FTT, i, ["ft0"])) for i in range(3)]
-    b = select([[(ks[i][0], TT(d), "T%d" % d), (ks[i][1], blk(T.EW, i), "EW"), (ks[i][2], W(d), "W16")] for i, d in enumerate(OD)])
-    take(b, 0, 3, blk(T.OM, 7, 3), ["T3n"])
-    lists(2, [(d, T.OM, 7 + i, "T3n") for i, d in enumerate(OD)])
-    differ(b, 0, 3, blk(T.OM, 4, 3), ["U3"], 3)
+        k = diag(F0, 3 + i, ["f0"]), diag(FU, 3 + i, ["fu3"]), diag(FTT, 3 + i, ["ft3"])
+        b = select([[(k[0], U(d), "UO"), (k[1], W(d), "W16"), (k[2], blk(T.EW, i), "EW")]])
+        take(b, 0, 1, blk(T.OM, 4 + i), ["U%dn" % d])
+        lists(1, [(d, T.OM, 4 + i, "U%dn" % d)])
+        differ(b, 0, i, W(d), WA)
+        k = diag(F0, i, ["f0"]), diag(FU, i, ["fu0"]), diag(FTT, i, ["ft0"])
+        ks.append(k)
+        b = select([[(k[0], TT(d), "T%d" % d), (k[1], blk(T.EW, i), "EW"), (k[2], W(d), "W16")]])
+        take(b, 0, 1, blk(T.OM, 7 + i), ["T%dn" % d])
+        lists(2, [(d, T.OM, 7 + i, "T%dn" % d)])
+        differ(b, 0, 3 + i, blk(T.OM, 4 + i), ["U%dn" % d])
     b = select([[(ks[i][0], W(d), "W16"), (ks[i][1], U(d), "UE"), (ks[i][2], TT(d), "T%d" % d)] for i, d in enumerate(EV)])
     take(b, 0, 3, blk(T.OM, 1, 3), ["fin"])
-    om = ["pi16", "fin", "U3", "T3n"]
+    om = ["pi16", "fin"] + [k % d for k in ("U%dn", "T%dn") for d in OD]
     dma("y", "sO", om, ["stO"], [(T.stO[:], T.OM[:])], 320, 128)
     dma("y", "ownO", om, ["ownO"], [(T.ldO[lay], T.OM[16 * me:16 * me + 16, :])], 40, 16)
     send(["stO"], ["rO"], [([relay[me, x]], on[q4 * i:q4 * i + q4], "rO", T.stO[x], T.ldO[0]) for i, x in enumerate(far)])
@@ -678,29 +733,27 @@ def rank_program(g, core, T, topo):
         for d in OD:
             judge(d, c)
     counts(OD)
-    s = 12 * lay
+    s = s3
     partial(OD, T.X3[:, s:s + 9], "X3")
-    send(["X3"], ["r3"], [([relay[me, x] for x in far], on, "r3", T.X3[:, s:s + 9], T.X3[:, 0:9])])
-    send([], [], [([cores[x] for x in near], off, "a3", T.X3[:, s:s + 9], T.X3[:, s:s + 9])])
+    send(["X3"], ["r3"], [([relay[me, x] for x in far], on, "r3", T.X3[:, s:s + 12], T.X3[:, 0:12])])
+    send([], [], [([cores[x] for x in near], off, "a3", T.X3[:, s:s + 12], T.X3[:, s:s + 12])])
     arrive("a3", 7 * nof, ["r3"], ["X3in"], 1.5 * HOP)
 
+    hold.append("X3")
     cp(["OWi"], ["OW"], blk(T.OW, 2, 5), blk(T.OWi, 2, 5), n=640)
     cp(["OI"], ["ya"], blk(T.YO, 0, 2), blk(T.OI, 0, 2), n=256)
     cp(["OI"], ["yb"], blk(T.YO, 3), blk(T.OI, 2), n=128)
     cp(["OI"], ["yc"], blk(T.YO, 5), blk(T.OI, 3), n=128)
-    dma("y", "y1", ["ya", "yb", "yc"], [], [(blk(T.ym, 0, 2), blk(T.YO, 0, 2)), (blk(T.ym, 3), blk(T.YO, 3)), (blk(T.ym, 5), blk(T.YO, 5))], 256, 384)
     X = ["X3", "X3in"]
-    for t, (o, k) in enumerate(((SA, "sa"), (SB, "sb"))):
-        c = 48 * t
-        tt(X, [k], SM[:, o:o + 9], T.X3[:, c:c + 9], T.X3[:, c + 12:c + 21], A.add)
-        tt(X, ["pr%d" % t], T.PR[:, 12 * t:12 * t + 9], T.X3[:, c + 24:c + 33], T.X3[:, c + 36:c + 45], A.add)
-    for t, (o, k) in enumerate(((SA, "sa"), (SB, "sb"))):
-        tt(["pr%d" % t], [k], SM[:, o:o + 9], SM[:, o:o + 9], T.PR[:, 12 * t:12 * t + 9], A.add)
-    decide(scores(["sa", "sb"], [(3 * i, [("O%d_0" % d, SA + 3 * i), ("O%d_1" % d, SB + 3 * i)]) for i, d in enumerate(OD)]), 3)
+    tt(X, ["xs"], T.XS[:, 0:48], T.X3[:, 0:48], T.X3[:, 48:96], A.add)
+    tt(["xs"], ["xt"], T.XS[:, 48:72], T.XS[:, 0:24], T.XS[:, 24:48], A.add)
+    tt(["xt", "im"], ["sa", "sb"], SM[:, SA:SA + 24], T.XS[:, 48:72], T.XS[:, 72:96], A.mult)
+    decide(scores(["sa", "sb"], [(0, [("O0", SA), ("O1", SB)])], 9), 3)
     for i, d in enumerate(OD):
         low = me < me ^ d
         ks = diag(F1 if low else F2, i, ["f1", "f2"]), diag(F2 if low else F1, i, ["f1", "f2"]), diag(F0, i, ["f0"])
         b = select([[(ks[0], blk(T.OI, 4 + i), "OI"), (ks[1], blk(T.OI, 7 + i), "OI"), (ks[2], blk(T.OW, d - 1), "OW")]])
         cp([], [b, "y%d" % d], blk(T.YO, d - 1), blk(b, 0), "s", n=128)
-        dma("s" if d == 7 else "y", "y3" if d == 7 else "y2", ["y%d" % d], [], [(blk(T.ym, d - 1), blk(T.YO, d - 1))], 64, 128)
+    dma("y", "y1", ["ya", "yb", "y3"], [], [(blk(T.ym, 0, 4), blk(T.YO, 0, 4))], 256, 128)
+    dma("s", "y2", ["yc", "y5", "y7"], [], [(blk(T.ym, 4, 3), blk(T.YO, 4, 3))], 192, 128)
     emit(best_order())

@@ -3,49 +3,56 @@ from concourse.mybir import AluOpType as A, AxisListType, ActivationFunctionType
 
 V, H, N = 2048, 1024, 8
 POS = {1: 0, 2: 1, 4: 2, 6: 3, 3: 4, 5: 5, 7: 6}
+EV, OD = (2, 4, 6), (3, 5, 7)
 HB = 1536
-NG = 5
-CYCLE, GATHER, WAKE, HOP, LOOK = 0.00091, 1.56, 0.06, 4.0, 0.4
-SHY, IDLE, SMALL, TRIES, SEED, MEMO = 5.0, 6.0, 4.0, 4000, 1, {}
+NG, NM = 5, 3
+CYCLE, GATHER, WAKE, HOP, LOOK = 0.00095, 1.56, 0.06, 3.5, 0.4
+SHY, IDLE, SMALL, TRIES, SEED, MEMO = 5.0, 6.0, 4.0, 500, 1, {}
 SLACK, EARLY = 0.2, 0.3
-FORCE = {(1, 2): "v", (1, 1): "s", (1, 0): "s"}
-HOLD = {2: ["ACC1_1"], 4: ["X1"], 6: ["X1"], 3: ["X1"], 5: ["X1"], 7: ["X1"], "back": ["X1"], "T5": ["FL6_2"], "T7": ["ACC2_2"], "T3": ["FL6_2"]}
-ONS = (7, 4, 6)
-SUB = ((3, 2), (5, 2), (7, 2))
-HALF = {3: 0, 5: 1, 7: 2}
+ARR_A, ARR_F, ARR_B = 7.0, 9.0, 10.5
+LONG = {"v": "Cr Cj J11 J20 J40 J60 U J21 J41 J61 E J30 J50 J31 J51 J71".split(),
+        "s": "J10 J12 A10 A12 T2 T4 T6 J22 J42 A22 J62 A42 A62 T3 T5 T7 J70 J32 A70 J52 A32 J72 A52 A72".split()}
+LOADS = "wa tc1 w1 fall ft1 fh1 lm wb ft2 fh2 tp ft4 fh4 ft6 fh6 tc2 ft3 fh3 tu2 tu4 tu6 ft5 fh5 ft7 fh7".split()
+GATE = {"ft6": ["X1"], "ft3": ["SL8"]}
 
 SCRATCH = {
+    "stA": ("dram", [8, 128, 64], "int32"), "ldA": ("dram", [8, 128, 64], "int32"),
+    "stB": ("dram", [8, 128, 64], "int32"), "ldB": ("dram", [8, 128, 64], "int32"),
     "stF": ("dram", [8, 128, 256], "bfloat16"), "ldF": ("dram", [8, 128, 256], "bfloat16"),
-    "stM": ("dram", [8, 128, 128], "int32"), "ldM": ("dram", [8, 128, 128], "int32"),
     "stO": ("dram", [8, 128, 160], "float16"), "ldO": ("dram", [8, 128, 160], "float16"),
     "Fall": ("sbuf", [128, 8 * V + 16], "bfloat16"), "OF": ("sbuf", [128, 7 * 66], "float16"),
-    "SH": ("sbuf", [128, 3 * H], "bfloat16"), "GB": ("sbuf", [128, NG * 1056], "bfloat16"),
-    "FH": ("sbuf", [128, 4 * 1040], "bfloat16"),
+    "GB": ("sbuf", [128, NG * 1056], "bfloat16"), "MX": ("sbuf", [128, NM * H], "bfloat16"),
+    "FH": ("sbuf", [128, 7 * 1040], "bfloat16"),
     "Wall": ("sbuf", [128, 896], "int32"), "W16": ("sbuf", [128, 896], "float16"), "H16": ("sbuf", [128, 896], "float16"),
-    "OWi": ("sbuf", [128, 896], "int32"), "OW": ("sbuf", [128, 896], "float16"),
-    "TB": ("sbuf", [128, V], "int32"), "TC": ("sbuf", [128, V], "int32"), "TP": ("sbuf", [128, V], "float32"),
-    "RA": ("sbuf", [128, V], "float16"), "RB": ("sbuf", [128, V], "float16"), "RU": ("sbuf", [128, V], "float16"),
-    "RS": ("sbuf", [128, V], "float32"), "RT": ("sbuf", [128, V], "float32"),
-    "PW": ("sbuf", [128, 512], "float16"), "UW": ("sbuf", [128, 768], "float16"), "TW": ("sbuf", [128, 768], "float16"),
+    "OWi": ("sbuf", [128, 384], "int32"), "OW": ("sbuf", [128, 384], "float16"),
+    "TC": ("sbuf", [128, V], "int32"), "TS": ("sbuf", [128, V], "float32"), "TP": ("sbuf", [128, V], "bfloat16"),
+    "TR": ("sbuf", [128, 6 * V], "bfloat16"),
+    "RA": ("sbuf", [128, V], "float16"), "RB": ("sbuf", [128, V], "float16"), "RS": ("sbuf", [128, V], "float32"),
+    "PW": ("sbuf", [128, 256], "float16"), "PK": ("sbuf", [128, 384], "float16"), "PH": ("sbuf", [128, 384], "float16"),
+    "SV": ("sbuf", [128, 384], "float16"), "HL": ("sbuf", [128, 768], "bfloat16"),
+    "UW": ("sbuf", [128, 768], "float16"), "TW": ("sbuf", [128, 768], "float16"),
     "EW": ("sbuf", [128, 384], "float16"), "OM": ("sbuf", [128, 1280], "float16"), "OI": ("sbuf", [128, 1280], "float16"),
-    "W32": ("sbuf", [128, 128], "float32"), "WI": ("sbuf", [128, 384], "int32"), "PH": ("sbuf", [128, 128], "float16"),
+    "W32": ("sbuf", [128, 256], "float32"), "WI": ("sbuf", [128, 384], "int32"),
     "SL": ("sbuf", [128, 9 * 128], "uint16"), "FL": ("sbuf", [128, 21 * 66], "uint16"),
-    "CT": ("sbuf", [128, 768], "float16"), "ZH": ("sbuf", [128, 128], "float16"), "ZF": ("sbuf", [128, 32], "float32"),
-    "NE": ("sbuf", [128, 768], "bfloat16"), "DG": ("sbuf", [128, 18 * 128], "float16"),
-    "MH": ("sbuf", [128, 34 * 128], "float16"), "MB": ("sbuf", [128, 18 * 128], "bfloat16"), "MF": ("sbuf", [128, 22 * 128], "float32"),
+    "CT": ("sbuf", [128, 768], "float16"), "ZH": ("sbuf", [128, 128], "float16"), "ZF": ("sbuf", [128, 16], "float32"),
+    "ZX": ("sbuf", [128, 72], "float16"), "ZC": ("sbuf", [128, 48], "bfloat16"), "ZT": ("sbuf", [128, 48], "bfloat16"),
+    "NE": ("sbuf", [128, 15 * 128], "float16"), "DG": ("sbuf", [128, 6 * 384], "float16"), "CD": ("sbuf", [128, 3 * 384], "float16"),
+    "MH": ("sbuf", [128, 36 * 128], "float16"), "MB": ("sbuf", [128, 2 * 128 + 16], "bfloat16"),
+    "G3": ("sbuf", [128, 72], "float16"), "GW": ("sbuf", [128, 7 * 24], "float16"),
     "IR": ("sbuf", [128, 128], "bfloat16"), "GM": ("sbuf", [128, 128], "bfloat16"),
     "CI": ("sbuf", [128, 8], "int32"), "CF": ("sbuf", [128, 96], "float32"),
-    "LMi": ("sbuf", [128, 8], "int32"), "LMf": ("sbuf", [128, 8], "float32"),
-    "ACC": ("sbuf", [128, 24], "float32"), "PR": ("sbuf", [128, 24], "float32"), "SM": ("sbuf", [128, 128], "float32"),
+    "LMi": ("sbuf", [128, 8], "int32"), "LMh": ("sbuf", [128, 8], "float16"),
+    "ACC": ("sbuf", [128, 24], "float32"), "P1": ("sbuf", [128, 8 * 42], "float32"), "SM": ("sbuf", [128, 64], "float32"),
+    "PR": ("sbuf", [128, 112], "float32"), "G8": ("sbuf", [128, 8], "float32"), "WH": ("sbuf", [128, 8], "float16"),
     "X1": ("sbuf", [128, 16], "float32"), "X2": ("sbuf", [128, 48], "float32"), "X3": ("sbuf", [128, 96], "float32"),
-    "XS": ("sbuf", [128, 96], "float32"), "YO": ("sbuf", [128, 896], "float32"),
+    "YO": ("sbuf", [128, 896], "float32"),
     "PF0": ("psum", [128, H], "float32"), "PF1": ("psum", [128, H], "float32"),
     "PA": ("psum", [128, 512], "float32"), "PB": ("psum", [128, 512], "float32"),
     "PC": ("psum", [128, 512], "float32"), "PD": ("psum", [128, 512], "float32"),
 }
-SEMAPHORES = ["cv", "cs", "cp", "cg", "out", "aF", "aM", "aO", "a1", "a2", "a3", "rF", "rM", "rO", "r3",
-              "sF", "sM", "sN", "ownF", "ownM", "ow", "wall", "tb1", "tb2", "fall", "lm", "pi", "tu2", "tu4", "tu6",
-              "sO", "ownO", "oi", "y1", "y2"] + ["ft%d" % d for d in range(1, 8)] + ["fh%d" % d for d in HALF]
+SEMAPHORES = (["cv", "cs", "cp", "cg", "out", "a1", "a2", "a3", "r3", "lam", "sF2", "ow", "wa", "w1", "wb", "tc1", "tc2", "ts", "tp", "fall", "lm", "oi"]
+              + [k + x for k in ("a", "r", "s", "own") for x in "AFBO"] + ["tu%d" % d for d in EV]
+              + [k % d for k in ("ft%d", "fh%d", "y%d") for d in POS])
 
 
 def top(d):
@@ -56,23 +63,17 @@ def bits(engines):
     return sum(1 << e for e in engines)
 
 
-def slot3(lay):
-    return 24 * (lay % 4) + 12 * (lay // 4)
-
-
 def plan(T, topo):
     cores = list(T.cores)
     teams = [[r for r in range(N) if r == 0 or topo.may_write(cores[0], cores[r])]]
     teams.append([r for r in range(N) if r not in teams[0]])
     layer = {r: 4 * t + i for t in range(2) for i, r in enumerate(teams[t])}
-    relay = {}
+    ports = {}
     for r in range(N):
         far = teams[1 - layer[r] // 4]
-        ports = [c for c in topo.cores_of(cores[r]) if c != cores[r] and all(topo.may_write(c, cores[x]) for x in far)]
-        ports.sort(key=lambda c: topo.die(c) != topo.die(cores[r]))
-        for i, x in enumerate(far):
-            relay[r, x] = ports[i]
-    return cores, teams, layer, relay
+        p = [c for c in topo.cores_of(cores[r]) if c != cores[r] and all(topo.may_write(c, cores[x]) for x in far)]
+        ports[r] = ([c for c in p if topo.die(c) == topo.die(cores[r])][:2], [c for c in p if topo.die(c) != topo.die(cores[r])][:2])
+    return cores, teams, layer, ports
 
 
 def dst(topo, to, frm):
@@ -80,27 +81,37 @@ def dst(topo, to, frm):
     return DstId(rid=rid, pnc=pid)
 
 
-def relay_program(g, core, T, topo, cores, layer, a, x):
-    to = cores[x]
-    en = topo.engines(core, to)
-    wide = len(topo.engines(cores[a], core))
-    s = slot3(layer[a])
-    steps = (("rM", wide // 4, "aM", T.ldM[0], T.ldM[a]), ("rF", wide // 4, "aF", T.ldF[0], T.ldF[a]),
-             ("rO", wide // 4, "aO", T.ldO[0], T.ldO[layer[a]]), ("r3", wide, "a3", T.X3[:, 0:12], T.X3[:, s:s + 12]))
-    for here, n, there, src, out in steps:
-        g.wait_ge(T.sem[here], n)
-        g.remote_dma_fused([RemoteDMATransfer(dst_ids=[dst(topo, to, core)], dma_engine_mask=bits(en), remote_sem=T.sem[there],
-                                              src=src, dst=out)], local_sem=T.sem.out)
-    g.wait_ge(T.sem.out, len(steps) * len(en))
+SIDE = {"A": 0, "F": 1, "B": 1, "O": 1, "3": 0}
+
+
+def relay_program(g, core, T, topo, cores, layer, a, side, xs):
+    en = topo.engines(core, cores[xs[0]])
+    k = len(en) // 2
+    sent = 0
+    for m in [m for m in "AFBO3" if SIDE[m] == side]:
+        if m == "3":
+            s = 12 * layer[a]
+            items = [(xs, en, T.X3[:, 0:12], T.X3[:, s:s + 12])]
+            g.wait_ge(T.sem.r3, len(en))
+        else:
+            ld = T["ld" + m]
+            items = [([x], en[k * j:k * j + k], ld[j], ld[layer[a] if m == "O" else a]) for j, x in enumerate(xs)]
+            g.wait_ge(T.sem["r" + m], k)
+        g.remote_dma_fused([RemoteDMATransfer(dst_ids=[dst(topo, cores[x], core) for x in to], dma_engine_mask=bits(e), remote_sem=T.sem["a" + m],
+                                              src=src, dsts=[out for x in to]) for to, e, src, out in items], local_sem=T.sem.out)
+        sent += len(en)
+    g.wait_ge(T.sem.out, sent)
 
 
 def rank_program(g, core, T, topo):
-    cores, teams, layer, relay = plan(T, topo)
+    cores, teams, layer, ports = plan(T, topo)
     me = T.rank_of(core)
     if me is None:
-        for (a, x), c in relay.items():
-            if c == core:
-                relay_program(g, core, T, topo, cores, layer, a, x)
+        for a in range(N):
+            for side in (0, 1):
+                if core in ports[a][side]:
+                    far = teams[1 - layer[a] // 4]
+                    relay_program(g, core, T, topo, cores, layer, a, side, far[ports[a][side].index(core)::2])
         return
     lay = layer[me]
     team = lay // 4
@@ -110,8 +121,8 @@ def rank_program(g, core, T, topo):
     ops, wr, rd, users, phys = [], {}, {}, {}, {}
     hold = []
     pools = {"b": [(T[x], 0) for x in ("PA", "PB", "PC", "PD")], "f": [(T.PF0, 0), (T.PF1, 0)],
-             "G": [(T.GB, 1056 * i) for i in range(NG)], "c": [(T.CT, 0), (T.CT, 384)],
-             "r": [(T.RA, 0), (T.RB, 0), (T.RU, 0)], "R": [(T.RS, 0), (T.RT, 0)]}
+             "G": [(T.GB, 1056 * i) for i in range(NG)], "m": [(T.MX, H * i) for i in range(NM)], "c": [(T.CT, 0), (T.CT, 384)],
+             "r": [(T.RA, 0), (T.RB, 0)], "R": [(T.RS, 0)]}
 
     def new(pool):
         k = "%s#%d" % (pool, len(users)); users[k] = []
@@ -134,13 +145,13 @@ def rank_program(g, core, T, topo):
             if k in users:
                 users[k].append(i)
 
-    def part(k, a, b, s=1):
-        return (k, a, b, s)
+    def part(k, a, b, s=1, rows=128):
+        return (k, a, b, s, rows)
 
     def ap(x):
         if isinstance(x, tuple):
             t, o = phys[x[0]]
-            return t[:, o + x[1]:o + x[2]:x[3]] if x[3] > 1 else t[:, o + x[1]:o + x[2]]
+            return t[0:x[4], o + x[1]:o + x[2]:x[3]] if x[3] > 1 else t[0:x[4], o + x[1]:o + x[2]]
         return x
 
     def do(e, R, W, n, call):
@@ -166,9 +177,9 @@ def rank_program(g, core, T, topo):
 
     def ts(R, W, o, i, s1, s2, op0, op1=None, n=64):
         if op1 is None:
-            do("v", R, W, n, lambda q: vv.tensor_scalar(ap(o), ap(i), s1, None, op0))
+            do("v", R, W, n, lambda q: vv.tensor_scalar(ap(o), ap(i), ap(s1), None, op0))
         else:
-            do("v", R, W, n, lambda q: vv.tensor_scalar(ap(o), ap(i), s1, s2, op0, op1))
+            do("v", R, W, n, lambda q: vv.tensor_scalar(ap(o), ap(i), ap(s1), ap(s2), op0, op1))
 
     def tt(R, W, o, a, b, op, n=64):
         do("v", R, W, n, lambda q: vv.tensor_tensor(ap(o), ap(a), ap(b), op))
@@ -176,11 +187,17 @@ def rank_program(g, core, T, topo):
     def cp(R, W, o, i, e="v", n=64):
         do(e, R, W, n, lambda q: vv.tensor_copy(ap(o), ap(i)) if q == "v" else sc.activation(ap(o), ap(i), AF.Copy))
 
+    def fill(W, o, n):
+        do("v", [], W, n, lambda q: vv.memset(o, 0))
+
     def mm(R, W, items, n, beside=False):
         first = wr.get(W[0])
         step("p", R, W, n * CYCLE / 2, 0.0, lambda q: [pe.matmul(ap(o), ap(l), ap(r), a, z) for o, l, r, a, z in items])
         if beside:
-            ops[-1]["hard"].discard(first); ops[-1]["like"] = first
+            ops[-1]["hard"].discard(first)
+
+    def group(out, terms):
+        return [(out, l, r, j == 0, j == len(terms) - 1) for j, (l, r) in enumerate(terms)]
 
     def blk(t, i, n=1, w=128):
         return part(t, i * w, (i + n) * w) if isinstance(t, str) else t[:, i * w:(i + n) * w]
@@ -189,8 +206,8 @@ def rank_program(g, core, T, topo):
         if "bias" not in MEMO:
             bias = [SMALL if o["busy"] < 0.6 else 0.0 for o in ops]
             for i, o in enumerate(ops):
-                bias[i] += 100.0 - i if o["sem"] in ("sM", "sF", "sN") else 50.0 if o["sem"] in ("wall", "tb1") else 0.0
-            big = [i for i, o in enumerate(ops) if o["busy"] > 0.5 and o["e"] in "vsp" and o["deps"]]
+                bias[i] += 100.0 - i if o["sem"] in ("sA", "sF", "sF2", "sB", "lam") else 50.0 if o["sem"] in ("wa", "tc1") else 0.0
+            big = [i for i, o in enumerate(ops) if o["busy"] > 0.4 and o["e"] in "vsp" and o["deps"]]
             best, seed = order(bias)[0], SEED
             now, top_ = best, bias
             for k in range(TRIES):
@@ -217,10 +234,18 @@ def rank_program(g, core, T, topo):
             for d in o["deps"]:
                 after[d].append(i)
         span = lambda o: o["busy"] + (2.0 + o["late"][0] / 250.0 if isinstance(o["late"], tuple) else o["late"]) + WAKE
+        behind = {o["next"]: [i] for i, o in enumerate(ops) if "next" in o}
+        left = [len(o["deps"]) + ("next" in o) for o in ops]
+        line = [i for i in range(n) if not left[i]]
+        for i in line:
+            for j in after[i] + behind.get(i, []):
+                left[j] -= 1
+                if not left[j]:
+                    line.append(j)
         rank = [0.0] * n
-        for i in range(n - 1, -1, -1):
-            rank[i] = span(ops[i]) + max([rank[j] for j in after[i]] + [0.0])
-        left = [len(o["deps"]) for o in ops]
+        for i in line[::-1]:
+            rank[i] = max([span(ops[i]) + rank[j] for j in after[i]] + [ops[i]["busy"] + rank[j] for j in behind.get(i, [])] + [span(ops[i])])
+        left = [len(o["deps"]) + ("next" in o) for o in ops]
         ready = [i for i in range(n) if not left[i]]
         end, free, pipe, seq = {}, {}, [0.0], []
         slots = {p: [None] * len(v) for p, v in pools.items()}
@@ -257,14 +282,14 @@ def rank_program(g, core, T, topo):
                 slots[k[0]][x] = k; where[k] = pools[k[0]][x]
             free[q] = t + o["busy"]
             if isinstance(o["late"], tuple):
-                pipe[0] = max(pipe[0], t + 1.8) + o["late"][0] / 320.0 + o["late"][1] * 0.0025
+                pipe[0] = max(pipe[0], t + 1.8) + o["late"][0] / 250.0 + o["late"][1] * 0.0025
                 end[i] = pipe[0]
             else:
                 end[i] = free[q] + o["late"]
             for k in uses.get(i, []):
                 open_[k] -= 1
             seq.append((i, q))
-            for j in after[i]:
+            for j in after[i] + behind.get(i, []):
                 left[j] -= 1
                 if not left[j]:
                     ready.append(j)
@@ -297,153 +322,182 @@ def rank_program(g, core, T, topo):
         for s, k in count.items():
             g.wait_ge(T.sem[s], k)
 
-    for t, sm, sf in ((1 - team, "sM", "sF"), (team, "sN", "sN")):
-        l = 4 * t
-        dma("s", sm, ["yq"], [sm + "b"], [(T.stM[k, 112, 0:7], T.lam[t]) for k in range(l, l + 4) if k != lay], 0, 16)
-        dma("y", sm, [], [sm + "a"],
-            [(T.stM[l:l + 4, 0:112, :], T.mp[16 * l:16 * l + 64, :]), (T.stM[l:l + 4, 113:128, :], T.mp[0:60, 0:128]),
-             (T.stM[l:l + 4, 112, 7:128], T.mp[0:4, 0:121])], 256, 96)
-        dma("y", sf, [], [sf + "c"], [(T.stF[l:l + 4], T.ft[16 * l:16 * l + 64, :])], 256, 16)
-    dma("s", "ownM", ["sMa"], ["ownM"], [(T.ldM[me, 0:112, :], T.mp[16 * lay:16 * lay + 16, :]), (T.ldM[me, 112, 0:7], T.lam[team])], 56, 16)
-    dma("s", "ownF", ["sMa"], ["ownF"], [(T.ldF[me], T.ft[16 * lay:16 * lay + 16, :])], 64, 16)
+    AD, BD = (2, 3, 1, 4), (5, 6, 7)
+    rows = lambda t, k: t[:, 32 * k:32 * k + 32, :]
+    dma("y", "sA", [], ["sA"], [(rows(T.stA, k), blk(T.mp, d - 1)) for k, d in enumerate(AD)], 256, 512)
+    dma("y", "sF", [], ["sF"], [(T.stF[:], T.ft[:])], 512, 16)
+    dma("y", "sB", [], ["sB"], [(rows(T.stB, k), blk(T.mp, d - 1)) for k, d in enumerate(BD)], 192, 384)
+    hold.append("sB")
+    dma("y", "lam", [], ["lam"], [(T.stB[k, 96, 0:7], T.lam[k // 4]) for k in range(N)]
+        + [(T.stB[:, 96, 7:64], T.mp[0:8, 0:57]), (T.stB[:, 97:128, :], T.mp[0:32, 0:496])], 64, 48)
     do("g", [], ["pi0", "gq"], 130, lambda q: g.iota(T.CI[:, 0:1], [[0, 1]], 0, 1))
     do("g", [], ["IR"], 400, lambda q: g.iota(T.IR[:], [[1, 128]], 0, 0, allow_small_or_imprecise_dtypes=True))
     do("g", [], ["GM"], 400, lambda q: g.iota(T.GM[:], [[16, 8], [0, 16]], 0, 0, allow_small_or_imprecise_dtypes=True))
-    on = topo.engines(core, relay[me, far[0]])
     off = topo.engines(core, cores[near[0]])
-    nof, q4 = len(off), len(on) // 4
-    for keys, sem, st, ld in ((["sMa", "sMb"], "rM", T.stM, T.ldM), (["sFc"], "rF", T.stF, T.ldF)):
-        send(keys, [sem], [([relay[me, x]], on[q4 * i:q4 * i + q4], sem, st[layer[x]], ld[0]) for i, x in enumerate(far)], 3.0 if sem == "rM" else 0.3)
-    send(["sNa", "sNb", "sNc"], ["sent"], [([cores[x]], off[2 * i + k:2 * i + k + 1], sem, st[layer[x]], ld[me])
-                                           for i, x in enumerate(near) for k, (sem, st, ld) in enumerate((("aM", T.stM, T.ldM), ("aF", T.stF, T.ldF)))])
-    do("g", ["sent"], ["TB"], 4200, lambda q: g.iota(T.TB[:], [[0, V]], 0, 0))
-    do("g", ["TB"], ["TC"], 4200, lambda q: g.iota(T.TC[:], [[0, V]], 0, 0))
-    do("g", ["TC"], ["TP"], 4200, lambda q: g.iota(T.TP[:], [[0, V]], 0, 0, allow_small_or_imprecise_dtypes=True))
-    arrive("aM", 3 + 4 * nof, ["rM"], ["ldM"], 8.0)
-    arrive("aF", 3 + 4 * nof, ["rF"], ["ldF"], 8.3)
+    on = [e for e in topo.engines(core, ports[me][0][0]) if e not in off]
+    nof, q4 = len(off), len(off) // 4
+
+    def spread(m, keys, slot, busy=0.3):
+        st, ld = T["st" + m], T["ld" + m]
+        of = (lambda x: x) if m == "O" else (lambda x: layer[x])
+        send(keys, ["sent" + m], [([ports[me][SIDE[m]][i % 2]], on[q4 * i:q4 * i + q4], "r" + m, st[of(x)], ld[i // 2]) for i, x in enumerate(far)]
+             + [([cores[x]], off[q4 * i:q4 * i + q4], "a" + m, st[of(x)], ld[slot]) for i, x in enumerate(near)], busy)
+        dma("s" if m != "O" else "y", "own" + m, keys, ["own" + m], [(ld[slot], st[of(me)])], 48, 16)
+
+    spread("A", ["sA"], me, 3.0)
+    spread("F", ["sF"], me)
+    spread("B", ["sB", "lam"], me)
+    for m, late in (("A", ARR_A), ("F", ARR_F), ("B", ARR_B)):
+        arrive("a" + m, 3 * q4 + 2 * nof, ["sent" + m], ["ld" + m], late)
+    dma("s", "ow", ["sB"], ["OWi"], [(blk(T.OWi, i), blk(T.mp, d - 1)) for i, d in enumerate(OD)], 192, 384)
+    fill(["TC"], T.TC[:], V)
+    fill(["TP"], T.TP[:], H)
 
     CF = T.CF
+    IR, GM = T.IR, T.GM
+    G8 = GM[:, 0:128:16]
     for j in range(3):
         ts(["pi0"], ["ci%d" % j], T.CI[:, 1 + j:2 + j], T.CI[:, 0:1], 4 + j, 1, A.logical_shift_right, A.bitwise_and)
     ts(["pi0"], ["ci3"], T.CI[:, 4:5], T.CI[:, 0:1], 15, None, A.bitwise_and)
-    cp(["pi0", "ci0", "ci1", "ci2", "ci3"], ["c0"], CF[:, 0:5], T.CI[:, 0:5])
-    XO, PX, GX, QM, IS, IN, QT, NI, I2 = 8, 16, 32, 40, 56, 64, 72, 80, 88
+    ts(["pi0"], ["ci4"], T.CI[:, 5:6], T.CI[:, 0:1], 1, 7, A.logical_shift_right, A.bitwise_and)
+    ts(["pi0"], ["ci5"], T.CI[:, 6:7], T.CI[:, 0:1], 1, None, A.bitwise_and)
+    cp(["pi0"] + ["ci%d" % j for j in range(6)], ["c0"], CF[:, 0:7], T.CI[:, 0:7])
+    XO, PX, SC, GX, QM, IS, EX = 8, 16, 24, 32, 40, 56, 64
     col = lambda base, i: CF[:, base + i:base + i + 1]
+    tb = {1: 0, 2: 1, 4: 2}
+    isr = lambda d: col(IS, tb[top(d)])
+    isj = lambda d: col(1, tb[top(d)])
     ts(["c0"], ["xo0"], col(XO, 0), col(0, 0), 0.0, None, A.mult)
     for j in range(3):
         ts(["c0"], ["xo%d" % (1 << j)], col(XO, 1 << j), col(1, j), -32.0 * (1 << j), 16.0 * (1 << j), A.mult, A.add)
-    ts(["c0"], ["isr"], CF[:, 5:8], CF[:, 1:4], -1.0, 1.0, A.mult, A.add)
-    ts(["c0"], ["nisr"], CF[:, NI:NI + 3], CF[:, 1:4], 1.0, None, A.subtract)
+    ts(["c0"], ["isr"], CF[:, IS:IS + 3], CF[:, 1:4], -1.0, 1.0, A.mult, A.add)
     ts(["c0", "IR"], ["qm"], CF[:, QM:QM + 16], T.IR[:, 0:16], col(0, 4), None, A.is_equal)
-    ts(["c0"], ["p16"], col(QT, 4), col(0, 0), 16.0, None, A.mult)
     tt(["xo1", "xo2"], ["xo3"], col(XO, 3), col(XO, 1), col(XO, 2), A.add)
     ts(["xo1", "xo2", "xo3", "xo4"], ["xo5"], CF[:, XO + 5:XO + 8], CF[:, XO + 1:XO + 4], col(XO, 4), None, A.add)
     xo = ["xo%d" % i for i in range(6)]
     ts(xo + ["c0"], ["px"], CF[:, PX:PX + 8], CF[:, XO:XO + 8], col(0, 0), None, A.add)
     ts(["px"], ["gx"], CF[:, GX:GX + 8], CF[:, PX:PX + 8], col(0, 4), None, A.subtract)
-    tb = {1: 0, 2: 1, 4: 2}
-    isr = lambda d: col(5, tb[top(d)])
-    nisr = lambda d: col(NI, tb[top(d)])
-    for i, d in enumerate((3, 5, 6, 7)):
-        ts(["c0"] + xo, ["qt%d" % d], col(QT, i), col(XO, d ^ top(d)), col(1, tb[top(d)]), col(0, 0), A.mult, A.add)
-    ts(["gx"], ["ind0"], CF[:, IN:IN + 8], CF[:, GX:GX + 8], 16.0 * me, None, A.is_equal)
-    mats, used = {}, {"MH": 0, "MB": 0, "MF": 0, "ZH": 0, "ZF": 0}
-    cols = ["px", "gx", "qm", "isr", "nisr", "IR", "GM", "p16", "qt3", "qt5", "qt6", "qt7", "ind"]
+    for i, (src, k) in enumerate(((isr(1), 128.0), (isr(1), -2047.0), (isj(1), 128.0), (isj(1), -2047.0))):
+        ts(["isr", "c0"], ["sc%d" % i], col(SC, i), src, k, None, A.mult)
+    for i, (q_, side) in enumerate(((2, isr), (1, isj), (1, isr), (2, isj))):
+        tt(["isr", "qm"], ["sc%d" % (4 + i)], col(SC, 4 + i), col(QM, q_), side(1), A.mult)
+    ts(["c0"], ["ex0"], col(EX, 0), col(0, 0), 16.0, None, A.mult)
+    ts(["c0"], ["ex1"], col(EX, 1), col(0, 6), -32.0, 16.0, A.mult, A.add)
+    tt(["ex0"], ["ex1"], col(EX, 1), col(EX, 1), col(EX, 0), A.add)
+    ts(["c0"], ["ex2"], col(EX, 2), col(0, 5), 1.0, None, A.add)
+    ts(["c0"], ["ex3"], CF[:, EX + 3:EX + 5], CF[:, 2:4], 2.0, None, A.add)
+    ts(["isr"], ["ex5"], CF[:, EX + 5:EX + 7], CF[:, IS + 1:IS + 3], 2.0, None, A.add)
+    ts(["c0"], ["one"], col(EX, 7), col(0, 0), 0.0, 1.0, A.mult, A.add)
+    mats, used = {}, {"MH": 0, "MB": 0, "CD": 0, "ZH": 0, "ZF": 0}
+    cols = ["px", "gx", "qm", "isr", "IR", "GM", "ex0", "ex1", "ex2", "ex3", "ex5"] + ["sc%d" % i for i in range(8)]
 
-    def mat(name, buf, row, s1, s2, op0=A.is_equal, parts=128):
+    def mat(name, buf, row, s1, s2, op0=A.is_equal, op1=A.mult, parts=128):
         o = 128 * used[buf]; used[buf] += 1
         mats[name] = (buf, o)
-        ts(cols, [name], T[buf][0:parts, o:o + 128], row[0:parts, :], s1, s2, op0, A.mult)
+        ts(cols, [name], T[buf][0:parts, o:o + 128], row[0:parts, :], s1, s2, op0, op1)
 
     def M(name, parts=128):
         buf, o = mats[name]
         return T[buf][0:parts, o:o + 128]
 
-    def smat(x):
-        mat("A%d" % x, "MH", IR, col(PX, x), 128.0)
-        mat("B%d" % x, "MH", IR, col(PX, x), -2047.0)
-
-    def zmat(q, x, buf="ZH"):
-        name = "Z%d_%d" % (q, x); o = 8 * used[buf]; used[buf] += 1
+    def zmat(name, x, pick, buf="ZH"):
+        o = 8 * used[buf]; used[buf] += 1
         mats[name] = (buf, o)
-        ts(cols, [name], T[buf][:, o:o + 8], GM[:, 0:128:16], col(GX, x), col(QM, q), A.is_equal, A.mult)
+        ts(cols, [name], T[buf][:, o:o + 8], G8, col(GX, x), pick, A.is_equal, A.mult)
 
-    IR, GM = T.IR, T.GM
-    for i, (src, k) in enumerate(((col(5, 0), 128.0), (col(5, 0), -2047.0), (col(1, 0), 128.0), (col(1, 0), -2047.0))):
-        ts(["isr", "c0"], ["sc%d" % i], col(24, i), src, k, None, A.mult)
-    cols += ["sc0", "sc1", "sc2", "sc3"]
     for i, side in enumerate("rj"):
         for x in (2, 3):
-            mat("A%d%s" % (x, side), "MH", IR, col(PX, x), col(24, 2 * i))
-            mat("B%d%s" % (x, side), "MH", IR, col(PX, x), col(24, 2 * i + 1))
-    mat("E1", "MH", IR, col(PX, 0), col(1, 0))
-    smat(2); smat(3)
+            mat("A%d%s" % (x, side), "MH", IR, col(PX, x), col(SC, 2 * i))
+            mat("B%d%s" % (x, side), "MH", IR, col(PX, x), col(SC, 2 * i + 1))
+    zmat("Zr1", 2, col(SC, 4)); zmat("Zr2", 3, col(SC, 5)); zmat("Zj1", 3, col(SC, 6)); zmat("Zj2", 2, col(SC, 7))
+    mat("I16", "MH", IR, col(PX, 0), 1.0)
     for t in (1, 2, 4):
         mat("D%d" % t, "MH", IR, col(PX, 0), isr(t))
     for d in range(1, 8):
         mat("P%d" % d, "MH", IR, col(PX, d), isr(d))
     mat("I", "MB", IR, col(PX, 0), 1.0)
     mat("nI", "MB", IR, col(PX, 0), -1.0)
-    for t in (1, 2, 4):
-        mat("bD%d" % t, "MB", IR, col(PX, 0), isr(t)); mat("nD%d" % t, "MB", IR, col(PX, 0), nisr(t))
-        mat("bP%d" % t, "MB", IR, col(PX, t), isr(t)); mat("nP%d" % t, "MB", IR, col(PX, t), nisr(t))
-    zmat(2, 2); zmat(1, 3)
-    mat("I16", "MH", IR, col(PX, 0), 1.0)
-    mat("ET", "MF", GM, CF[0:8, QT + 4:QT + 5], 1.0, parts=8)
-    for d, p in POS.items():
-        cp(["isr"], ["is%d" % d], col(IS, p), isr(d))
-    for i, d in enumerate((3, 5, 6, 7)):
-        mat("Q%d" % d, "MB", IR, col(QT, i), 1.0)
-    for x in (1, 4, 5, 6, 7):
-        smat(x)
-    for q in (2, 4, 6, 1, 3, 5, 7, 8, 9):
-        zmat(q, 1)
-    for x in range(2, 8):
-        zmat(0, x, "ZF" if x in ONS else "ZH")
+    G2, nG2 = T.MB[:, 256:264], T.MB[:, 264:272]
+    ts(cols, ["G2"], G2, G8, col(GX, 0), 2.0, A.is_equal, A.mult)
+    ts(cols, ["nG2"], nG2, G8, col(GX, 0), -2.0, A.is_equal, A.mult)
+    ts(cols, ["G8"], T.G8[:], G8, col(GX, 0), None, A.is_equal)
     for x in range(8):
-        mat("S%d" % x, "MF", GM, col(GX, x), 1.0)
-    for x, y in ((0, 1), (0, 2), (0, 4), (0, 6), (1, 3), (1, 5), (1, 7)):
-        mats["S%d_%d" % (x, y)] = ("MF", 128 * used["MF"]); used["MF"] += 1
-        tt(["S%d" % x, "S%d" % y], ["S%d_%d" % (x, y)], M("S%d_%d" % (x, y)), M("S%d" % x), M("S%d" % y), A.add, n=256)
-    ts(["ind0"], ["ind"], CF[:, I2:I2 + 8], CF[:, IN:IN + 8], col(IN, 0), None, A.add)
-    mat("O0", "MF", GM, 64.0, 1.0, op0=A.is_lt)
-    mat("O1", "MF", GM, 64.0, 1.0, op0=A.is_ge)
-    for i, d in enumerate((3, 5, 7, 0)):
-        ts(["ind", "IR"], ["im%d" % d], T.XS[:, 72 + 3 * i:75 + 3 * i], IR[:, 0:3], 0.0, col(I2, d), A.mult, A.add)
-    cp(["im3", "im5", "im7", "im0"], ["im"], T.XS[:, 84:96], T.XS[:, 72:84])
-    s3 = slot3(lay)
-    ts(["IR"], ["X3"], T.X3[:, s3:s3 + 12], IR[:, 0:12], 0.0, None, A.mult)
+        ts(cols, ["zx%d" % x], blk(T.ZX, x, 1, 8), G8, col(GX, x), None, A.is_equal)
+    ts(cols, ["zx8"], blk(T.ZX, 8, 1, 8), G8, col(GX, 0), col(QM, 0), A.is_equal, A.mult)
+    zx = ["zx%d" % x for x in range(9)]
+    ts(zx + cols, ["ZC"], T.ZC[:], T.ZX[:, 16:64], col(EX, 2), None, A.mult)
+    for t in (1, 2, 4):
+        for k, s in enumerate((1.0, isr(t), isj(t))):
+            ts(zx + cols, ["g3%d%d" % (t, k)], blk(T.G3, 3 * tb[t] + k, 1, 8), T.ZX[:, 0:8], s, None, A.mult)
+    b = new("b")
+    mm(zx, [b], [x for d in range(1, 8) for x in group(part(b, 8 * d - 8, 8 * d, rows=8), [(blk(T.ZX, 8, 1, 8), blk(T.ZX, k, 1, 8)) for k in (0, d)])], 128)
+    cp([], [b, "PR"], T.PR[0:8, 0:56], part(b, 0, 56, rows=8))
+    for i, d in enumerate(OD):
+        for t in (0, 1):
+            o = 56 + 8 * (2 * i + t)
+            ts(["PR", "IR"], ["own%d%d" % (d, t)], T.PR[0:8, o:o + 8], IR[0:8, 0:8], float(t), T.PR[0:8, 8 * d - 8 + me:8 * d - 7 + me], A.is_equal, A.mult)
+    mat("B0", "MH", GM, CF[0:8, EX:EX + 1], 1.0, parts=8)
+    mat("B1", "MH", GM, CF[0:8, EX + 1:EX + 2], 1.0, parts=8)
+    mat("BT", "MH", GM, 64.0, CF[0:8, 0:1], A.is_ge, A.is_equal, parts=8)
+    for x in range(1, 8):
+        mat("A%d" % x, "MH", IR, col(PX, x), 128.0)
+        mat("B%d" % (10 + x), "MH", IR, col(PX, x), -2047.0)
+    for q in (2, 4, 6, 1, 3, 5, 7, 8, 9):
+        zmat("Z%d" % q, 1, col(QM, q))
+    for t, codes in ((1, (1.0, 2.0, 3.0)), (2, (1.0, col(EX, 3), col(EX, 5))), (4, (1.0, col(EX, 4), col(EX, 6)))):
+        for k, s in enumerate(codes):
+            mat("cd%d%d" % (t, k), "CD", IR, col(PX, 0), s)
+    slot = {"X1": (T.X1, 4 * (lay % 4), 4), "X2": (T.X2, 12 * (lay % 4), 12), "X3": (T.X3, 12 * lay, 12)}
+    for k, (buf, s, w) in slot.items():
+        fill([k], buf[:, s:s + w], w)
+    cp(["OWi"], ["OW"], T.OW[:], T.OWi[:], n=384)
 
-    LM, LF = ["ldM", "ownM"], ["ldF", "ownF"]
-    dma("y", "wall", LM, ["Wall"], [(T.Wall[:], T.ldM[:, 0:112, :])], 448, 128)
-    dma("y", "tb1", LM, ["TB"], [(T.TB[q:128:16, :], T.ldM[:, q:112:7, :]) for q in (2, 1)], 128, 256)
+    LA, LF, LB = ["ldA", "ownA"], ["ldF", "ownF"], ["ldB", "ownB"]
+    dma("y", "wa", LA, ["WallA"], [(blk(T.Wall, d - 1), rows(T.ldA, k)) for k, d in enumerate(AD[:2])], 128, 256)
+    dma("y", "tc1", LA, ["TC"], [(T.TC[d - 1:128:16, :], rows(T.ldA, k)) for k, d in enumerate(AD[:2])], 128, 16)
+    dma("y", "w1", LA, ["Wall1"], [(blk(T.Wall, AD[k] - 1), rows(T.ldA, k)) for k in (2, 3)], 128, 256)
     dma("y", "fall", LF, ["Fall"], [(T.Fall[:, 0:V], T.ldF[:])], 512, 128)
-    dma("y", "lm", LM + LF, ["LMi"], [(T.LMi[0:8, 0:7], T.ldM[:, 112, 0:7])], 0, 16)
+    dma("y", "lm", LB, ["LMi"], [(T.LMi[0:8, 0:7], T.ldB[:, 96, 0:7])], 0, 16)
+    dma("y", "wb", LB, ["WallB"], [(blk(T.Wall, d - 1), rows(T.ldB, k)) for k, d in enumerate(BD)], 192, 384)
+    cp(["Fall"], ["Fw"], T.Fall[:, V:V + 16], T.Fall[:, 0:16], "vs")
 
-    def load_ft(d):
-        at = V + 16 + V * POS[d]
-        if d in (1, 2, 4):
-            do("v", [], ["FT%d" % d], H, lambda q: vv.memset(T.Fall[:, at:at + V], 0.0))
-        else:
-            cp(["FH3", "FH5"], ["FT%d" % d], T.Fall[:, at:at + V], T.FH[:, 0:V], "s", n=V)
-        ts(["IR"], ["of%d" % d], blk(T.OF, POS[d], 1, 66), IR[:, 0:66], 0.0, float(at), A.mult, A.add)
-        pairs, a = [], 0
+    def runs(src, same):
+        out, a = [], 0
         while a < N:
             b = a + 1
-            if not a & top(d):
-                while b < N and not b & top(d) and b ^ d == (b - 1 ^ d) + 1:
-                    b += 1
-                pairs.append((T.Fall[16 * a:16 * b, at:at + V], T.ldF[a ^ d:(a ^ d) + b - a]))
-            a = b
-        dma("y", "ft%d" % d, LF, ["FT%d" % d], pairs, 256, 64)
+            while b < N and src(b) == src(b - 1) + 1 and same(a, b):
+                b += 1
+            out.append((a, b)); a = b
+        return out
 
-    turn = {"d": 0}
+    def load_features(d):
+        at, t = V + 16 + V * POS[d], top(d)
+        if POS[d] < 3:
+            fill(["FT%d" % d], T.Fall[:, at:at + V], H)
+        else:
+            cp(["TP"], ["FT%d" % d], T.Fall[:, at:at + V], T.TP[:], "s", n=V)
+        ts(["IR"], ["of%d" % d], blk(T.OF, POS[d], 1, 66), IR[:, 0:66], 0.0, float(at), A.mult, A.add)
+        same = lambda a, b: a & t == b & t
+        dma("y", "ft%d" % d, LF, ["FT%d" % d],
+            [(T.Fall[16 * a:16 * b, at:at + V], T.ldF[a ^ d:(a ^ d) + b - a]) for a, b in runs(lambda a: a ^ d, same) if not a & t], 256, 64)
+        r = lambda a: a ^ d if a & t else a
+        pairs = []
+        for a, b in runs(r, same):
+            h = H if a & t else 0
+            pairs.append((T.FH[16 * a:16 * b, 1040 * POS[d]:1040 * (POS[d] + 1)], T.Fall[16 * r(a):16 * (r(a) + b - a), h:h + 1040]))
+        dma("y", "fh%d" % d, ["Fall", "Fw"], ["FH%d" % d], pairs, 260, 128)
 
-    def lists(c, items):
+    for d in POS:
+        load_features(d)
+
+    place = {}
+
+    def lists(items):
         b = new("b"); its = []; R = []
-        first = POS[items[0][0]] + 7 * c
-        for i, (d, buf, k, key) in enumerate(items):
+        first = len(place)
+        for i, (d, c, buf, k, key) in enumerate(items):
             o, s = i * 66, k * 128
+            place[d, c] = first + i
             its += [(part(b, o, o + 66), M("D%d" % top(d)), blk(T.OF, POS[d], 1, 66), True, False),
                     (part(b, o, o + 66), M("D%d" % top(d)), buf[:, s:s + 66], False, False),
                     (part(b, o, o + 64), M("P%d" % d), buf[:, s + 64:s + 128], False, False),
@@ -451,309 +505,273 @@ def rank_program(g, core, T, topo):
             R += [key, "D%d" % top(d), "P%d" % d, "of%d" % d]
         n = len(items) * 66
         mm(R, [b], its, 4 * n)
-        cp([], [b] + ["FL%d_%d" % (it[0], c) for it in items], T.FL[:, first * 66:first * 66 + n], part(b, 0, n), n=n)
+        cp([], [b] + ["FL%d_%d" % it[:2] for it in items], T.FL[:, first * 66:first * 66 + n], part(b, 0, n), n=n)
 
-    def slists(slot, items):
-        b = new("b"); its = []; R = []
-        for i, (x, u, h, keys) in enumerate(items):
-            its += [(blk(b, i), M("A%d" % x), u, True, False), (blk(b, i), M("B%d" % x), h, False, True)]
-            R += keys + ["A%d" % x, "B%d" % x]
-        n = len(items)
-        mm(R, [b], its, 256 * n)
-        ts([], [b] + ["SL%d" % (slot + i) for i in range(n)], blk(T.SL, slot, n), blk(b, 0, n), float(2047 * HB), None, A.add, n=128 * n)
+    def stored(out, key, n, terms, R):
+        b = new("b")
+        mm(R, [b], [x for o, w, t in terms for x in group(part(b, o, o + w), t)], sum(w * len(t) for o, w, t in terms))
+        ts([], [b] + key, out, part(b, 0, n), float(2047 * HB), None, A.add, n=n)
 
-    def compose(e, win, slot, keys):
-        row = new("r" if e == "v" else "R")
-        cp(keys + ["SL%d" % slot], [row], part(row, 0, V), T[win][:, 0:V].indirect(blk(T.SL, slot)), e, n=V * GATHER)
-        return row
+    named = {}
 
-    def extract(row, zs):
-        b = new("b"); n = len(zs)
-        buf, o = mats[zs[0]]
-        k = 16 if row[0] == "r" else 4
-        for s0 in range(0, 16, k):
-            mm([row] + list(zs), [b], [(part(b, s, 128 * n, 16), part(row, s, V, 16), T[buf][:, o:o + 8 * n], True, True) for s in range(s0, s0 + k)],
-               1024, s0 > 0)
+    def long_step(name):
+        named[name] = len(ops) - 1
+        ops[-1]["e"] = "v" if name in LONG["v"] else "s"
+
+    def compose(name, win, slot, keys, row):
+        cp(keys + ["SL%d" % slot], [row[0]], row[1], T[win][:, 0:V].indirect(blk(T.SL, slot)), "vs", n=V * GATHER)
+        long_step(name)
+
+    def turn(items, R, slow=False):
+        b = new("b"); o = 0
+        k = 4 if slow else 16
+        for row, z, n in items:
+            for s0 in range(0, 16, k):
+                mm(R, [b], [(part(b, o + s, o + 128 * n, 16), row(s), z, True, True) for s in range(s0, s0 + k)], 1024, o + s0 > 0)
+            o += 128 * n
         c = new("c")
-        cp([], [b, c], blk(c, 0, n), blk(b, 0, n), n=128 * n)
+        cp([], [b, c], part(c, 0, o), part(b, 0, o), n=o)
+        return c
+
+    def back(c, n):
         b = new("b")
         mm([c, "I16"], [b], [(blk(b, i), blk(c, i), M("I16"), True, True) for i in range(n)], 128 * n)
         return b
 
-    def take(b, i, n, out, keys):
-        cp([], [b] + keys, out, blk(b, i, n), n=128 * n)
+    def extract(row, zs):
+        buf, o = mats[zs[0]]
+        return turn([(lambda s: part(row, s, V, 16), T[buf][:, o:o + 8 * len(zs)], len(zs))], [row] + list(zs), row[0] == "R")
+
+    def take(b, i, n, out, keys, e="v"):
+        cp([], [b] + keys, out, blk(b, i, n), e, n=128 * n)
 
     def judge(d, c):
         G = new("G")
-        o = (POS[d] + 7 * c) * 66
+        o, e = place[d, c] * 66, 3 * POS[d] + c
         src = T.Fall[:, 0:2 * V + 16 + V * POS[d]].indirect(T.FL[:, o:o + 65])
         R = ["Fall", "Fw", "FL%d_%d" % (d, c)] + ["FT%d" % x for x in POS if POS[x] <= POS[d]]
-        sub = (d, c) in SUB
-        if sub:
-            tt(R + ["FH%d" % d], [G], part(G, 0, 1040), src, blk(T.FH, HALF[d], 1, 1040), A.subtract, n=1040 * GATHER)
+        fh = 1040 * POS[d]
+        if "J%d%d" % (d, c) in LONG["s"]:
+            cp(R, [G], part(G, 0, 1040), src, "s", n=1040 * GATHER)
+            long_step("J%d%d" % (d, c))
+            pf = new("f")
+            for k in (0, 512):
+                mm([G, "I", "nI", "FH%d" % d], [pf], group(part(pf, k, k + 512), [(M("I"), T.FH[:, fh + k:fh + k + 512]), (M("nI"), T.FH[:, fh + k + 1:fh + k + 513]),
+                                                                                   (M("nI"), part(G, k, k + 512)), (M("I"), part(G, k + 1, k + 513))]), 2 * H, k > 0)
+            acc = T.ACC[:, e:e + 1]; src = part(pf, 0, H)
+            do("vs", [], [pf, G, "sum%d" % e], H + 150,
+               lambda q: vv.tensor_reduce(acc, ap(src), AxisListType.X, A.add, apply_absolute_value=True) if q == "v"
+               else sc.activation(ap(part(G, 0, H)), ap(src), AF.Abs, accum_out=acc))
+            long_step("A%d%d" % (d, c))
         else:
-            cp(R, [G], part(G, 0, 1040), src, FORCE.get((d, c), "vs"), n=1040 * GATHER)
-        pf = new("f")
-        m = "I" if d == top(d) else "Q%d" % d
-        t = tb[top(d)]
-        for k in (0, 512):
-            o = part(pf, k, k + 512)
-            its = [] if sub else [(o, M(m), T.SH[:, t * H + k:t * H + k + 512], True, False)]
-            its += [(o, M("I"), part(G, k, k + 512), sub, False), (o, M("nI"), part(G, k + 1, k + 513), False, True)]
-            mm([G, "I", "nI"] + ([] if sub else ["SH%d" % t, m]), [pf], its, 512 * len(its), k > 0)
-        acc = T.ACC[:, 3 * POS[d] + c:3 * POS[d] + c + 1]; src = part(pf, 0, H)
-        do("vs", [], [pf, G, "ACC%d_%d" % (d, c)], H,
-           lambda q: vv.tensor_reduce(acc, ap(src), AxisListType.X, A.add, apply_absolute_value=True) if q == "v"
-           else sc.activation(ap(part(G, 0, H)), ap(src), AF.Abs, accum_out=acc))
-
-    def steps_of_r(t):
-        pf = new("f")
-        F = T.Fall
-        for k in (0, 512):
-            o = part(pf, k, k + 512)
-            its = [(o, M("bD%d" % t), F[:, k + 1:k + 513], True, False), (o, M("nD%d" % t), F[:, k:k + 512], False, False),
-                   (o, M("bP%d" % t), F[:, H + k + 1:H + k + 513], False, False), (o, M("nP%d" % t), F[:, H + k:H + k + 512], False, True)]
-            mm(["Fall", "Fw", "bD%d" % t, "nD%d" % t, "bP%d" % t, "nP%d" % t], [pf], its, 2 * H, k > 0)
-        cp([], [pf, "SH%d" % tb[t]], T.SH[:, tb[t] * H:(tb[t] + 1) * H], part(pf, 0, H), "vs", n=H)
-
-    SM = T.SM
-    WW, WR, CU, CT, T1, T2 = 0, 8, 16, 20, 24, 28
+            tt(R + ["FH%d" % d], [G], part(G, 0, 1040), src, T.FH[:, fh:fh + 1040], A.subtract, n=1040 * GATHER)
+            long_step("J%d%d" % (d, c))
+            m = new("m")
+            do("v", [G], [m], H // 2, lambda q: vv.tensor_tensor_scan(ap(part(m, 0, H)), ap(part(G, 0, H)), ap(part(G, 1, H + 1)), 64.0, A.min, A.max))
+            b = new("b")
+            mm([G, m, "G2", "nG2"], [b], group(part(b, 0, 8), [(blk(G, k), nG2) for k in range(8)] + [(blk(m, k), G2) for k in range(8)]), H)
+            cp([], [b, "sum%d" % e], blk(T.P1, e, 1, 8), part(b, 0, 8), "vs")
 
     def differ(b, i, k, other, keys, n=1):
         tt(keys, [b] + ["ne%d" % (k + j) for j in range(n)], blk(T.NE, k, n), blk(b, i, n), other, A.not_equal, n=128 * n)
-        for j in range(k, k + n):
-            o = CU + j if j < 3 else CT + j - 3
-            o = SM[:, o:o + 1]
-            do("vs", [], ["ne%d" % j, "cn%d" % j], 128,
-               lambda q, j=j, o=o: vv.tensor_reduce(o, blk(T.NE, j), AxisListType.X, A.add) if q == "v"
-               else sc.activation(blk(T.NE, j), blk(T.NE, j), AF.Copy, accum_out=o))
 
-    def counts(ds):
-        n = len(ds); p = POS[ds[0]]
-        cn = ["cn%d" % k for k in range(6)]
-        cu, ct = SM[:, CU:CU + n], SM[:, CT:CT + n]
-        pr = lambda c: T.PR[:, 3 * p + c:3 * (p + n):3]
-        tt(cn, ["t2"], SM[:, T2:T2 + n], ct, cu, A.subtract)
-        tt(cn + ["W"], ["pr0"], pr(0), cu, SM[:, WW + p:WW + p + n], A.mult)
-        tt(cn, ["t1"], SM[:, T1:T1 + n], cu, ct, A.add)
-        tt(["WR"], ["t2"], SM[:, T2:T2 + n], SM[:, T2:T2 + n], SM[:, WR + p:WR + p + n], A.mult)
-        tt(["t1", "WR"], ["pr1"], pr(1), SM[:, T1:T1 + n], SM[:, WR + p:WR + p + n], A.mult)
-        tt(["t2", "pr0"], ["pr2"], pr(2), SM[:, T2:T2 + n], pr(0), A.add)
+    def counts(ds, terms):
+        b = new("b"); its, R = [], []
+        for i, d in enumerate(ds):
+            for c, t in enumerate(terms(i)):
+                o = 8 * (3 * i + c)
+                its += group(part(b, o, o + 8), [(blk(T.NE, k), blk(T.GW, 3 * POS[d] + s, 1, 8)) for k, s in t])
+                R += ["ne%d" % k for k, s in t] + ["GW%d" % d]
+        mm(R, [b], its, 64 * len(its))
+        n = 24 * len(ds); o = 8 * (21 + 3 * POS[ds[0]])
+        cp([], [b, "cnt%d" % ds[0]], T.P1[:, o:o + n], part(b, 0, n), "vs", n=n)
 
-    def partial(ds, out, key):
-        p, n = POS[ds[0]], len(ds)
-        tt(["pr0", "pr1", "pr2"] + ["ACC%d_%d" % (d, c) for d in ds for c in range(3)], [key], out,
-           T.ACC[:, 3 * p:3 * (p + n)], T.PR[:, 3 * p:3 * (p + n)], A.add)
+    def ways(k):
+        return lambda i: ([(k + i, 0)], [(k + i, 1), (k + 3 + i, 1)], [(k + i, 2), (k + 3 + i, 1)])
 
-    def team_send(ds, buf, w, sem, key):
-        s, n = w * (lay % 4), 3 * len(ds)
-        partial(ds, buf[:, s:s + n], key)
-        send([key], [sem], [([cores[x] for x in near], off, sem, buf[:, s:s + n], buf[:, s:s + n])])
+    def partial(ds, key):
+        buf, s, w = slot[key]
+        b = new("b"); its, R = [], ["cnt%d" % ds[0], "one", "G8"]
+        for i, d in enumerate(ds):
+            for c in range(3):
+                e = 3 * POS[d] + c
+                its += group(part(b, 3 * i + c, 3 * i + c + 1, rows=8),
+                             [(blk(T.P1, 21 + e, 1, 8), col(EX, 7)),
+                              (T.G8[:], T.ACC[:, e:e + 1]) if "J%d%d" % (d, c) in LONG["s"] else (blk(T.P1, e, 1, 8), col(EX, 7))])
+                R.append("sum%d" % e)
+        mm(R, [b], its, 32 * len(its))
+        cp([], [b, key], buf[0:8, s:s + 3 * len(ds)], part(b, 0, 3 * len(ds), rows=8))
+        return buf[:, s:s + w]
+
+    def team_send(ds, sem, key):
+        x = partial(ds, key)
+        send([key], [sem], [([cores[k] for k in near], off, sem, x, x)])
         arrive(sem, 3 * nof, [sem], [key + "in"], HOP)
 
-    SA, SB, SC, FA, FM, F0, F1, F2, FU, FTT = 32, 44, 56, 76, 82, 88, 94, 100, 106, 112
-
-    def team_sum(buf, w, n, key):
-        tt([key, key + "in"], ["sa"], SM[:, SA:SA + n], buf[:, 0:n], buf[:, w:w + n], A.add)
-        tt([key, key + "in"], ["sb"], SM[:, SB:SB + n], buf[:, 2 * w:2 * w + n], buf[:, 3 * w:3 * w + n], A.add)
-        tt(["sb"], ["sa"], SM[:, SA:SA + n], SM[:, SA:SA + n], SM[:, SB:SB + n], A.add)
-
-    def decide(b, n):
-        cp([], [b, "sc"], SM[:, SC:SC + 3 * n], part(b, 0, 3 * n))
-        s = lambda c: SM[:, SC + c:SC + 3 * n:3]
-        f = lambda x: SM[:, x:x + n]
-        tt(["sc"], ["fm"], f(FM), s(1), s(0), A.min)
-        tt(["sc"], ["fa", "fa0", "fa3"], f(FA), s(1), s(0), A.is_lt)
-        tt(["sc", "fm"], ["f2"], f(F2), s(2), f(FM), A.is_lt)
-        tt(["fa", "f2"], ["f1"], f(F1), f(FA), f(F2), A.is_gt)
-        tt(["fa", "f2"], ["fm"], f(FM), f(FA), f(F2), A.max)
-        ts(["fm"], ["f0"], f(F0), f(FM), -1.0, 1.0, A.mult, A.add)
-
-    def swap(lo, n, ds):
-        p = POS[ds[0]]
-        f = lambda x: SM[:, x + lo:x + lo + n]
-        k = str(lo)
-        tt(["f1", "f2"], ["fa" + k, "fa"], f(FA), f(F1), f(F2), A.subtract)
-        tt(["is%d" % d for d in ds], ["fa" + k], f(FA), f(FA), CF[:, IS + p:IS + p + n], A.mult)
-        tt(["fa" + k, "f2"], ["fu" + k], f(FU), f(FA), f(F2), A.add)
-        tt(["fa" + k, "f1"], ["ft" + k], f(FTT), f(F1), f(FA), A.subtract)
-
-    def diag(flag, i, keys, m="I16"):
-        k = turn["d"] % 18; turn["d"] += 1
-        ts(keys + [m], ["dg%d" % k], blk(T.DG, k), M(m), SM[:, flag + i:flag + i + 1], None, A.mult)
-        return k
-
-    def select(sets):
+    def decide(key, terms, spreads):
+        n = len(terms); buf = slot[key][0]; SM = T.SM
         b = new("b")
-        mm(["dg%d" % k for t in sets for k, _, _ in t] + [key for t in sets for _, _, key in t], [b],
-           [(blk(b, i), blk(T.DG, k), src, j == 0, j == len(t) - 1) for i, t in enumerate(sets) for j, (k, src, _) in enumerate(t)],
-           128 * sum(len(t) for t in sets))
+        its = [x for i, t in enumerate(terms) for x in group(part(b, 3 * i, 3 * i + 3, rows=8), [(m, buf[0:8, o:o + 3]) for m, o in t])]
+        mm([key, key + "in", "PR"] + ["own%d%d" % (d, t) for d in OD for t in (0, 1)], [b], its, 32 * len(its))
+        cp([], [b, "sc"], SM[0:8, 0:3 * n], part(b, 0, 3 * n, rows=8))
+        s = lambda c: SM[0:8, c:3 * n:3] if n > 1 else SM[0:8, c:c + 1]
+        tt(["sc"], ["ma"], SM[0:8, 16:16 + n], s(1), s(2), A.min)
+        tt(["sc"], ["mb"], SM[0:8, 24:24 + n], s(0), s(1), A.min)
+        tt(["sc", "ma"], ["wa"], T.WH[0:8, 0:n], SM[0:8, 16:16 + n], s(0), A.is_lt)
+        tt(["sc", "mb"], ["wb"], T.WH[0:8, 4:4 + n], s(2), SM[0:8, 24:24 + n], A.is_lt)
+        b = new("b")
+        mm(["wa", "wb"] + spreads, [b],
+           [x for k, m in enumerate(spreads) for x in group(part(b, n * k, n * k + n), [(M(m, 8), T.WH[0:8, o:o + n]) for o in (0, 4)])], 128 * len(spreads))
         return b
 
-    def scores(R, terms, w=3):
+    def pair(d):
+        return T.PR[0:8, 8 * d - 8:8 * d]
+
+    def diag(wb, i, t, k):
+        ts(["cd%d%d" % (t, j) for j in range(3)], [wb, "dg%d" % k], blk(T.DG, k, 1, 384), blk(T.CD, tb[t], 1, 384), part(wb, i, i + 1), 1.0,
+           A.subtract, A.is_equal, n=192)
+
+    def pick(sets):
         b = new("b")
-        its = [(part(b, c, c + w), M(m), SM[:, o:o + w], j == 0, j == len(t) - 1) for c, t in terms for j, (m, o) in enumerate(t)]
-        mm(R + [m for c, t in terms for m, o in t], [b], its, 256 * len(its))
+        mm(["dg%d" % k for k, t in sets] + [key for k, t in sets for _, key in t], [b],
+           [x for i, (k, t) in enumerate(sets) for x in group(blk(b, i), [(blk(T.DG, 3 * k + j), src) for j, (src, _) in enumerate(t)])], 384 * len(sets))
         return b
 
     W = lambda d: blk(T.W16, d - 1)
+    WK = lambda d: "W1" if d == 1 else "WA" if d < 4 else "WB"
     Hh = lambda d: blk(T.H16, d - 1)
     UP = {2: 0, 4: 1, 6: 2, 3: 3, 5: 4, 7: 5}
     U = lambda d: blk(T.UW, UP[d])
     TT = lambda d: blk(T.TW, UP[d])
-    SLOT = {3: 2, 5: 3, 7: 4, 2: 5, 4: 6, 6: 7}
-    EV, OD = (2, 4, 6), (3, 5, 7)
+    floor16 = lambda R, Wk, o, i, n: ts(R, Wk, o, i, 0.0625, HB - 0.46875, A.mult, A.add, n=n)
 
-    WA, WH = ["W16", "W16a"], ["W16", "W16a", "H16", "H16a"]
-
-    do("v", [], ["FH3", "FH5"], H, lambda q: vv.memset(T.FH[:, 0:V], 0.0))
-    for d in (1, 2, 4, 6, 3, 5, 7):
-        load_ft(d)
-    cp(["Wall"], ["W16a"], blk(T.W16, 0, 4), blk(T.Wall, 0, 4), n=512)
-    ts(["W16a"], ["H16a"], blk(T.H16, 1, 2), blk(T.W16, 1, 2), 0.0625, HB - 0.46875, A.mult, A.add, n=128)
+    cp(["WallA"], ["WA"], blk(T.W16, 1, 2), blk(T.Wall, 1, 2), n=256)
+    floor16(["WA"], ["HA"], blk(T.H16, 1, 2), blk(T.W16, 1, 2), 128)
     for k, side in enumerate("rj"):
-        b = new("b")
-        mm(["W16a", "H16a"] + [m + side for m in ("A2", "B2", "A3", "B3")], [b],
-           [(blk(b, 0), M(m + side), src, m == "A2", m == "B3") for m, src in (("A2", W(2)), ("B2", Hh(2)), ("A3", W(3)), ("B3", Hh(3)))], 512)
-        ts([], [b, "SL%d" % k], blk(T.SL, k), blk(b, 0), float(2047 * HB), None, A.add, n=128)
-    cp(["Fall"], ["Fw"], T.Fall[:, V:V + 16], T.Fall[:, 0:16], "vs")
-    halves = []
-    for d, k in HALF.items():
-        rs = [a ^ d if a & top(d) else a for a in range(N)]
-        pairs, a = [], 0
-        while a < N:
-            b = a + 1
-            while b < N and rs[b] == rs[b - 1] + 1 and b & top(d) == a & top(d):
-                b += 1
-            h = H if a & top(d) else 0
-            pairs.append((T.FH[16 * a:16 * b, 1040 * k:1040 * (k + 1)], T.Fall[16 * rs[a]:16 * (rs[a] + b - a), h:h + 1040]))
-            a = b
-        halves.append(("y", "fh%d" % d, ["Fall", "Fw", "TP"], ["FH%d" % d], pairs, 260, 128))
-    for t in (1, 2, 4):
-        steps_of_r(t)
-    lists(0, [(d, T.W16, d - 1, "W16a") for d in (1, 2, 4)])
-    cp(["Wall"], ["W16"], blk(T.W16, 4, 3), blk(T.Wall, 4, 3), n=384)
-    lists(0, [(d, T.W16, d - 1, "W16") for d in (6, 3, 5, 7)])
-    ts(WA, ["H16"], blk(T.H16, 3, 4), blk(T.W16, 3, 4), 0.0625, HB - 0.46875, A.mult, A.add, n=256)
-    slists(2, [(x, W(x), Hh(x), WH) for x in OD])
-    slists(5, [(x, W(x), Hh(x), WH) for x in EV])
-    cp(["LMi"], ["LMf"], T.LMf[0:8, 0:7], T.LMi[0:8, 0:7])
+        ms = [m + side for m in ("A2", "B2", "A3", "B3")]
+        stored(blk(T.SL, k), ["SL%d" % k], 128, [(0, 128, [(M(m), src) for m, src in zip(ms, (W(2), Hh(2), W(3), Hh(3)))])], ["WA", "HA"] + ms)
+    cp(["Wall1"], ["W1"], W(1), blk(T.Wall, 0), n=128)
+    cp(["WallB", "Wall1"], ["WB"], blk(T.W16, 3, 4), blk(T.Wall, 3, 4), n=512)
+    floor16(["WB"], ["HB"], blk(T.H16, 3, 4), blk(T.W16, 3, 4), 256)
+    lists([(1, 0, T.W16, 0, "W1"), (2, 0, T.W16, 1, "WA"), (3, 0, T.W16, 2, "WA")])
+    lists([(d, 0, T.W16, d - 1, "WB") for d in (4, 5, 6, 7)])
+    for xs in ((2, 3), (4, 5, 6, 7)):
+        stored(blk(T.SL, xs[0], len(xs)), ["SL%d" % x for x in xs], 128 * len(xs),
+               [(128 * i, 128, [(M("A%d" % x), W(x)), (M("B%d" % (10 + x)), Hh(x))]) for i, x in enumerate(xs)],
+               [WK(xs[0]), "HA" if xs[0] == 2 else "HB"] + [k % x for x in xs for k in ("A%d", "B1%d")])
+    cp(["LMi"], ["LMh"], T.LMh[0:8, 0:7], T.LMi[0:8, 0:7])
     bw = new("b")
-    mm(["ET", "LMf"], [bw], [(part(bw, 0, 7), M("ET", parts=8), T.LMf[0:8, 0:7], True, True)], 256)
-    cp([], [bw, "Wa"], SM[:, WW:WW + 1], part(bw, 0, 1))
-    cp([], [bw, "Wb"], SM[:, WW + 1:WW + 4], part(bw, 1, 7, 2))
-    cp(["Wa", "Wb"], [bw, "W"], SM[:, WW + 4:WW + 7], part(bw, 2, 7, 2))
-    tt(["W"] + ["is%d" % d for d in POS], ["WR"], SM[:, WR:WR + 7], SM[:, WW:WW + 7], CF[:, IS:IS + 7], A.mult)
-    b = extract(compose("v", "TB", 0, ["TB"]), ["Z2_2", "Z1_3"])
-    take(b, 0, 2, blk(T.PW, 0, 2), ["PR"])
-    lists(1, [(1, T.PW, 0, "PR")])
-    lists(2, [(1, T.PW, 1, "PR")])
-    differ(b, 0, 0, W(1), ["W16a"])
-    differ(b, 1, 1, W(1), ["W16a"])
-    differ(b, 1, 3, blk(T.PW, 0), ["PR"])
-    dma("y", "tb2", LM + ["FT7"], ["TC"], [(T.TC[q:128:16, :], T.ldM[:, q:112:7, :]) for q in range(1, 7)], 384, 768)
+    mm(["B0", "LMh"], [bw], [(part(bw, 0, 7), M("B0", 8), T.LMh[0:8, 0:7], True, True)], 64)
+    for d in POS:
+        ts(["g3%d%d" % (top(d), k) for k in range(3)], [bw, "GW%d" % d], blk(T.GW, POS[d], 1, 24), blk(T.G3, tb[top(d)], 1, 24), part(bw, d - 1, d), None, A.mult)
+    row = new("r")
+    compose("Cr", "TC", 0, ["TC"], (row, part(row, 0, V)))
+    b = back(extract(row, ["Zr1", "Zr2"]), 2)
+    take(b, 0, 2, T.PW[:], ["PW"])
+    lists([(1, 1, T.PW, 0, "PW"), (1, 2, T.PW, 1, "PW")])
+    differ(b, 0, 0, W(1), ["W1"])
+    differ(b, 1, 1, W(1), ["W1"])
+    differ(b, 1, 2, blk(T.PW, 0), ["PW"])
+    counts([1], lambda i: ([(0, 1), (1, 1)], [(0, 1), (2, 1)], [(1, 1), (2, 1)]))
     for c in range(3):
         judge(1, c)
-    for c, (x, y) in enumerate(((CU, CU + 1), (CU, CT), (CU + 1, CT))):
-        ts(["cn0", "cn1", "cn3", "WR"], ["pr%d" % c], T.PR[:, c:c + 1], SM[:, x:x + 1], SM[:, y:y + 1], SM[:, WR:WR + 1], A.add, A.mult)
-    team_send([1], T.X1, 4, "a1", "X1")
-    hold.extend(HOLD.get("back", []))
-    take(extract(compose("v", "TB", 1, ["TB"]), ["Z2_2", "Z1_3"]), 0, 2, blk(T.PW, 2, 2), ["PJ"])
+    team_send([1], "a1", "X1")
+    row = new("r")
+    compose("Cj", "TC", 1, ["TC"], (row, part(row, 0, V)))
+    dma("y", "tc2", LB, ["TC"], [(T.TC[3:128:16, :], rows(T.ldA, 3))] + [(T.TC[d - 1:128:16, :], rows(T.ldB, k)) for k, d in enumerate(BD)], 256, 32)
+    c = extract(row, ["Zj1", "Zj2"])
+    b = new("b")
+    mm([c, "I16", "W1", "PW"], [b], group(blk(b, 0), [(M("I16"), W(1))])
+       + [x for i in (0, 1) for x in group(blk(b, 1 + i), [(blk(c, i), M("I16")), (M("I16"), blk(T.PW, i))])], 640)
+    take(b, 0, 3, blk(T.HL, 0, 3), ["HI"], "vs")
+    tt(["HI"], [b, "LO"], blk(T.HL, 3, 3), blk(b, 0, 3), blk(T.HL, 0, 3), A.subtract, n=384)
+    dma("y", "tp", ["HI", "LO"], ["TP"], [(T.TP[2 * c_ + h:128:16, :], blk(T.HL, 3 * h + c_)) for c_ in range(3) for h in (0, 1)], 192, 768)
+    take(b, 0, 3, T.PK[:], ["PK"])
+    floor16(["PK"], ["PH"], T.PH[:], T.PK[:], 192)
+    stored(T.SV[:], ["SV"], 384, [(0, 384, [(M("A1"), T.PK[:]), (M("B11"), T.PH[:])])], ["PK", "PH", "A1", "B11"])
     for d in EV + OD:
-        hold.extend(HOLD.get(d, []))
+        x = d ^ 1
+        compose("T%d" % d, "TP", x, ["TP"], ("TR%d" % d, blk(T.TR, x - 2, 1, V)))
+    for d in EV + OD:
         judge(d, 0)
-    team_sum(T.X1, 4, 3, "X1")
-    decide(scores(["sa"], [(0, [("S0_1", SA)])]), 1)
-    b = select([[(diag(F1, 0, ["f1"], "D1"), blk(T.PW, 0), "PR"), (diag(F2, 0, ["f2"], "D1"), blk(T.PW, 1), "PR"),
-                 (diag(F2, 0, ["f2"], "E1"), blk(T.PW, 2), "PJ"), (diag(F1, 0, ["f1"], "E1"), blk(T.PW, 3), "PJ"),
-                 (diag(F0, 0, ["f0"]), W(1), "W16a")]])
-    take(b, 0, 1, T.W32[:], ["pi32"])
-    dma("y", "pi", ["pi32"], ["TP"], [(T.TP[0:128:16, :], T.W32[:])], 64, 128)
-    for x in halves:
-        dma(*x)
-    dma("y", "ow", ["FH7"], ["OWi"], [(blk(T.OWi, 2, 5), blk(T.mp, 2, 5))], 320, 128)
-    take(b, 0, 1, blk(T.OM, 0), ["pi16"])
-    ts([], [b, "PH"], T.PH[:], blk(b, 0), 0.0625, HB - 0.46875, A.mult, A.add, n=128)
-    slists(8, [(1, blk(T.OM, 0), T.PH[:], ["pi16", "PH"])])
+    wb = decide("X1", [[(pair(1), 4 * k) for k in range(4)]], ["B0"])
+    diag(wb, 0, 1, 0)
+    ts(["ZC"], [wb, "ZT"], T.ZT[:], T.ZC[:], part(wb, 0, 1), 1.0, A.subtract, A.is_equal)
+    b = pick([(0, [(blk(T.SV, j), "SV") for j in range(3)])])
+    take(b, 0, 1, blk(T.SL, 8), ["SL8"])
+    take(pick([(0, [(blk(T.PK, j), "PK") for j in range(3)])]), 0, 1, blk(T.OM, 0), ["pi"])
 
-    row = compose("v", "TC", 8, ["TC"])
-    b = extract(row, ["Z2_1", "Z4_1", "Z6_1"])
+    def by_far(ds):
+        o = lambda d: V * ((d ^ 1) - 2)
+        c = turn([(lambda s, d=d: T.TR[:, o(d) + s:o(d) + V:16], blk(T.ZT, (d ^ 1) - 2, 1, 8), 1) for d in ds], ["ZT"] + ["TR%d" % d for d in ds])
+        b = back(c, len(ds))
+        take(b, 0, len(ds), blk(T.TW, UP[ds[0]], len(ds)), ["T%d" % d for d in ds])
+        return b
+
+    row = new("r")
+    compose("U", "TC", 8, ["TC"], (row, part(row, 0, V)))
+    b = back(extract(row, ["Z2", "Z4", "Z6"]), 3)
     take(b, 0, 3, blk(T.UW, 0, 3), ["UE"])
-    lists(1, [(d, T.UW, UP[d], "UE") for d in EV])
+    lists([(d, 1, T.UW, UP[d], "UE") for d in EV])
     for i, d in enumerate(EV):
-        differ(b, i, i, W(d), WA)
-    take(extract(row, ["Z1_1", "Z3_1", "Z5_1"]), 0, 3, blk(T.UW, 3, 3), ["UO"])
-    def by_b1(d):
-        x, i = d ^ 1, UP[d]
-        hold.extend(HOLD.get("T%d" % d, []))
-        b = extract(compose("s" if x in ONS else "v", "TP", SLOT[x], ["TP"]), ["Z0_%d" % x])
-        take(b, 0, 1, TT(d), ["T%d" % d])
-        if d in EV:
-            lists(2, [(d, T.TW, i, "T%d" % d)])
-            take(b, 0, 1, blk(T.WI, i), ["wi%d" % d])
-            differ(b, 0, 3 + i, U(d), ["UE"])
-            dma("y", "tu%d" % d, ["wi%d" % d, "UE"], ["TE%d" % d], [(T.TC[7 + i:128:16, :], blk(T.WI, i))], 64, 128)
-    for d in EV:
-        by_b1(d)
-    take(extract(compose("v", "TC", 8, ["TC", "TE2", "TE4", "TE6"]), ["Z7_1", "Z8_1", "Z9_1"]), 0, 3, T.EW[:], ["EW"])
+        differ(b, i, 3 + i, W(d), [WK(d)])
+    take(back(extract(row, ["Z1", "Z3", "Z5"]), 3), 0, 3, blk(T.UW, 3, 3), ["UO"])
+    for i, d in enumerate(EV):
+        b = by_far([d])
+        lists([(d, 2, T.TW, i, "T%d" % d)])
+        take(b, 0, 1, blk(T.WI, i), ["wi%d" % d])
+        dma("y", "tu%d" % d, ["wi%d" % d, "UE"], ["TE%d" % d], [(T.TC[7 + i:128:16, :], blk(T.WI, i))], 64, 128)
+    tt(["UE"] + ["T%d" % d for d in EV], ["ne6", "ne7", "ne8"], blk(T.NE, 6, 3), blk(T.TW, 0, 3), blk(T.UW, 0, 3), A.not_equal, n=768)
+    counts(EV, ways(3))
     for c in (1, 2):
         for d in EV:
             judge(d, c)
-    for d in OD:
-        by_b1(d)
-    counts(EV)
-    team_send(EV, T.X2, 12, "a2", "X2")
-    team_sum(T.X2, 12, 9, "X2")
-    decide(scores(["sa"], [(9 * k + 3 * i, [("S%d_%d" % (k, d ^ k), SA + 3 * i)]) for k in (0, 1) for i, d in enumerate(EV)]), 6)
-    swap(3, 3, EV); swap(0, 3, EV)
+    team_send(EV, "a2", "X2")
+    row = new("r")
+    compose("E", "TC", 8, ["TC", "TE2", "TE4", "TE6"], (row, part(row, 0, V)))
+    take(back(extract(row, ["Z7", "Z8", "Z9"]), 3), 0, 3, T.EW[:], ["EW"])
+    by_far(OD)
+    wb = decide("X2", [[(pair(d), 12 * k + 3 * i) for k in range(4)] for i, d in enumerate(EV)], ["B0", "B1"])
 
-    ks = []
     for i, d in enumerate(OD):
-        k = diag(F0, 3 + i, ["f0"]), diag(FU, 3 + i, ["fu3"]), diag(FTT, 3 + i, ["ft3"])
-        b = select([[(k[0], U(d), "UO"), (k[1], W(d), "W16"), (k[2], blk(T.EW, i), "EW")]])
-        take(b, 0, 1, blk(T.OM, 4 + i), ["U%dn" % d])
-        lists(1, [(d, T.OM, 4 + i, "U%dn" % d)])
-        differ(b, 0, i, W(d), WA)
-        k = diag(F0, i, ["f0"]), diag(FU, i, ["fu0"]), diag(FTT, i, ["ft0"])
-        ks.append(k)
-        b = select([[(k[0], TT(d), "T%d" % d), (k[1], blk(T.EW, i), "EW"), (k[2], W(d), "W16")]])
-        take(b, 0, 1, blk(T.OM, 7 + i), ["T%dn" % d])
-        lists(2, [(d, T.OM, 7 + i, "T%dn" % d)])
-        differ(b, 0, 3 + i, blk(T.OM, 4 + i), ["U%dn" % d])
-    b = select([[(ks[i][0], W(d), "W16"), (ks[i][1], U(d), "UE"), (ks[i][2], TT(d), "T%d" % d)] for i, d in enumerate(EV)])
+        diag(wb, 3 + i, top(d), 2 * i); diag(wb, i, top(d), 2 * i + 1)
+    for i, d in enumerate(OD):
+        e = (blk(T.EW, i), "EW"); w = (W(d), WK(d))
+        b = pick([(2 * i, [(U(d), "UO"), w, e]), (2 * i + 1, [(TT(d), "T%d" % d), e, w])])
+        take(b, 0, 2, blk(T.OM, 4 + 2 * i, 2), ["N%d" % d])
+        lists([(d, 1, T.OM, 4 + 2 * i, "N%d" % d), (d, 2, T.OM, 5 + 2 * i, "N%d" % d)])
+        differ(b, 0, 9 + i, W(d), [WK(d)])
+        differ(b, 1, 12 + i, blk(T.OM, 4 + 2 * i), ["N%d" % d])
+    b = pick([(2 * i + 1, [(W(d), WK(d)), (U(d), "UE"), (TT(d), "T%d" % d)]) for i, d in enumerate(EV)])
     take(b, 0, 3, blk(T.OM, 1, 3), ["fin"])
-    om = ["pi16", "fin"] + [k % d for k in ("U%dn", "T%dn") for d in OD]
-    dma("y", "sO", om, ["stO"], [(T.stO[:], T.OM[:])], 320, 128)
-    dma("y", "ownO", om, ["ownO"], [(T.ldO[lay], T.OM[16 * me:16 * me + 16, :])], 40, 16)
-    send(["stO"], ["rO"], [([relay[me, x]], on[q4 * i:q4 * i + q4], "rO", T.stO[x], T.ldO[0]) for i, x in enumerate(far)])
-    send([], [], [([cores[x]], off[2 * i:2 * i + 2], "aO", T.stO[x], T.ldO[lay]) for i, x in enumerate(near)])
-    arrive("aO", 6 + 4 * nof, ["rO"], ["ldO"], 1.5 * HOP)
+    dma("y", "sO", ["pi", "fin"] + ["N%d" % d for d in OD], ["stO"], [(T.stO[:], T.OM[:])], 320, 128)
+    spread("O", ["stO"], lay)
+    arrive("aO", 3 * q4 + 2 * nof, ["sentO"], ["ldO"], 1.7 * HOP)
     dma("y", "oi", ["ldO", "ownO"], ["OI"], [(T.OI[:], T.ldO[:])], 320, 128)
+    counts(OD, ways(9))
     for c in (1, 2):
         for d in OD:
             judge(d, c)
-    counts(OD)
-    s = s3
-    partial(OD, T.X3[:, s:s + 9], "X3")
-    send(["X3"], ["r3"], [([relay[me, x] for x in far], on, "r3", T.X3[:, s:s + 12], T.X3[:, 0:12])])
-    send([], [], [([cores[x] for x in near], off, "a3", T.X3[:, s:s + 12], T.X3[:, s:s + 12])])
-    arrive("a3", 7 * nof, ["r3"], ["X3in"], 1.5 * HOP)
+    x = partial(OD, "X3")
+    send(["X3"], ["r3"], [(ports[me][SIDE["3"]], on, "r3", x, T.X3[:, 0:12]), ([cores[k] for k in near], off, "a3", x, x)])
+    arrive("a3", 7 * nof, ["r3"], ["X3in"], 1.6 * HOP)
 
-    hold.append("X3")
-    cp(["OWi"], ["OW"], blk(T.OW, 2, 5), blk(T.OWi, 2, 5), n=640)
-    cp(["OI"], ["ya"], blk(T.YO, 0, 2), blk(T.OI, 0, 2), n=256)
-    cp(["OI"], ["yb"], blk(T.YO, 3), blk(T.OI, 2), n=128)
-    cp(["OI"], ["yc"], blk(T.YO, 5), blk(T.OI, 3), n=128)
-    X = ["X3", "X3in"]
-    tt(X, ["xs"], T.XS[:, 0:48], T.X3[:, 0:48], T.X3[:, 48:96], A.add)
-    tt(["xs"], ["xt"], T.XS[:, 48:72], T.XS[:, 0:24], T.XS[:, 24:48], A.add)
-    tt(["xt", "im"], ["sa", "sb"], SM[:, SA:SA + 24], T.XS[:, 48:72], T.XS[:, 72:96], A.mult)
-    decide(scores(["sa", "sb"], [(0, [("O0", SA), ("O1", SB)])], 9), 3)
+    for i, d in enumerate((1,) + EV):
+        hold.append("X3")
+        cp(["OI"], ["y%d" % d], blk(T.YO, d - 1), blk(T.OI, i), n=128)
+        dma("y", "y%d" % d, ["y%d" % d], [], [(blk(T.ym, d - 1), blk(T.YO, d - 1))], 64, 128)
+    wb = decide("X3", [[(T.PR[0:8, 56 + 8 * (2 * i + k // 4):64 + 8 * (2 * i + k // 4)], 12 * k + 3 * i) for k in range(N)] for i in range(3)], ["BT"])
     for i, d in enumerate(OD):
-        low = me < me ^ d
-        ks = diag(F1 if low else F2, i, ["f1", "f2"]), diag(F2 if low else F1, i, ["f1", "f2"]), diag(F0, i, ["f0"])
-        b = select([[(ks[0], blk(T.OI, 4 + i), "OI"), (ks[1], blk(T.OI, 7 + i), "OI"), (ks[2], blk(T.OW, d - 1), "OW")]])
-        cp([], [b, "y%d" % d], blk(T.YO, d - 1), blk(b, 0), "s", n=128)
-    dma("y", "y1", ["ya", "yb", "y3"], [], [(blk(T.ym, 0, 4), blk(T.YO, 0, 4))], 256, 128)
-    dma("s", "y2", ["yc", "y5", "y7"], [], [(blk(T.ym, 4, 3), blk(T.YO, 4, 3))], 192, 128)
+        diag(wb, i, 1, i)
+    for i, d in enumerate(OD):
+        two = [(blk(T.OI, 4 + 2 * i), "OI"), (blk(T.OI, 5 + 2 * i), "OI")]
+        b = pick([(i, [(blk(T.OW, i), "OW")] + (two if me < me ^ d else two[::-1]))])
+        take(b, 0, 1, blk(T.YO, d - 1), ["y%d" % d], "vs")
+        dma("ys"[i % 2], "y%d" % d, ["y%d" % d], [], [(blk(T.ym, d - 1), blk(T.YO, d - 1))], 64, 128)
+    for o in ops:
+        for k in GATE.get(o["sem"], ()):
+            o["deps"].add(wr[k]); o["hard"].add(wr[k])
+    for line in [[[i for i, o in enumerate(ops) if o["sem"] == s][0] for s in LOADS]] + [[named[k] for k in LONG[q]] for q in "vs"]:
+        for i, j in zip(line, line[1:]):
+            ops[j]["next"] = i
     emit(best_order())

@@ -6,20 +6,51 @@ POS = {1: 0, 2: 1, 4: 2, 6: 3, 3: 4, 5: 5, 7: 6}
 EV, OD = (2, 4, 6), (3, 5, 7)
 HB = 1536
 NG, NM = 5, 3
-CYCLE, GATHER, WAKE, HOP, LOOK = 0.00095, 1.56, 0.06, 3.5, 0.4
-SHY, IDLE, SMALL, TRIES, SEED, MEMO = 5.0, 6.0, 4.0, 500, 1, {}
-SLACK, EARLY = 0.2, 0.3
-ARR_A, ARR_F, ARR_B = 7.0, 9.0, 10.5
-LONG = {"v": "Cr Cj J11 J20 J40 J60 U J21 J41 J61 E J30 J50 J31 J51 J71".split(),
-        "s": "J10 J12 A10 A12 T2 T4 T6 J22 J42 A22 J62 A42 A62 T3 T5 T7 J70 J32 A70 J52 A32 J72 A52 A72".split()}
-LOADS = "wa tc1 w1 fall ft1 fh1 lm wb ft2 fh2 tp ft4 fh4 ft6 fh6 tc2 ft3 fh3 tu2 tu4 tu6 ft5 fh5 ft7 fh7".split()
-GATE = {"ft6": ["X1"], "ft3": ["SL8"]}
+CYCLE, GATHER, WAKE, HOP, LOOK = 0.00089, 1.56, 0.06, 3.1, 0.3
+SHY, IDLE, SMALL, MEMO = 5.0, 3.0, 0.5, {}
+EARLY, SOON, PASSES, MIX = 0.0, 2.0, 6, 0.5
+TRIES, SEED, MOVE, SLACK = 3000, 1, 2.5, 0.15
+ARRIVE = {"A": 8.1, "F": 9.0, "B": 9.4, "C": 9.6}
+LONG = {"v": dict(Cr=17, Cj=20.5, J11=25, J40=29.5, U=32, J60=37, J21=39, J41=41, J61=43, E=47.5, J30=51, J31=54, J51=56, J50=58, J70=60, J71=62),
+        "s": dict(J10=21.5, J12=23, A10=24.5, A12=25.5, J20=26.5, A20=28.5, T2=29.5, T4=32.5, T6=35.5, J22=38.5, J42=40, A22=41.5, J62=42.5, A42=44,
+                  A62=45, T3=46, T5=49, T7=52, J32=56.5, J52=58, A32=59.5, J72=60.5, A52=62, A72=63)}
+LOADS = "sA sF sB sC ownA ownF ownB ownC ow wa tc1 fall w1 ft1 fh1 lm wb ft2 fh2 ft4 fh4 ft6 fh6 tp tc2 ft3 fh3 ft5 fh5 ft7 fh7 tu2 tu4 tu6 sO sY".split()
+SENDS = dict(a1=27.5, a2=47.0, sO=57.0, a3=65.0)
+ORDER = {"v": """WA HA SL0 Cr SL1 Cr FL3_0 SL3 Cr W1 Cr FL1_0
+                 Cj cr Cj PW LMh Cj FL1_2 w ne0 ne1 Cj ne2 GW1 cj WB HI LO J11 J11 m11 cnt1 HB s11 PK X1
+                 SL7 FL7_0 PH SV GW2 GW4 GW6 J40 J40 m40 sc ma mb wa wb s40 dg0 ZT J60 SL8
+                 U c2 U t2 U FL2_2 U c4 J60 t4 cu m60 FL4_2 UE wi2 wi4 FL6_1 ne3 s60 c6 J21 t6 J21 FL6_2 m21 ne4 ne5 wi6
+                 J41 J41 s21 m41 ne7 ne8 J61 J61 s41 m61 cnt2 co s61 UO X2
+                 E E J30 ce J30 EW m30 GW3 GW5 GW7 s30 sc ma mb wa wb dg0 dg1 dg2 dg3 NU dg4 dg5 FL7_1 c7 ne9 t7 J31 NT J31 FL7_2
+                 m31 ne10 ne11 ne14 J51 J51 s31 m51 cnt3 J71 J71 s51 m71 J72 J72 s71 m72 s72 X3
+                 sc ma mb wa wb dg0 dg1 dg2""".split(),
+         "s": """J10 A10 J12 J20 A12 A20 T2 T4 T6 J22 J42 A22 J62 A42 T3 A62 T5 T7 pi J70 J50 A70 fin A50
+                 J32 J52 A32 A52 y3 y5 y7""".split()}
+ORDER = dict(v="""WA HA SL0 Cr SL1 Cr Cr W1 Cr FL1_0 Cj cr Cj LMh PW Cj FL1_2 Cj WB GW1 ne0 cj ne1 FL3_0 SL3 HI ne2 LO J11 J11 HB m11 FL7_0 PK s11 PH X1
+    J40 J60 J40 SL7 m40 SV sc ma mb wa wb GW4 dg0 ZT SL8 U c2 U t2 U c4 U J60 cu FL2_2 s40 m60 UE t4 ne3 wi2 c6 FL6_1 ne4 FL4_2 J21 t6 GW6 J61 ne8
+    GW2 ne5 J21 wi6 wi4 s60 FL6_2 m21 J41 s21 J41 ne7 J61 m41 cnt2 E m61 E X2 J30 ce pi co J30 EW UO m30 sc GW3 ma mb wa wb GW7 dg0 dg1 GW5 dg2 dg3
+    dg4 NU dg5 ne9 ne10 FL7_1 ne11 J51 c7 J31 t7 J31 NT m31 ne14 J71 FL7_2 J71 J51 J72 m51 J72 m71 m72 A32 s71 s72 X3
+    sc ma mb wa wb dg0 dg1 y3 dg2 y5""".split(),
+             s="""J10 w J12 J20 A10 cnt1 A12 T2 T4 T6 A20 J22 J42 T3 A22 J62 A42 s41 A62 s61 J70 T5 T7 J50 A70 A50 fin s30 J52 s31 cnt3 J32 s51 A52
+    y7""".split(),
+             p="""SL0 SL1 FL1_0 cr A10 PW A12 A10 w FL1_2 A12 SL3 cj FL3_0 HI A10 A10 A12 FL7_0 cnt1 A12 A22 X1 s11 X1 SV SL7 A20 A20 sc A20 dg0 SL8
+    s40 c2 A22 t2 A20 c4 t4 FL2_2 cu UE c6 FL6_1 FL4_2 t6 co A22 A42 s60 FL6_2 A42 A42 A22 s21 A42 cnt2 A62 A62 s41 A62 A62 s61 A70 X2 pi X2 ce A50
+    c7 A70 EW UO A70 sc A70 dg0 A50 NU FL7_1 c7 c7 s30 t7 A50 NT A50 A52 fin FL7_2 s31 A32 A52 cnt3 A32 A52 A52 s51 A32 A32 s71 s72 X3 X3
+    sc dg0 y3 y5 y7""".split())
+LEAD, LAST = {"b": 3, "f": 2}, ((1, 1), (1, 2), (6, 1), (6, 2), (7, 2), (5, 2))
+CHAINS = []
+RATE, END, KEEP = 350.0, 75.0, {"b": 0.7, "m": 0.6, "G": 2.5, "c": 0.7}
+AFTER = {}
+PIECES = {"C": (4, 2), "U": (4, 2), "E": (4, 2), "T": (4, 2), "J": (2, 1)}
+GATE = {"tc2": ["X1"]}
 
 SCRATCH = {
-    "stA": ("dram", [8, 128, 64], "int32"), "ldA": ("dram", [8, 128, 64], "int32"),
+    "stA": ("dram", [8, 128, 32], "int32"), "ldA": ("dram", [8, 128, 32], "int32"),
+    "stC": ("dram", [8, 128, 32], "int32"), "ldC": ("dram", [8, 128, 32], "int32"),
     "stB": ("dram", [8, 128, 64], "int32"), "ldB": ("dram", [8, 128, 64], "int32"),
     "stF": ("dram", [8, 128, 256], "bfloat16"), "ldF": ("dram", [8, 128, 256], "bfloat16"),
-    "stO": ("dram", [8, 128, 160], "float16"), "ldO": ("dram", [8, 128, 160], "float16"),
+    "stO": ("dram", [8, 128, 96], "float16"), "ldO": ("dram", [8, 128, 96], "float16"),
+    "stY": ("dram", [8, 128, 64], "float32"), "ldY": ("dram", [8, 128, 64], "float32"),
     "Fall": ("sbuf", [128, 8 * V + 16], "bfloat16"), "OF": ("sbuf", [128, 7 * 66], "float16"),
     "GB": ("sbuf", [128, NG * 1056], "bfloat16"), "MX": ("sbuf", [128, NM * H], "bfloat16"),
     "FH": ("sbuf", [128, 7 * 1040], "bfloat16"),
@@ -31,13 +62,13 @@ SCRATCH = {
     "PW": ("sbuf", [128, 256], "float16"), "PK": ("sbuf", [128, 384], "float16"), "PH": ("sbuf", [128, 384], "float16"),
     "SV": ("sbuf", [128, 384], "float16"), "HL": ("sbuf", [128, 768], "bfloat16"),
     "UW": ("sbuf", [128, 768], "float16"), "TW": ("sbuf", [128, 768], "float16"),
-    "EW": ("sbuf", [128, 384], "float16"), "OM": ("sbuf", [128, 1280], "float16"), "OI": ("sbuf", [128, 1280], "float16"),
-    "W32": ("sbuf", [128, 256], "float32"), "WI": ("sbuf", [128, 384], "int32"),
+    "EW": ("sbuf", [128, 384], "float16"), "OM": ("sbuf", [128, 768], "float16"), "OI": ("sbuf", [128, 768], "float16"),
+    "OY": ("sbuf", [128, 512], "float32"), "WI": ("sbuf", [128, 384], "int32"),
     "SL": ("sbuf", [128, 9 * 128], "uint16"), "FL": ("sbuf", [128, 21 * 66], "uint16"),
     "CT": ("sbuf", [128, 768], "float16"), "ZH": ("sbuf", [128, 128], "float16"), "ZF": ("sbuf", [128, 16], "float32"),
     "ZX": ("sbuf", [128, 72], "float16"), "ZC": ("sbuf", [128, 48], "bfloat16"), "ZT": ("sbuf", [128, 48], "bfloat16"),
     "NE": ("sbuf", [128, 15 * 128], "float16"), "DG": ("sbuf", [128, 6 * 384], "float16"), "CD": ("sbuf", [128, 3 * 384], "float16"),
-    "MH": ("sbuf", [128, 36 * 128], "float16"), "MB": ("sbuf", [128, 2 * 128 + 16], "bfloat16"),
+    "MH": ("sbuf", [128, 36 * 128], "float16"), "MB": ("sbuf", [128, 4 * 128 + 16], "bfloat16"),
     "G3": ("sbuf", [128, 72], "float16"), "GW": ("sbuf", [128, 7 * 24], "float16"),
     "IR": ("sbuf", [128, 128], "bfloat16"), "GM": ("sbuf", [128, 128], "bfloat16"),
     "CI": ("sbuf", [128, 8], "int32"), "CF": ("sbuf", [128, 96], "float32"),
@@ -45,13 +76,13 @@ SCRATCH = {
     "ACC": ("sbuf", [128, 24], "float32"), "P1": ("sbuf", [128, 8 * 42], "float32"), "SM": ("sbuf", [128, 64], "float32"),
     "PR": ("sbuf", [128, 112], "float32"), "G8": ("sbuf", [128, 8], "float32"), "WH": ("sbuf", [128, 8], "float16"),
     "X1": ("sbuf", [128, 16], "float32"), "X2": ("sbuf", [128, 48], "float32"), "X3": ("sbuf", [128, 96], "float32"),
-    "YO": ("sbuf", [128, 896], "float32"),
+    "YO": ("sbuf", [128, 384], "float32"),
     "PF0": ("psum", [128, H], "float32"), "PF1": ("psum", [128, H], "float32"),
     "PA": ("psum", [128, 512], "float32"), "PB": ("psum", [128, 512], "float32"),
     "PC": ("psum", [128, 512], "float32"), "PD": ("psum", [128, 512], "float32"),
 }
-SEMAPHORES = (["cv", "cs", "cp", "cg", "out", "a1", "a2", "a3", "r3", "lam", "sF2", "ow", "wa", "w1", "wb", "tc1", "tc2", "ts", "tp", "fall", "lm", "oi"]
-              + [k + x for k in ("a", "r", "s", "own") for x in "AFBO"] + ["tu%d" % d for d in EV]
+SEMAPHORES = (["cv", "cs", "cp", "cg", "out", "a1", "a2", "a3", "r3", "ow", "wa", "w1", "wb", "tc1", "tc2", "tp", "fall", "lm", "oi"]
+              + [k + x for k in ("a", "r", "s", "own") for x in "AFBCOY"] + ["tu%d" % d for d in EV]
               + [k % d for k in ("ft%d", "fh%d", "y%d") for d in POS])
 
 
@@ -72,7 +103,9 @@ def plan(T, topo):
     for r in range(N):
         far = teams[1 - layer[r] // 4]
         p = [c for c in topo.cores_of(cores[r]) if c != cores[r] and all(topo.may_write(c, cores[x]) for x in far)]
-        ports[r] = ([c for c in p if topo.die(c) == topo.die(cores[r])][:2], [c for c in p if topo.die(c) != topo.die(cores[r])][:2])
+        same, other = ([c for c in p if (topo.die(c) == topo.die(cores[r])) == k] for k in (True, False))
+        ring = [same[0], other[0], same[1], other[1]]
+        ports[r] = ([ring[(i + layer[r]) % 4] for i in range(4)], same[:2])
     return cores, teams, layer, ports
 
 
@@ -81,26 +114,17 @@ def dst(topo, to, frm):
     return DstId(rid=rid, pnc=pid)
 
 
-SIDE = {"A": 0, "F": 1, "B": 1, "O": 1, "3": 0}
-
-
-def relay_program(g, core, T, topo, cores, layer, a, side, xs):
-    en = topo.engines(core, cores[xs[0]])
-    k = len(en) // 2
-    sent = 0
-    for m in [m for m in "AFBO3" if SIDE[m] == side]:
-        if m == "3":
-            s = 12 * layer[a]
-            items = [(xs, en, T.X3[:, 0:12], T.X3[:, s:s + 12])]
-            g.wait_ge(T.sem.r3, len(en))
-        else:
-            ld = T["ld" + m]
-            items = [([x], en[k * j:k * j + k], ld[j], ld[layer[a] if m == "O" else a]) for j, x in enumerate(xs)]
-            g.wait_ge(T.sem["r" + m], k)
-        g.remote_dma_fused([RemoteDMATransfer(dst_ids=[dst(topo, cores[x], core) for x in to], dma_engine_mask=bits(e), remote_sem=T.sem["a" + m],
-                                              src=src, dsts=[out for x in to]) for to, e, src, out in items], local_sem=T.sem.out)
-        sent += len(en)
-    g.wait_ge(T.sem.out, sent)
+def relay_program(g, core, T, topo, cores, layer, a, x, xs):
+    en = topo.engines(core, cores[x])
+    s = 12 * layer[a]
+    steps = [(m, len(en) // (2 if m == "F" else 4), [x], T["ld" + m][0], T["ld" + m][layer[a] if m in "OY" else a]) for m in "AFBCOY"]
+    if xs:
+        steps.append(("3", len(topo.engines(cores[a], core)), xs, T.X3[:, 0:12], T.X3[:, s:s + 12]))
+    for m, n, to, src, out in steps:
+        g.wait_ge(T.sem["r" + m], n)
+        g.remote_dma_fused([RemoteDMATransfer(dst_ids=[dst(topo, cores[k], core) for k in to], dma_engine_mask=bits(en), remote_sem=T.sem["a" + m],
+                                              src=src, dsts=[out for k in to])], local_sem=T.sem.out)
+    g.wait_ge(T.sem.out, len(steps) * len(en))
 
 
 def rank_program(g, core, T, topo):
@@ -108,10 +132,10 @@ def rank_program(g, core, T, topo):
     me = T.rank_of(core)
     if me is None:
         for a in range(N):
-            for side in (0, 1):
-                if core in ports[a][side]:
-                    far = teams[1 - layer[a] // 4]
-                    relay_program(g, core, T, topo, cores, layer, a, side, far[ports[a][side].index(core)::2])
+            if core in ports[a][0]:
+                far = teams[1 - layer[a] // 4]
+                relay_program(g, core, T, topo, cores, layer, a, far[ports[a][0].index(core)],
+                              far[ports[a][1].index(core)::2] if core in ports[a][1] else [])
         return
     lay = layer[me]
     team = lay // 4
@@ -136,7 +160,7 @@ def rank_program(g, core, T, topo):
         hard = set(deps)
         deps |= set(wr[k] for k in hold)
         del hold[:]
-        ops.append(dict(e=e, deps=deps, hard=hard, busy=busy, late=late, issue=issue, sem=sem, takes=[k for k in W if users.get(k) == []]))
+        ops.append(dict(e=e, tag=(W or [""])[-1], next=[], deps=deps, hard=hard, busy=busy, late=late, issue=issue, sem=sem, takes=[k for k in W if users.get(k) == []]))
         for k in R:
             rd.setdefault(k, []).append(i)
         for k in W:
@@ -204,37 +228,53 @@ def rank_program(g, core, T, topo):
 
     def best_order():
         if "bias" not in MEMO:
-            bias = [SMALL if o["busy"] < 0.6 else 0.0 for o in ops]
-            for i, o in enumerate(ops):
-                bias[i] += 100.0 - i if o["sem"] in ("sA", "sF", "sF2", "sB", "lam") else 50.0 if o["sem"] in ("wa", "tc1") else 0.0
-            big = [i for i, o in enumerate(ops) if o["busy"] > 0.4 and o["e"] in "vsp" and o["deps"]]
-            best, seed = order(bias)[0], SEED
-            now, top_ = best, bias
-            for k in range(TRIES):
-                new_ = list(bias)
-                for _ in range(3):
-                    seed = (seed * 1103515245 + 12345) % 2147483648
-                    new_[big[(seed >> 3) % len(big)]] += ((seed >> 14) % 1000) / 1000.0 * 24.0 - 12.0
-                t = order(new_)[0]
-                if t is not None and t <= now + SLACK * (1.0 - k / TRIES):
-                    now, bias = t, new_
-                    if t < best:
-                        best, top_ = t, new_
-            MEMO["bias"] = top_; MEMO["time"] = best
-        _, seq, extra, where = order(MEMO["bias"])
+            MEMO["bias"] = order
+            MEMO["plan"] = plan_ = refine(dict(LONG["v"], **LONG["s"], **SENDS))
+            MEMO["all"] = (ops, users, pools, body[0])
+        _, seq, extra, where = order(None, MEMO["plan"][1])
+        if "force" in MEMO:
+            seq, extra, slots_ = MEMO["force"]
+            where = {k: pools[k[0]][x] for k, x in slots_.items()}
+        MEMO["seq"] = seq
         phys.update(where)
         for i, more in extra.items():
             ops[i]["hard"] = ops[i]["hard"] | more
         return seq
 
-    def order(bias):
+    def refine(starts):
+        t = order(starts)[0]
+        best, due = (t, MEMO["due"]), MEMO["latest"]
+        for k in range(PASSES):
+            t = order(None, due)[0]
+            if t is None:
+                break
+            best = min(best, (t, due))
+            due = [MIX * a + (1.0 - MIX) * b for a, b in zip(MEMO["latest"], due)]
+        (now, due), seed = best, SEED
+        sets = [[i] for i in range(body[0], len(ops)) if "name" not in ops[i]] + 3 * [list(range(named[k], last[k] + 1)) for k in last]
+        for k in range(TRIES):
+            new_ = list(due)
+            for _ in range(2):
+                seed = (seed * 1103515245 + 12345) % 2147483648
+                for i in sets[(seed >> 3) % len(sets)]:
+                    new_[i] += ((seed >> 14) % 1000) / 1000.0 * 2 * MOVE - MOVE
+            t = order(None, new_)[0]
+            if t is not None and t <= now + SLACK * (1.0 - k / TRIES):
+                now, due = t, new_
+                best = min(best, (t, due))
+        return best
+
+    def order(bias, given=None):
         n = len(ops); extra, where, since = {}, {}, {}
         after = [[] for _ in ops]
         for i, o in enumerate(ops):
             for d in o["deps"]:
                 after[d].append(i)
-        span = lambda o: o["busy"] + (2.0 + o["late"][0] / 250.0 if isinstance(o["late"], tuple) else o["late"]) + WAKE
-        behind = {o["next"]: [i] for i, o in enumerate(ops) if "next" in o}
+        span = lambda o: o["busy"] + (2.0 + o["late"][0] / RATE if isinstance(o["late"], tuple) else o["late"]) + WAKE
+        behind = {}
+        for i, o in enumerate(ops):
+            if "next" in o:
+                behind.setdefault(o["next"], []).append(i)
         left = [len(o["deps"]) + ("next" in o) for o in ops]
         line = [i for i in range(n) if not left[i]]
         for i in line:
@@ -242,12 +282,99 @@ def rank_program(g, core, T, topo):
                 left[j] -= 1
                 if not left[j]:
                     line.append(j)
-        rank = [0.0] * n
-        for i in line[::-1]:
-            rank[i] = max([span(ops[i]) + rank[j] for j in after[i]] + [ops[i]["busy"] + rank[j] for j in behind.get(i, [])] + [span(ops[i])])
+        due = given or [bias[o["name"]] + o.get("into", 0.0) if "name" in o else bias.get(o["sem"], END) for o in ops]
+        for again in (() if given else (0, 1)):
+            for i in line[::-1]:
+                due[i] = min([due[i]] + [due[j] - span(ops[i]) for j in after[i]] + [due[j] - ops[i]["busy"] for j in behind.get(i, [])])
+            for k, v in users.items():
+                for i in v[1:]:
+                    due[i] = min(due[i], due[v[0]] + KEEP.get(k[0], END))
+        rank = [-x for x in due]
         left = [len(o["deps"]) + ("next" in o) for o in ops]
         ready = [i for i in range(n) if not left[i]]
-        end, free, pipe, seq = {}, {}, [0.0], []
+        end, free, pipe, seq, start = {}, {}, [0.0], [], {}
+        slots = {p: [None] * len(v) for p, v in pools.items()}
+        open_ = {k: len(v) for k, v in users.items()}
+        uses = {}
+        for k, v in users.items():
+            for i in v:
+                uses.setdefault(i, []).append(k)
+        while ready:
+            cand = []
+            for i in ready:
+                o = ops[i]; got = []
+                if i not in since:
+                    since[i] = max([end[d] + WAKE for d in o["deps"]] + [due[i] - SOON if o["e"] == "p" and o["takes"] and i >= body[0] else 0.0])
+                t = since[i]
+                for k in o["takes"]:
+                    fr = [(max(end[u] for u in users[h]) if h else 0.0, x) for x, h in enumerate(slots[k[0]]) if h is None or not open_[h]]
+                    if not fr:
+                        break
+                    got.append((k, min(fr)[1])); t = max(t, min(fr)[0] + WAKE)
+                else:
+                    for q in (o["e"] if o["e"] == "vs" else [o["e"]]):
+                        cand.append((max(t, free.get(q, 0.0)) if q != "net" else t, q, i, got))
+            if not cand:
+                return None, None, None, None
+            t0, q0 = min((c[0], c[1]) for c in cand)
+            worth = lambda c: rank[c[2]] + (SMALL if ops[c[2]]["busy"] < 0.6 else 0.0) - IDLE * (c[0] - t0) - (SHY if c[1] == "v" and ops[c[2]]["e"] == "vs" else 0.0)
+            t, q, i, got = max([c for c in cand if c[1] == q0 and c[0] <= t0 + LOOK], key=worth)
+            o = ops[i]; ready.remove(i)
+            for k, x in got:
+                h = slots[k[0]][x]
+                if h:
+                    extra[i] = extra.get(i, set()) | set(users[h])
+                slots[k[0]][x] = k; where[k] = pools[k[0]][x]
+            free[q] = t + o["busy"]; start[i] = t
+            if isinstance(o["late"], tuple):
+                pipe[0] = max(pipe[0], t + 1.8) + o["late"][0] / RATE + o["late"][1] * 0.002
+                end[i] = pipe[0]
+            else:
+                end[i] = free[q] + o["late"]
+            for k in uses.get(i, []):
+                open_[k] -= 1
+            seq.append((i, q))
+            for j in after[i] + behind.get(i, []):
+                left[j] -= 1
+                if not left[j]:
+                    ready.append(j)
+        MEMO["end"] = stop = max(end.values())
+        latest, then, waits = [0.0] * n, {}, [list(a) for a in after]
+        for i, more in extra.items():
+            for j in more:
+                waits[j].append(i)
+        for i, q in seq[::-1]:
+            took = end[i] - start[i] + WAKE
+            latest[i] = min([stop - took] + [latest[j] - took for j in waits[i]] + [latest[j] for j in behind.get(i, [])]
+                            + ([then[q] - ops[i]["busy"]] if q in then and q != "net" else []))
+            then[q] = latest[i]
+        MEMO["latest"], MEMO["due"] = latest, due
+        MEMO["log"] = [(q, round(end[i], 1), ops[i].get("name") or ops[i]["sem"] or ops[i]["W"]) for i, q in seq]
+        return max(end.values()) + EARLY * sum(end[i] for i in range(n) if ops[i]["e"] == "net"), seq, extra, where
+
+    def arrange():
+        n = len(ops); extra, since = {}, {}
+        after, behind = [[] for _ in ops], [[] for _ in ops]
+        for i, o in enumerate(ops):
+            for d in o["deps"]:
+                after[d].append(i)
+            for d in o["next"]:
+                behind[d].append(i)
+        span = lambda o: o["busy"] + (2.0 + o["late"][0] / RATE if isinstance(o["late"], tuple) else o["late"]) + WAKE
+        left = [len(o["deps"]) + len(o["next"]) for o in ops]
+        line = [i for i in range(n) if not left[i]]
+        for i in line:
+            for j in after[i] + behind[i]:
+                left[j] -= 1
+                if not left[j]:
+                    line.append(j)
+        assert len(line) == n, [ops[i]["tag"] for i in range(n) if left[i]][:20]
+        rank = [0.0] * n
+        for i in line[::-1]:
+            rank[i] = max([span(ops[i]) + rank[j] for j in after[i]] + [ops[i]["busy"] + rank[j] for j in behind[i]] + [span(ops[i])])
+        left = [len(o["deps"]) + len(o["next"]) for o in ops]
+        ready = [i for i in range(n) if not left[i]]
+        end, free, pipe, seq = {}, {}, 0.0, []
         slots = {p: [None] * len(v) for p, v in pools.items()}
         open_ = {k: len(v) for k, v in users.items()}
         uses = {}
@@ -267,34 +394,36 @@ def rank_program(g, core, T, topo):
                         break
                     got.append((k, min(fr)[1])); t = max(t, min(fr)[0] + WAKE)
                 else:
-                    for q in (o["e"] if o["e"] == "vs" else [o["e"]]):
-                        cand.append((max(t, free.get(q, 0.0)) if q != "net" else t, q, i, got))
-            if not cand:
-                return None, None, None, None
+                    cand.append((max(t, free.get(o["e"], 0.0)) if o["e"] != "net" else t, o["e"], i, got))
+            assert cand, ([ops[i]["tag"] for i in ready], [[ops[u]["tag"] for u in users[h]] for h in slots["b"]], seq[-1])
             t0, q0 = min((c[0], c[1]) for c in cand)
-            t, q, i, got = max([c for c in cand if c[1] == q0 and c[0] <= t0 + LOOK],
-                               key=lambda c: rank[c[2]] + bias[c[2]] - IDLE * (c[0] - t0) - (SHY if c[1] == "v" and ops[c[2]]["e"] == "vs" else 0.0))
+            t, q, i, got = max([c for c in cand if c[1] == q0 and c[0] <= t0 + LOOK], key=lambda c: rank[c[2]] - IDLE * (c[0] - t0))
             o = ops[i]; ready.remove(i)
             for k, x in got:
                 h = slots[k[0]][x]
                 if h:
                     extra[i] = extra.get(i, set()) | set(users[h])
-                slots[k[0]][x] = k; where[k] = pools[k[0]][x]
+                slots[k[0]][x] = k; phys[k] = pools[k[0]][x]
             free[q] = t + o["busy"]
             if isinstance(o["late"], tuple):
-                pipe[0] = max(pipe[0], t + 1.8) + o["late"][0] / 250.0 + o["late"][1] * 0.0025
-                end[i] = pipe[0]
+                pipe = end[i] = max(pipe, t + 1.8) + o["late"][0] / RATE + o["late"][1] * 0.002
             else:
                 end[i] = free[q] + o["late"]
             for k in uses.get(i, []):
                 open_[k] -= 1
             seq.append((i, q))
-            for j in after[i] + behind.get(i, []):
+            for j in after[i] + behind[i]:
                 left[j] -= 1
                 if not left[j]:
                     ready.append(j)
-        MEMO["end"] = max(end.values())
-        return max(end.values()) + EARLY * sum(end[i] for i in range(n) if ops[i]["e"] == "net"), seq, extra, where
+        MEMO.update(end=max(end.values()), all=(ops, users, pools, body[0]), seq=seq,
+                    log=[(q, round(end[i], 1), ops[i]["sem"] or ops[i]["tag"]) for i, q in seq])
+        if "force" in MEMO:
+            seq, extra, slots_ = MEMO["force"]
+            phys.update({k: pools[k[0]][x] for k, x in slots_.items()})
+        for i, more in extra.items():
+            ops[i]["hard"] = ops[i]["hard"] | more
+        return seq
 
     def emit(seq):
         count, seen, tok = {}, {}, {}
@@ -322,14 +451,19 @@ def rank_program(g, core, T, topo):
         for s, k in count.items():
             g.wait_ge(T.sem[s], k)
 
-    AD, BD = (2, 3, 1, 4), (5, 6, 7)
-    rows = lambda t, k: t[:, 32 * k:32 * k + 32, :]
-    dma("y", "sA", [], ["sA"], [(rows(T.stA, k), blk(T.mp, d - 1)) for k, d in enumerate(AD)], 256, 512)
-    dma("y", "sF", [], ["sF"], [(T.stF[:], T.ft[:])], 512, 16)
-    dma("y", "sB", [], ["sB"], [(rows(T.stB, k), blk(T.mp, d - 1)) for k, d in enumerate(BD)], 192, 384)
-    hold.append("sB")
-    dma("y", "lam", [], ["lam"], [(T.stB[k, 96, 0:7], T.lam[k // 4]) for k in range(N)]
-        + [(T.stB[:, 96, 7:64], T.mp[0:8, 0:57]), (T.stB[:, 97:128, :], T.mp[0:32, 0:496])], 64, 48)
+    MAPS = {"A": (2, 3), "B": (1, 4, 5, 6), "C": (7, 0)}
+
+    def rows(kind, d):
+        m = [m for m in MAPS if d in MAPS[m]][0]
+        k, n = MAPS[m].index(d), 128 // len(MAPS[m])
+        return T[kind + m][:, n * k:n * k + n, :]
+
+    half = lambda t, h: t[:, 64 * h:64 * h + 64, :]
+    dma("y", "sA", [], ["sA"], [(rows("st", d), blk(T.mp, d - 1)) for d in MAPS["A"]], 128, 256)
+    dma("y", "sF", [], ["sF"], [(half(T.stF, h), T.ft[:, H * h:H * h + H]) for h in (0, 1)], 512, 256)
+    dma("y", "sB", [], ["sB"], [(rows("st", d), blk(T.mp, d - 1)) for d in MAPS["B"]], 256, 512)
+    dma("y", "sC", [], ["sC"], [(rows("st", 7), blk(T.mp, 6))] + [(T.stC[k, 64, 0:7], T.lam[k // 4]) for k in range(N)]
+        + [(T.stC[:, 64, 7:32], T.mp[0:8, 0:25]), (T.stC[:, 65:128, :], T.mp[0:32, 0:504])], 128, 200)
     do("g", [], ["pi0", "gq"], 130, lambda q: g.iota(T.CI[:, 0:1], [[0, 1]], 0, 1))
     do("g", [], ["IR"], 400, lambda q: g.iota(T.IR[:], [[1, 128]], 0, 0, allow_small_or_imprecise_dtypes=True))
     do("g", [], ["GM"], 400, lambda q: g.iota(T.GM[:], [[16, 8], [0, 16]], 0, 0, allow_small_or_imprecise_dtypes=True))
@@ -339,17 +473,18 @@ def rank_program(g, core, T, topo):
 
     def spread(m, keys, slot, busy=0.3):
         st, ld = T["st" + m], T["ld" + m]
-        of = (lambda x: x) if m == "O" else (lambda x: layer[x])
-        send(keys, ["sent" + m], [([ports[me][SIDE[m]][i % 2]], on[q4 * i:q4 * i + q4], "r" + m, st[of(x)], ld[i // 2]) for i, x in enumerate(far)]
-             + [([cores[x]], off[q4 * i:q4 * i + q4], "a" + m, st[of(x)], ld[slot]) for i, x in enumerate(near)], busy)
-        dma("s" if m != "O" else "y", "own" + m, keys, ["own" + m], [(ld[slot], st[of(me)])], 48, 16)
+        of = (lambda x: x) if m in "OY" else (lambda x: layer[x])
+        en, k = (on + off, 2 * q4) if m == "F" else (on, q4)
+        out = [([ports[me][0][i]], en[k * i:k * i + k], "r" + m, st[of(x)], ld[0]) for i, x in enumerate(far)]
+        inside = [([cores[x]], off[q4 * i:q4 * i + q4], "a" + m, st[of(x)], ld[slot]) for i, x in enumerate(near)]
+        for items in ((out, inside) if m == "F" else (out + inside,)):
+            send(keys, ["sent" + m], items, busy)
+        dma("y", "own" + m, keys, ["own" + m], [(ld[slot], st[of(me)])], 48, 16)
 
-    spread("A", ["sA"], me, 3.0)
-    spread("F", ["sF"], me)
-    spread("B", ["sB", "lam"], me)
-    for m, late in (("A", ARR_A), ("F", ARR_F), ("B", ARR_B)):
-        arrive("a" + m, 3 * q4 + 2 * nof, ["sent" + m], ["ld" + m], late)
-    dma("s", "ow", ["sB"], ["OWi"], [(blk(T.OWi, i), blk(T.mp, d - 1)) for i, d in enumerate(OD)], 192, 384)
+    for m in "AFBC":
+        spread(m, ["s" + m], me, 3.0 if m == "A" else 0.3)
+        arrive("a" + m, 3 * q4 + 4 * nof, ["sent" + m], ["ld" + m], ARRIVE[m])
+    dma("y", "ow", ["sC"], ["OWi"], [(blk(T.OWi, i), blk(T.mp, d - 1)) for i, d in enumerate(OD)], 192, 384)
     fill(["TC"], T.TC[:], V)
     fill(["TP"], T.TP[:], H)
 
@@ -417,7 +552,8 @@ def rank_program(g, core, T, topo):
         mat("P%d" % d, "MH", IR, col(PX, d), isr(d))
     mat("I", "MB", IR, col(PX, 0), 1.0)
     mat("nI", "MB", IR, col(PX, 0), -1.0)
-    G2, nG2 = T.MB[:, 256:264], T.MB[:, 264:272]
+    mat("bD", "MB", IR, col(PX, 0), isr(1)); mat("bP", "MB", IR, col(PX, 1), isr(1))
+    G2, nG2 = T.MB[:, 512:520], T.MB[:, 520:528]
     ts(cols, ["G2"], G2, G8, col(GX, 0), 2.0, A.is_equal, A.mult)
     ts(cols, ["nG2"], nG2, G8, col(GX, 0), -2.0, A.is_equal, A.mult)
     ts(cols, ["G8"], T.G8[:], G8, col(GX, 0), None, A.is_equal)
@@ -434,8 +570,8 @@ def rank_program(g, core, T, topo):
     cp([], [b, "PR"], T.PR[0:8, 0:56], part(b, 0, 56, rows=8))
     for i, d in enumerate(OD):
         for t in (0, 1):
-            o = 56 + 8 * (2 * i + t)
-            ts(["PR", "IR"], ["own%d%d" % (d, t)], T.PR[0:8, o:o + 8], IR[0:8, 0:8], float(t), T.PR[0:8, 8 * d - 8 + me:8 * d - 7 + me], A.is_equal, A.mult)
+            o = 56 + 2 * (2 * i + t)
+            ts(["PR", "IR"], ["own%d%d" % (d, t)], T.PR[0:8, o:o + 2], IR[0:8, 0:2], float(t), T.PR[0:8, 8 * d - 8 + me:8 * d - 7 + me], A.is_equal, A.mult)
     mat("B0", "MH", GM, CF[0:8, EX:EX + 1], 1.0, parts=8)
     mat("B1", "MH", GM, CF[0:8, EX + 1:EX + 2], 1.0, parts=8)
     mat("BT", "MH", GM, 64.0, CF[0:8, 0:1], A.is_ge, A.is_equal, parts=8)
@@ -452,14 +588,14 @@ def rank_program(g, core, T, topo):
         fill([k], buf[:, s:s + w], w)
     cp(["OWi"], ["OW"], T.OW[:], T.OWi[:], n=384)
 
-    LA, LF, LB = ["ldA", "ownA"], ["ldF", "ownF"], ["ldB", "ownB"]
-    dma("y", "wa", LA, ["WallA"], [(blk(T.Wall, d - 1), rows(T.ldA, k)) for k, d in enumerate(AD[:2])], 128, 256)
-    dma("y", "tc1", LA, ["TC"], [(T.TC[d - 1:128:16, :], rows(T.ldA, k)) for k, d in enumerate(AD[:2])], 128, 16)
-    dma("y", "w1", LA, ["Wall1"], [(blk(T.Wall, AD[k] - 1), rows(T.ldA, k)) for k in (2, 3)], 128, 256)
-    dma("y", "fall", LF, ["Fall"], [(T.Fall[:, 0:V], T.ldF[:])], 512, 128)
-    dma("y", "lm", LB, ["LMi"], [(T.LMi[0:8, 0:7], T.ldB[:, 96, 0:7])], 0, 16)
-    dma("y", "wb", LB, ["WallB"], [(blk(T.Wall, d - 1), rows(T.ldB, k)) for k, d in enumerate(BD)], 192, 384)
-    cp(["Fall"], ["Fw"], T.Fall[:, V:V + 16], T.Fall[:, 0:16], "vs")
+    LA, LF, LB, LC = ([k + m for k in ("ld", "own")] for m in "AFBC")
+    dma("y", "wa", LA, ["WallA"], [(blk(T.Wall, d - 1), rows("ld", d)) for d in (2, 3)], 128, 256)
+    dma("y", "tc1", LA, ["TC"], [(T.TC[d - 1:128:16, :], rows("ld", d)) for d in (2, 3)], 128, 16)
+    dma("y", "fall", LF, ["Fall"], [(T.Fall[:, H * h:H * h + H], half(T.ldF, h)) for h in (0, 1)], 512, 256)
+    dma("y", "w1", LB, ["Wall1"], [(blk(T.Wall, 0), rows("ld", 1))], 64, 128)
+    dma("y", "lm", LC, ["LMi"], [(T.LMi[0:8, 0:7], T.ldC[:, 64, 0:7])], 0, 16)
+    dma("y", "wb", LB + LC, ["WallB"], [(blk(T.Wall, d - 1), rows("ld", d)) for d in (4, 5, 6, 7)], 256, 512)
+    cp(["Fall"], ["Fw"], T.Fall[:, V:V + 16], T.Fall[:, 0:16], "s")
 
     def runs(src, same):
         out, a = [], 0
@@ -478,8 +614,16 @@ def rank_program(g, core, T, topo):
             cp(["TP"], ["FT%d" % d], T.Fall[:, at:at + V], T.TP[:], "s", n=V)
         ts(["IR"], ["of%d" % d], blk(T.OF, POS[d], 1, 66), IR[:, 0:66], 0.0, float(at), A.mult, A.add)
         same = lambda a, b: a & t == b & t
-        dma("y", "ft%d" % d, LF, ["FT%d" % d],
-            [(T.Fall[16 * a:16 * b, at:at + V], T.ldF[a ^ d:(a ^ d) + b - a]) for a, b in runs(lambda a: a ^ d, same) if not a & t], 256, 64)
+        if d == 1:
+            dma("y", "ft1", LF, ["FT1"], [(T.Fall[16 * a:16 * a + 16, at + H * h:at + H * h + H], T.ldF[a + 1, 64 * h:64 * h + 64, :])
+                                          for a in range(0, N, 2) for h in (0, 1)], 256, 128)
+            dma("y", "fh1", LF, ["FH1a"], [(T.FH[:, 0:H], T.ldF[0:N:2])], 256, 128)
+            b = new("b")
+            mm(["Fall", "bD", "bP"], [b], group(part(b, 0, 16), [(M("bD"), T.Fall[:, H:H + 16]), (M("bP"), T.Fall[:, 0:16])]), 128)
+            cp(["FH1a"], [b, "FH1"], T.FH[:, H:H + 16], part(b, 0, 16), "s")
+            return
+        dma("y", "ft%d" % d, ["Fall"], ["FT%d" % d],
+            [(T.Fall[16 * a:16 * b, at:at + V], T.Fall[16 * (a ^ d):16 * ((a ^ d) + b - a), 0:V]) for a, b in runs(lambda a: a ^ d, same) if not a & t], 256, 64)
         r = lambda a: a ^ d if a & t else a
         pairs = []
         for a, b in runs(r, same):
@@ -491,6 +635,7 @@ def rank_program(g, core, T, topo):
         load_features(d)
 
     place = {}
+    body = [len(ops)]
 
     def lists(items):
         b = new("b"); its = []; R = []
@@ -512,25 +657,34 @@ def rank_program(g, core, T, topo):
         mm(R, [b], [x for o, w, t in terms for x in group(part(b, o, o + w), t)], sum(w * len(t) for o, w, t in terms))
         ts([], [b] + key, out, part(b, 0, n), float(2047 * HB), None, A.add, n=n)
 
-    named = {}
+    named, last = {}, {}
 
     def long_step(name):
-        named[name] = len(ops) - 1
-        ops[-1]["e"] = "v" if name in LONG["v"] else "s"
+        ops[-1]["tag"] = name
 
-    def compose(name, win, slot, keys, row):
-        cp(keys + ["SL%d" % slot], [row[0]], row[1], T[win][:, 0:V].indirect(blk(T.SL, slot)), "vs", n=V * GATHER)
-        long_step(name)
+    def gather(name, R, key, out, win, offs, o, n, less=None):
+        k = (ORDER["v"] + ORDER["s"]).count(name)
+        cuts = [n // k // 2 * 2 * j for j in range(k)] + [n]
+        for a, b in zip(cuts, cuts[1:]):
+            first = wr.get(key) if a else None
+            src = win.indirect(offs[:, o + a:o + b])
+            if less is None:
+                cp(R, [key], out(16 * a, 16 * b), src, "vs", n=16 * (b - a) * GATHER + 60)
+            else:
+                tt(R, [key], out(16 * a, 16 * b), src, less(16 * a, 16 * b), A.subtract, n=16 * (b - a) * GATHER + 60)
+            ops[-1]["hard"].discard(first)
+            long_step(name)
 
-    def turn(items, R, slow=False):
+    def compose(name, win, slot, keys, row, out=None):
+        gather(name, keys + ["SL%d" % slot], row, out or (lambda a, b: part(row, a, b)), T[win][:, 0:V], T.SL, 128 * slot, 128)
+
+    def turn(name, items):
         b = new("b"); o = 0
-        k = 4 if slow else 16
-        for row, z, n in items:
-            for s0 in range(0, 16, k):
-                mm(R, [b], [(part(b, o + s, o + 128 * n, 16), row(s), z, True, True) for s in range(s0, s0 + k)], 1024, o + s0 > 0)
+        for row, z, n, R in items:
+            mm(R, [b], [(part(b, o + s, o + 128 * n, 16), row(s), z, True, True) for s in range(16)], 1024, o > 0)
             o += 128 * n
         c = new("c")
-        cp([], [b, c], part(c, 0, o), part(b, 0, o), n=o)
+        cp([], [b, c, name], part(c, 0, o), part(b, 0, o), n=o)
         return c
 
     def back(c, n):
@@ -538,9 +692,9 @@ def rank_program(g, core, T, topo):
         mm([c, "I16"], [b], [(blk(b, i), blk(c, i), M("I16"), True, True) for i in range(n)], 128 * n)
         return b
 
-    def extract(row, zs):
+    def extract(name, row, zs):
         buf, o = mats[zs[0]]
-        return turn([(lambda s: part(row, s, V, 16), T[buf][:, o:o + 8 * len(zs)], len(zs))], [row] + list(zs), row[0] == "R")
+        return turn(name, [(lambda s: part(row, s, V, 16), T[buf][:, o:o + 8 * len(zs)], len(zs), [row] + list(zs))])
 
     def take(b, i, n, out, keys, e="v"):
         cp([], [b] + keys, out, blk(b, i, n), e, n=128 * n)
@@ -548,29 +702,28 @@ def rank_program(g, core, T, topo):
     def judge(d, c):
         G = new("G")
         o, e = place[d, c] * 66, 3 * POS[d] + c
-        src = T.Fall[:, 0:2 * V + 16 + V * POS[d]].indirect(T.FL[:, o:o + 65])
+        win = T.Fall[:, 0:2 * V + 16 + V * POS[d]]
         R = ["Fall", "Fw", "FL%d_%d" % (d, c)] + ["FT%d" % x for x in POS if POS[x] <= POS[d]]
         fh = 1040 * POS[d]
-        if "J%d%d" % (d, c) in LONG["s"]:
-            cp(R, [G], part(G, 0, 1040), src, "s", n=1040 * GATHER)
-            long_step("J%d%d" % (d, c))
+        if "J%d%d" % (d, c) in ORDER["s"]:
+            gather("J%d%d" % (d, c), R, G, lambda a, b: part(G, a, b), win, T.FL, o, 65)
             pf = new("f")
-            for k in (0, 512):
-                mm([G, "I", "nI", "FH%d" % d], [pf], group(part(pf, k, k + 512), [(M("I"), T.FH[:, fh + k:fh + k + 512]), (M("nI"), T.FH[:, fh + k + 1:fh + k + 513]),
-                                                                                   (M("nI"), part(G, k, k + 512)), (M("I"), part(G, k + 1, k + 513))]), 2 * H, k > 0)
+            two = [group(part(pf, k, k + 512), [(M("I"), T.FH[:, fh + k:fh + k + 512]), (M("nI"), T.FH[:, fh + k + 1:fh + k + 513]),
+                                                (M("nI"), part(G, k, k + 512)), (M("I"), part(G, k + 1, k + 513))]) for k in (0, 512)]
+            for j, (k, n) in enumerate(((0, 0), (1, 0), (0, 2), (1, 2))):
+                mm(["I", "nI", G if n else "FH%d" % d], [pf], two[k][n:n + 2], H, j > 0)
             acc = T.ACC[:, e:e + 1]; src = part(pf, 0, H)
             do("vs", [], [pf, G, "sum%d" % e], H + 150,
                lambda q: vv.tensor_reduce(acc, ap(src), AxisListType.X, A.add, apply_absolute_value=True) if q == "v"
                else sc.activation(ap(part(G, 0, H)), ap(src), AF.Abs, accum_out=acc))
             long_step("A%d%d" % (d, c))
         else:
-            tt(R + ["FH%d" % d], [G], part(G, 0, 1040), src, T.FH[:, fh:fh + 1040], A.subtract, n=1040 * GATHER)
-            long_step("J%d%d" % (d, c))
+            gather("J%d%d" % (d, c), R + ["FH%d" % d], G, lambda a, b: part(G, a, b), win, T.FL, o, 65, lambda a, b: T.FH[:, fh + a:fh + b])
             m = new("m")
-            do("v", [G], [m], H // 2, lambda q: vv.tensor_tensor_scan(ap(part(m, 0, H)), ap(part(G, 0, H)), ap(part(G, 1, H + 1)), 64.0, A.min, A.max))
+            do("v", [G], [m, "m%d%d" % (d, c)], H // 2, lambda q: vv.tensor_tensor_scan(ap(part(m, 0, H)), ap(part(G, 0, H)), ap(part(G, 1, H + 1)), 64.0, A.min, A.max))
             b = new("b")
             mm([G, m, "G2", "nG2"], [b], group(part(b, 0, 8), [(blk(G, k), nG2) for k in range(8)] + [(blk(m, k), G2) for k in range(8)]), H)
-            cp([], [b, "sum%d" % e], blk(T.P1, e, 1, 8), part(b, 0, 8), "vs")
+            cp([], [b, "sum%d" % e, "s%d%d" % (d, c)], blk(T.P1, e, 1, 8), part(b, 0, 8), "vs")
 
     def differ(b, i, k, other, keys, n=1):
         tt(keys, [b] + ["ne%d" % (k + j) for j in range(n)], blk(T.NE, k, n), blk(b, i, n), other, A.not_equal, n=128 * n)
@@ -591,15 +744,17 @@ def rank_program(g, core, T, topo):
 
     def partial(ds, key):
         buf, s, w = slot[key]
-        b = new("b"); its, R = [], ["cnt%d" % ds[0], "one", "G8"]
-        for i, d in enumerate(ds):
-            for c in range(3):
-                e = 3 * POS[d] + c
-                its += group(part(b, 3 * i + c, 3 * i + c + 1, rows=8),
+        b = new("b")
+        line = sorted([(d, c) for d in ds for c in range(3)], key=lambda x: x in LAST)
+        for k, some in enumerate((line[:-2], line[-2:])):
+            its, R = [], ["cnt%d" % ds[0], "one", "G8"]
+            for d, c in some:
+                e, o = 3 * POS[d] + c, 3 * ds.index(d) + c
+                its += group(part(b, o, o + 1, rows=8),
                              [(blk(T.P1, 21 + e, 1, 8), col(EX, 7)),
-                              (T.G8[:], T.ACC[:, e:e + 1]) if "J%d%d" % (d, c) in LONG["s"] else (blk(T.P1, e, 1, 8), col(EX, 7))])
+                              (T.G8[:], T.ACC[:, e:e + 1]) if "J%d%d" % (d, c) in ORDER["s"] else (blk(T.P1, e, 1, 8), col(EX, 7))])
                 R.append("sum%d" % e)
-        mm(R, [b], its, 32 * len(its))
+            mm(R, [b], its, 32 * len(its), k > 0)
         cp([], [b, key], buf[0:8, s:s + 3 * len(ds)], part(b, 0, 3 * len(ds), rows=8))
         return buf[:, s:s + w]
 
@@ -608,20 +763,20 @@ def rank_program(g, core, T, topo):
         send([key], [sem], [([cores[k] for k in near], off, sem, x, x)])
         arrive(sem, 3 * nof, [sem], [key + "in"], HOP)
 
-    def decide(key, terms, spreads):
+    def decide(key, terms, spreads, r=8):
         n = len(terms); buf = slot[key][0]; SM = T.SM
         b = new("b")
-        its = [x for i, t in enumerate(terms) for x in group(part(b, 3 * i, 3 * i + 3, rows=8), [(m, buf[0:8, o:o + 3]) for m, o in t])]
-        mm([key, key + "in", "PR"] + ["own%d%d" % (d, t) for d in OD for t in (0, 1)], [b], its, 32 * len(its))
-        cp([], [b, "sc"], SM[0:8, 0:3 * n], part(b, 0, 3 * n, rows=8))
-        s = lambda c: SM[0:8, c:3 * n:3] if n > 1 else SM[0:8, c:c + 1]
-        tt(["sc"], ["ma"], SM[0:8, 16:16 + n], s(1), s(2), A.min)
-        tt(["sc"], ["mb"], SM[0:8, 24:24 + n], s(0), s(1), A.min)
-        tt(["sc", "ma"], ["wa"], T.WH[0:8, 0:n], SM[0:8, 16:16 + n], s(0), A.is_lt)
-        tt(["sc", "mb"], ["wb"], T.WH[0:8, 4:4 + n], s(2), SM[0:8, 24:24 + n], A.is_lt)
+        its = [x for i, t in enumerate(terms) for x in group(part(b, 3 * i, 3 * i + 3, rows=r), [(m, buf[0:8, o:o + 3]) for m, o in t])]
+        mm([key, key + "in", "PR"] + ["own%d%d" % (d, t) for d in OD for t in (0, 1)], [b], its, 4 * max(r, 3) * len(its))
+        cp([], [b, "sc"], SM[0:r, 0:3 * n], part(b, 0, 3 * n, rows=r))
+        s = lambda c: SM[0:r, c:3 * n:3] if n > 1 else SM[0:r, c:c + 1]
+        tt(["sc"], ["ma"], SM[0:r, 16:16 + n], s(1), s(2), A.min)
+        tt(["sc"], ["mb"], SM[0:r, 24:24 + n], s(0), s(1), A.min)
+        tt(["sc", "ma"], ["wa"], T.WH[0:r, 0:n], SM[0:r, 16:16 + n], s(0), A.is_lt)
+        tt(["sc", "mb"], ["wb"], T.WH[0:r, 4:4 + n], s(2), SM[0:r, 24:24 + n], A.is_lt)
         b = new("b")
         mm(["wa", "wb"] + spreads, [b],
-           [x for k, m in enumerate(spreads) for x in group(part(b, n * k, n * k + n), [(M(m, 8), T.WH[0:8, o:o + n]) for o in (0, 4)])], 128 * len(spreads))
+           [x for k, m in enumerate(spreads) for x in group(part(b, n * k, n * k + n), [(M(m, r), T.WH[0:r, o:o + n]) for o in (0, 4)])], 128 * len(spreads))
         return b
 
     def pair(d):
@@ -651,9 +806,10 @@ def rank_program(g, core, T, topo):
         ms = [m + side for m in ("A2", "B2", "A3", "B3")]
         stored(blk(T.SL, k), ["SL%d" % k], 128, [(0, 128, [(M(m), src) for m, src in zip(ms, (W(2), Hh(2), W(3), Hh(3)))])], ["WA", "HA"] + ms)
     cp(["Wall1"], ["W1"], W(1), blk(T.Wall, 0), n=128)
-    cp(["WallB", "Wall1"], ["WB"], blk(T.W16, 3, 4), blk(T.Wall, 3, 4), n=512)
+    cp(["WallB"], ["WB"], blk(T.W16, 3, 4), blk(T.Wall, 3, 4), n=512)
     floor16(["WB"], ["HB"], blk(T.H16, 3, 4), blk(T.W16, 3, 4), 256)
-    lists([(1, 0, T.W16, 0, "W1"), (2, 0, T.W16, 1, "WA"), (3, 0, T.W16, 2, "WA")])
+    lists([(1, 0, T.W16, 0, "W1")])
+    lists([(2, 0, T.W16, 1, "WA"), (3, 0, T.W16, 2, "WA")])
     lists([(d, 0, T.W16, d - 1, "WB") for d in (4, 5, 6, 7)])
     for xs in ((2, 3), (4, 5, 6, 7)):
         stored(blk(T.SL, xs[0], len(xs)), ["SL%d" % x for x in xs], 128 * len(xs),
@@ -662,11 +818,12 @@ def rank_program(g, core, T, topo):
     cp(["LMi"], ["LMh"], T.LMh[0:8, 0:7], T.LMi[0:8, 0:7])
     bw = new("b")
     mm(["B0", "LMh"], [bw], [(part(bw, 0, 7), M("B0", 8), T.LMh[0:8, 0:7], True, True)], 64)
+    cp([], [bw, "w"], T.SM[:, 32:39], part(bw, 0, 7), "vs")
     for d in POS:
-        ts(["g3%d%d" % (top(d), k) for k in range(3)], [bw, "GW%d" % d], blk(T.GW, POS[d], 1, 24), blk(T.G3, tb[top(d)], 1, 24), part(bw, d - 1, d), None, A.mult)
+        ts(["w"] + ["g3%d%d" % (top(d), k) for k in range(3)], ["GW%d" % d], blk(T.GW, POS[d], 1, 24), blk(T.G3, tb[top(d)], 1, 24), T.SM[:, 31 + d:32 + d], None, A.mult)
     row = new("r")
-    compose("Cr", "TC", 0, ["TC"], (row, part(row, 0, V)))
-    b = back(extract(row, ["Zr1", "Zr2"]), 2)
+    compose("Cr", "TC", 0, ["TC"], row)
+    b = back(extract("cr", row, ["Zr1", "Zr2"]), 2)
     take(b, 0, 2, T.PW[:], ["PW"])
     lists([(1, 1, T.PW, 0, "PW"), (1, 2, T.PW, 1, "PW")])
     differ(b, 0, 0, W(1), ["W1"])
@@ -675,11 +832,11 @@ def rank_program(g, core, T, topo):
     counts([1], lambda i: ([(0, 1), (1, 1)], [(0, 1), (2, 1)], [(1, 1), (2, 1)]))
     for c in range(3):
         judge(1, c)
-    team_send([1], "a1", "X1")
+    team_send((1,), "a1", "X1")
     row = new("r")
-    compose("Cj", "TC", 1, ["TC"], (row, part(row, 0, V)))
-    dma("y", "tc2", LB, ["TC"], [(T.TC[3:128:16, :], rows(T.ldA, 3))] + [(T.TC[d - 1:128:16, :], rows(T.ldB, k)) for k, d in enumerate(BD)], 256, 32)
-    c = extract(row, ["Zj1", "Zj2"])
+    compose("Cj", "TC", 1, ["TC"], row)
+    dma("y", "tc2", LB + LC, ["TC"], [(T.TC[d - 1:128:16, :], rows("ld", d)) for d in (4, 5, 6, 7)], 256, 32)
+    c = extract("cj", row, ["Zj1", "Zj2"])
     b = new("b")
     mm([c, "I16", "W1", "PW"], [b], group(blk(b, 0), [(M("I16"), W(1))])
        + [x for i in (0, 1) for x in group(blk(b, 1 + i), [(blk(c, i), M("I16")), (M("I16"), blk(T.PW, i))])], 640)
@@ -691,7 +848,7 @@ def rank_program(g, core, T, topo):
     stored(T.SV[:], ["SV"], 384, [(0, 384, [(M("A1"), T.PK[:]), (M("B11"), T.PH[:])])], ["PK", "PH", "A1", "B11"])
     for d in EV + OD:
         x = d ^ 1
-        compose("T%d" % d, "TP", x, ["TP"], ("TR%d" % d, blk(T.TR, x - 2, 1, V)))
+        compose("T%d" % d, "TP", x, ["TP"], "TR%d" % d, lambda a, b, o=V * (x - 2): T.TR[:, o + a:o + b])
     for d in EV + OD:
         judge(d, 0)
     wb = decide("X1", [[(pair(1), 4 * k) for k in range(4)]], ["B0"])
@@ -699,79 +856,104 @@ def rank_program(g, core, T, topo):
     ts(["ZC"], [wb, "ZT"], T.ZT[:], T.ZC[:], part(wb, 0, 1), 1.0, A.subtract, A.is_equal)
     b = pick([(0, [(blk(T.SV, j), "SV") for j in range(3)])])
     take(b, 0, 1, blk(T.SL, 8), ["SL8"])
-    take(pick([(0, [(blk(T.PK, j), "PK") for j in range(3)])]), 0, 1, blk(T.OM, 0), ["pi"])
+    take(pick([(0, [(blk(T.PK, j), "PK") for j in range(3)])]), 0, 1, blk(T.OY, 0), ["pi"], "vs")
 
     def by_far(ds):
         o = lambda d: V * ((d ^ 1) - 2)
-        c = turn([(lambda s, d=d: T.TR[:, o(d) + s:o(d) + V:16], blk(T.ZT, (d ^ 1) - 2, 1, 8), 1) for d in ds], ["ZT"] + ["TR%d" % d for d in ds])
+        c = turn("c%d" % ds[-1], [(lambda s, d=d: T.TR[:, o(d) + s:o(d) + V:16], blk(T.ZT, (d ^ 1) - 2, 1, 8), 1, ["ZT", "TR%d" % d]) for d in ds])
         b = back(c, len(ds))
-        take(b, 0, len(ds), blk(T.TW, UP[ds[0]], len(ds)), ["T%d" % d for d in ds])
+        take(b, 0, len(ds), blk(T.TW, UP[ds[0]], len(ds)), ["T%d" % d for d in ds] + ["t%d" % ds[-1]])
         return b
 
     row = new("r")
-    compose("U", "TC", 8, ["TC"], (row, part(row, 0, V)))
-    b = back(extract(row, ["Z2", "Z4", "Z6"]), 3)
+    compose("U", "TC", 8, ["TC"], row)
+    b = bu = back(extract("cu", row, ["Z2", "Z4", "Z6"]), 3)
     take(b, 0, 3, blk(T.UW, 0, 3), ["UE"])
     lists([(d, 1, T.UW, UP[d], "UE") for d in EV])
     for i, d in enumerate(EV):
         differ(b, i, 3 + i, W(d), [WK(d)])
-    take(back(extract(row, ["Z1", "Z3", "Z5"]), 3), 0, 3, blk(T.UW, 3, 3), ["UO"])
+    take(back(extract("co", row, ["Z1", "Z3", "Z5"]), 3), 0, 3, blk(T.UW, 3, 3), ["UO"])
     for i, d in enumerate(EV):
         b = by_far([d])
         lists([(d, 2, T.TW, i, "T%d" % d)])
-        take(b, 0, 1, blk(T.WI, i), ["wi%d" % d])
+        cp(["T%d" % d], ["wi%d" % d], blk(T.WI, i), TT(d), n=128)
         dma("y", "tu%d" % d, ["wi%d" % d, "UE"], ["TE%d" % d], [(T.TC[7 + i:128:16, :], blk(T.WI, i))], 64, 128)
-    tt(["UE"] + ["T%d" % d for d in EV], ["ne6", "ne7", "ne8"], blk(T.NE, 6, 3), blk(T.TW, 0, 3), blk(T.UW, 0, 3), A.not_equal, n=768)
+    differ(bu, 0, 6, blk(T.TW, 0, 2), ["T2", "T4"], 2)
+    differ(b, 0, 8, U(6), ["UE"])
     counts(EV, ways(3))
     for c in (1, 2):
         for d in EV:
             judge(d, c)
     team_send(EV, "a2", "X2")
     row = new("r")
-    compose("E", "TC", 8, ["TC", "TE2", "TE4", "TE6"], (row, part(row, 0, V)))
-    take(back(extract(row, ["Z7", "Z8", "Z9"]), 3), 0, 3, T.EW[:], ["EW"])
+    compose("E", "TC", 8, ["TC", "TE2", "TE4", "TE6"], row)
+    take(back(extract("ce", row, ["Z7", "Z8", "Z9"]), 3), 0, 3, T.EW[:], ["EW"])
     by_far(OD)
     wb = decide("X2", [[(pair(d), 12 * k + 3 * i) for k in range(4)] for i, d in enumerate(EV)], ["B0", "B1"])
 
     for i, d in enumerate(OD):
-        diag(wb, 3 + i, top(d), 2 * i); diag(wb, i, top(d), 2 * i + 1)
+        diag(wb, 3 + i, top(d), i)
     for i, d in enumerate(OD):
-        e = (blk(T.EW, i), "EW"); w = (W(d), WK(d))
-        b = pick([(2 * i, [(U(d), "UO"), w, e]), (2 * i + 1, [(TT(d), "T%d" % d), e, w])])
-        take(b, 0, 2, blk(T.OM, 4 + 2 * i, 2), ["N%d" % d])
-        lists([(d, 1, T.OM, 4 + 2 * i, "N%d" % d), (d, 2, T.OM, 5 + 2 * i, "N%d" % d)])
-        differ(b, 0, 9 + i, W(d), [WK(d)])
-        differ(b, 1, 12 + i, blk(T.OM, 4 + 2 * i), ["N%d" % d])
-    b = pick([(2 * i + 1, [(W(d), WK(d)), (U(d), "UE"), (TT(d), "T%d" % d)]) for i, d in enumerate(EV)])
-    take(b, 0, 3, blk(T.OM, 1, 3), ["fin"])
-    dma("y", "sO", ["pi", "fin"] + ["N%d" % d for d in OD], ["stO"], [(T.stO[:], T.OM[:])], 320, 128)
-    spread("O", ["stO"], lay)
-    arrive("aO", 3 * q4 + 2 * nof, ["sentO"], ["ldO"], 1.7 * HOP)
-    dma("y", "oi", ["ldO", "ownO"], ["OI"], [(T.OI[:], T.ldO[:])], 320, 128)
+        diag(wb, i, top(d), 3 + i)
+    e = lambda i: (blk(T.EW, i), "EW")
+    w = lambda d: (W(d), WK(d))
+    b = pick([(i, [(U(d), "UO"), w(d), e(i)]) for i, d in enumerate(OD)])
+    take(b, 0, 3, blk(T.OM, 0, 3), ["NU"])
+    lists([(d, 1, T.OM, i, "NU") for i, d in enumerate(OD)])
+    for i, d in enumerate(OD):
+        differ(b, i, 9 + i, W(d), [WK(d)])
+    b = pick([(3 + i, [(TT(d), "T%d" % d), e(i), w(d)]) for i, d in enumerate(OD)])
+    take(b, 0, 3, blk(T.OM, 3, 3), ["NT"])
+    lists([(d, 2, T.OM, 3 + i, "NT") for i, d in enumerate(OD)])
+    differ(b, 0, 12, blk(T.OM, 0, 3), ["NU"], 3)
+    b = pick([(3 + i, [w(d), (U(d), "UE"), (TT(d), "T%d" % d)]) for i, d in enumerate(EV)])
+    take(b, 0, 3, blk(T.OY, 1, 3), ["fin"], "vs")
+    dma("y", "sO", ["NU", "NT"], ["sO"], [(T.stO[:], T.OM[:])], 192, 128)
+    dma("y", "sY", ["pi", "fin"], ["sY"], [(T.stY[:, 32 * k:32 * k + 32, :], blk(T.OY, k)) for k in range(4)], 256, 512)
+    for m in "OY":
+        spread(m, ["s" + m], lay)
+        arrive("a" + m, 3 * q4 + 4 * nof, ["sent" + m], ["ld" + m], 1.75 * HOP)
+    dma("y", "oi", ["ldO", "ownO"], ["OI"], [(T.OI[:], T.ldO[:])], 192, 128)
+    dma("y", "y1", ["ldY", "ownY"], [], [(blk(T.ym, d - 1), T.ldY[:, 32 * k:32 * k + 32, :]) for k, d in enumerate((1,) + EV)], 256, 512)
     counts(OD, ways(9))
     for c in (1, 2):
         for d in OD:
             judge(d, c)
     x = partial(OD, "X3")
-    send(["X3"], ["r3"], [(ports[me][SIDE["3"]], on, "r3", x, T.X3[:, 0:12]), ([cores[k] for k in near], off, "a3", x, x)])
-    arrive("a3", 7 * nof, ["r3"], ["X3in"], 1.6 * HOP)
+    send(["X3"], ["r3"], [(ports[me][1], on + off, "r3", x, T.X3[:, 0:12])])
+    send(["X3"], ["r3"], [([cores[k] for k in near], off, "a3", x, x)])
+    arrive("a3", 7 * nof, ["r3"], ["X3in"], 1.45 * HOP)
 
-    for i, d in enumerate((1,) + EV):
-        hold.append("X3")
-        cp(["OI"], ["y%d" % d], blk(T.YO, d - 1), blk(T.OI, i), n=128)
-        dma("y", "y%d" % d, ["y%d" % d], [], [(blk(T.ym, d - 1), blk(T.YO, d - 1))], 64, 128)
-    wb = decide("X3", [[(T.PR[0:8, 56 + 8 * (2 * i + k // 4):64 + 8 * (2 * i + k // 4)], 12 * k + 3 * i) for k in range(N)] for i in range(3)], ["BT"])
+    wb = decide("X3", [[(T.PR[0:8, 56 + 2 * (2 * i + k // 4):58 + 2 * (2 * i + k // 4)], 12 * k + 3 * i) for k in range(N)] for i in range(3)], ["BT"], 2)
     for i, d in enumerate(OD):
         diag(wb, i, 1, i)
     for i, d in enumerate(OD):
-        two = [(blk(T.OI, 4 + 2 * i), "OI"), (blk(T.OI, 5 + 2 * i), "OI")]
+        two = [(blk(T.OI, i), "OI"), (blk(T.OI, 3 + i), "OI")]
         b = pick([(i, [(blk(T.OW, i), "OW")] + (two if me < me ^ d else two[::-1]))])
-        take(b, 0, 1, blk(T.YO, d - 1), ["y%d" % d], "vs")
-        dma("ys"[i % 2], "y%d" % d, ["y%d" % d], [], [(blk(T.ym, d - 1), blk(T.YO, d - 1))], 64, 128)
+        take(b, 0, 1, blk(T.YO, i), ["y%d" % d], "vs")
+        dma("ys"[i % 2], "y%d" % d, ["y%d" % d], [], [(blk(T.ym, d - 1), blk(T.YO, i))], 64, 128)
     for o in ops:
         for k in GATE.get(o["sem"], ()):
             o["deps"].add(wr[k]); o["hard"].add(wr[k])
-    for line in [[[i for i, o in enumerate(ops) if o["sem"] == s][0] for s in LOADS]] + [[named[k] for k in LONG[q]] for q in "vs"]:
+    lines = {"y": [[i for i, o in enumerate(ops) if o["sem"] == s][0] for s in LOADS]}
+    tagged = {}
+    for i in range(body[0], len(ops)):
+        o = ops[i]
+        if o["e"] == "p":
+            o["tag"] = [ops[j]["tag"] for j in users[o["tag"]] if ops[j]["e"] != "p"][0]
+        if o["e"] in ("v", "s", "vs", "p") and not o["sem"]:
+            tagged.setdefault((o["e"] == "p", o["tag"]), []).append(i)
+    for q in ORDER:
+        lines[q] = [tagged[q == "p", k].pop(0) for k in ORDER[q]]
+        for i in lines[q]:
+            ops[i]["e"] = q
+    for line in lines.values():
         for i, j in zip(line, line[1:]):
-            ops[j]["next"] = i
-    emit(best_order())
+            ops[j]["next"].append(i)
+    if "p" not in ORDER:
+      for k, v in users.items():
+        if k[0] in "bf" and v[0] >= body[0]:
+            i = [i for i in v if ops[i]["e"] != "p"][0]
+            line = lines[ops[i]["e"]]
+            ops[v[0]]["next"].append(line[max(0, line.index(i) - LEAD[k[0]])])
+    emit(arrange())

from concourse.bass import DstId, RemoteDMATransfer
from concourse.mybir import AluOpType as A, AxisListType, ActivationFunctionType as AF

V, H, N = 2048, 1024, 8
POS = {1: 0, 2: 1, 4: 2, 6: 3, 3: 4, 5: 5, 7: 6}
EV, OD = (2, 4, 6), (3, 5, 7)
HB = 1536
NG, NM = 5, 3
CYCLE, GATHER, WAKE, HOP, LOOK = 0.00089, 1.56, 0.06, 3.1, 0.3
SHY, IDLE, SMALL, MEMO = 5.0, 3.0, 0.5, {}
EARLY, SOON, PASSES, MIX = 0.0, 2.0, 6, 0.5
TRIES, SEED, MOVE, SLACK = 3000, 1, 2.5, 0.15
ARRIVE = {"A": 8.1, "F": 9.0, "B": 9.4, "C": 9.6}
LONG = {"v": dict(Cr=17, Cj=20.5, J11=25, J40=29.5, U=32, J60=37, J21=39, J41=41, J61=43, E=47.5, J30=51, J31=54, J51=56, J50=58, J70=60, J71=62),
        "s": dict(J10=21.5, J12=23, A10=24.5, A12=25.5, J20=26.5, A20=28.5, T2=29.5, T4=32.5, T6=35.5, J22=38.5, J42=40, A22=41.5, J62=42.5, A42=44,
                  A62=45, T3=46, T5=49, T7=52, J32=56.5, J52=58, A32=59.5, J72=60.5, A52=62, A72=63)}
LOADS = "sA sF sB sC ownA ownF ownB ownC ow wa tc1 fall w1 ft1 fh1 lm wb ft2 fh2 ft4 fh4 ft6 fh6 tp tc2 ft3 fh3 ft5 fh5 ft7 fh7 tu2 tu4 tu6 sO sY".split()
SENDS = dict(a1=27.5, a2=47.0, sO=57.0, a3=65.0)
ORDER = {"v": """WA HA SL0 Cr SL1 Cr FL3_0 SL3 Cr W1 Cr FL1_0
                 Cj cr Cj PW LMh Cj FL1_2 w ne0 ne1 Cj ne2 GW1 cj WB HI LO J11 J11 m11 cnt1 HB s11 PK X1
                 SL7 FL7_0 PH SV GW2 GW4 GW6 J40 J40 m40 sc ma mb wa wb s40 dg0 ZT J60 SL8
                 U c2 U t2 U FL2_2 U c4 J60 t4 cu m60 FL4_2 UE wi2 wi4 FL6_1 ne3 s60 c6 J21 t6 J21 FL6_2 m21 ne4 ne5 wi6
                 J41 J41 s21 m41 ne7 ne8 J61 J61 s41 m61 cnt2 co s61 UO X2
                 E E J30 ce J30 EW m30 GW3 GW5 GW7 s30 sc ma mb wa wb dg0 dg1 dg2 dg3 NU dg4 dg5 FL7_1 c7 ne9 t7 J31 NT J31 FL7_2
                 m31 ne10 ne11 ne14 J51 J51 s31 m51 cnt3 J71 J71 s51 m71 J72 J72 s71 m72 s72 X3
                 sc ma mb wa wb dg0 dg1 dg2""".split(),
         "s": """J10 A10 J12 J20 A12 A20 T2 T4 T6 J22 J42 A22 J62 A42 T3 A62 T5 T7 pi J70 J50 A70 fin A50
                 J32 J52 A32 A52 y3 y5 y7""".split()}
ORDER = dict(v="""WA HA SL0 Cr SL1 Cr Cr W1 Cr FL1_0 Cj cr Cj LMh PW Cj FL1_2 Cj WB GW1 ne0 cj ne1 FL3_0 SL3 HI ne2 LO J11 J11 HB m11 FL7_0 PK s11 PH X1
    J40 J60 J40 SL7 m40 SV sc ma mb wa wb GW4 dg0 ZT SL8 U c2 U t2 U c4 U J60 cu FL2_2 s40 m60 UE t4 ne3 wi2 c6 FL6_1 ne4 FL4_2 J21 t6 GW6 J61 ne8
    GW2 ne5 J21 wi6 wi4 s60 FL6_2 m21 J41 s21 J41 ne7 J61 m41 cnt2 E m61 E X2 J30 ce pi co J30 EW UO m30 sc GW3 ma mb wa wb GW7 dg0 dg1 GW5 dg2 dg3
    dg4 NU dg5 ne9 ne10 FL7_1 ne11 J51 c7 J31 t7 J31 NT m31 ne14 J71 FL7_2 J71 J51 J72 m51 J72 m71 m72 A32 s71 s72 X3
    sc ma mb wa wb dg0 dg1 y3 dg2 y5""".split(),
             s="""J10 w J12 J20 A10 cnt1 A12 T2 T4 T6 A20 J22 J42 T3 A22 J62 A42 s41 A62 s61 J70 T5 T7 J50 A70 A50 fin s30 J52 s31 cnt3 J32 s51 A52
    y7""".split(),
             p="""SL0 SL1 FL1_0 cr A10 PW A12 A10 w FL1_2 A12 SL3 cj FL3_0 HI A10 A10 A12 FL7_0 cnt1 A12 A22 X1 s11 X1 SV SL7 A20 A20 sc A20 dg0 SL8
    s40 c2 A22 t2 A20 c4 t4 FL2_2 cu UE c6 FL6_1 FL4_2 t6 co A22 A42 s60 FL6_2 A42 A42 A22 s21 A42 cnt2 A62 A62 s41 A62 A62 s61 A70 X2 pi X2 ce A50
    c7 A70 EW UO A70 sc A70 dg0 A50 NU FL7_1 c7 c7 s30 t7 A50 NT A50 A52 fin FL7_2 s31 A32 A52 cnt3 A32 A52 A52 s51 A32 A32 s71 s72 X3 X3
    sc dg0 y3 y5 y7""".split())
LEAD, LAST = {"b": 3, "f": 2}, ((1, 1), (1, 2), (6, 1), (6, 2), (7, 2), (5, 2))
CHAINS = []
RATE, END, KEEP = 350.0, 75.0, {"b": 0.7, "m": 0.6, "G": 2.5, "c": 0.7}
AFTER = {}
PIECES = {"C": (4, 2), "U": (4, 2), "E": (4, 2), "T": (4, 2), "J": (2, 1)}
GATE = {"tc2": ["X1"]}

SCRATCH = {
    "stA": ("dram", [8, 128, 32], "int32"), "ldA": ("dram", [8, 128, 32], "int32"),
    "stC": ("dram", [8, 128, 32], "int32"), "ldC": ("dram", [8, 128, 32], "int32"),
    "stB": ("dram", [8, 128, 64], "int32"), "ldB": ("dram", [8, 128, 64], "int32"),
    "stF": ("dram", [8, 128, 256], "bfloat16"), "ldF": ("dram", [8, 128, 256], "bfloat16"),
    "stO": ("dram", [8, 128, 96], "float16"), "ldO": ("dram", [8, 128, 96], "float16"),
    "stY": ("dram", [8, 128, 64], "float32"), "ldY": ("dram", [8, 128, 64], "float32"),
    "Fall": ("sbuf", [128, 8 * V + 16], "bfloat16"), "OF": ("sbuf", [128, 7 * 66], "float16"),
    "GB": ("sbuf", [128, NG * 1056], "bfloat16"), "MX": ("sbuf", [128, NM * H], "bfloat16"),
    "FH": ("sbuf", [128, 7 * 1040], "bfloat16"),
    "Wall": ("sbuf", [128, 896], "int32"), "W16": ("sbuf", [128, 896], "float16"), "H16": ("sbuf", [128, 896], "float16"),
    "OWi": ("sbuf", [128, 384], "int32"), "OW": ("sbuf", [128, 384], "float16"),
    "TC": ("sbuf", [128, V], "int32"), "TS": ("sbuf", [128, V], "float32"), "TP": ("sbuf", [128, V], "bfloat16"),
    "TR": ("sbuf", [128, 6 * V], "bfloat16"),
    "RA": ("sbuf", [128, V], "float16"), "RB": ("sbuf", [128, V], "float16"), "RS": ("sbuf", [128, V], "float32"),
    "PW": ("sbuf", [128, 256], "float16"), "PK": ("sbuf", [128, 384], "float16"), "PH": ("sbuf", [128, 384], "float16"),
    "SV": ("sbuf", [128, 384], "float16"), "HL": ("sbuf", [128, 768], "bfloat16"),
    "UW": ("sbuf", [128, 768], "float16"), "TW": ("sbuf", [128, 768], "float16"),
    "EW": ("sbuf", [128, 384], "float16"), "OM": ("sbuf", [128, 768], "float16"), "OI": ("sbuf", [128, 768], "float16"),
    "OY": ("sbuf", [128, 512], "float32"), "WI": ("sbuf", [128, 384], "int32"),
    "SL": ("sbuf", [128, 9 * 128], "uint16"), "FL": ("sbuf", [128, 21 * 66], "uint16"),
    "CT": ("sbuf", [128, 768], "float16"), "ZH": ("sbuf", [128, 128], "float16"), "ZF": ("sbuf", [128, 16], "float32"),
    "ZX": ("sbuf", [128, 72], "float16"), "ZC": ("sbuf", [128, 48], "bfloat16"), "ZT": ("sbuf", [128, 48], "bfloat16"),
    "NE": ("sbuf", [128, 15 * 128], "float16"), "DG": ("sbuf", [128, 6 * 384], "float16"), "CD": ("sbuf", [128, 3 * 384], "float16"),
    "MH": ("sbuf", [128, 36 * 128], "float16"), "MB": ("sbuf", [128, 4 * 128 + 16], "bfloat16"),
    "G3": ("sbuf", [128, 72], "float16"), "GW": ("sbuf", [128, 7 * 24], "float16"),
    "IR": ("sbuf", [128, 128], "bfloat16"), "GM": ("sbuf", [128, 128], "bfloat16"),
    "CI": ("sbuf", [128, 8], "int32"), "CF": ("sbuf", [128, 96], "float32"),
    "LMi": ("sbuf", [128, 8], "int32"), "LMh": ("sbuf", [128, 8], "float16"),
    "ACC": ("sbuf", [128, 24], "float32"), "P1": ("sbuf", [128, 8 * 42], "float32"), "SM": ("sbuf", [128, 64], "float32"),
    "PR": ("sbuf", [128, 112], "float32"), "G8": ("sbuf", [128, 8], "float32"), "WH": ("sbuf", [128, 8], "float16"),
    "X1": ("sbuf", [128, 16], "float32"), "X2": ("sbuf", [128, 48], "float32"), "X3": ("sbuf", [128, 96], "float32"),
    "YO": ("sbuf", [128, 384], "float32"),
    "PF0": ("psum", [128, H], "float32"), "PF1": ("psum", [128, H], "float32"),
    "PA": ("psum", [128, 512], "float32"), "PB": ("psum", [128, 512], "float32"),
    "PC": ("psum", [128, 512], "float32"), "PD": ("psum", [128, 512], "float32"),
}
SEMAPHORES = (["cv", "cs", "cp", "cg", "out", "a1", "a2", "a3", "r3", "ow", "wa", "w1", "wb", "tc1", "tc2", "tp", "fall", "lm", "oi"]
              + [k + x for k in ("a", "r", "s", "own") for x in "AFBCOY"] + ["tu%d" % d for d in EV]
              + [k % d for k in ("ft%d", "fh%d", "y%d") for d in POS])


def top(d):
    return 1 << (d.bit_length() - 1)


def bits(engines):
    return sum(1 << e for e in engines)


def plan(T, topo):
    cores = list(T.cores)
    teams = [[r for r in range(N) if r == 0 or topo.may_write(cores[0], cores[r])]]
    teams.append([r for r in range(N) if r not in teams[0]])
    layer = {r: 4 * t + i for t in range(2) for i, r in enumerate(teams[t])}
    ports = {}
    for r in range(N):
        far = teams[1 - layer[r] // 4]
        p = [c for c in topo.cores_of(cores[r]) if c != cores[r] and all(topo.may_write(c, cores[x]) for x in far)]
        same, other = ([c for c in p if (topo.die(c) == topo.die(cores[r])) == k] for k in (True, False))
        ring = [same[0], other[0], same[1], other[1]]
        ports[r] = ([ring[(i + layer[r]) % 4] for i in range(4)], same[:2])
    return cores, teams, layer, ports


def dst(topo, to, frm):
    rid, pid = topo.addr(to, frm)
    return DstId(rid=rid, pnc=pid)


def relay_program(g, core, T, topo, cores, layer, a, x, xs):
    en = topo.engines(core, cores[x])
    s = 12 * layer[a]
    steps = [(m, len(en) // (2 if m == "F" else 4), [x], T["ld" + m][0], T["ld" + m][layer[a] if m in "OY" else a]) for m in "AFBCOY"]
    if xs:
        steps.append(("3", len(topo.engines(cores[a], core)), xs, T.X3[:, 0:12], T.X3[:, s:s + 12]))
    for m, n, to, src, out in steps:
        g.wait_ge(T.sem["r" + m], n)
        g.remote_dma_fused([RemoteDMATransfer(dst_ids=[dst(topo, cores[k], core) for k in to], dma_engine_mask=bits(en), remote_sem=T.sem["a" + m],
                                              src=src, dsts=[out for k in to])], local_sem=T.sem.out)
    g.wait_ge(T.sem.out, len(steps) * len(en))


def rank_program(g, core, T, topo):
    cores, teams, layer, ports = plan(T, topo)
    me = T.rank_of(core)
    if me is None:
        for a in range(N):
            if core in ports[a][0]:
                far = teams[1 - layer[a] // 4]
                relay_program(g, core, T, topo, cores, layer, a, far[ports[a][0].index(core)],
                              far[ports[a][1].index(core)::2] if core in ports[a][1] else [])
        return
    lay = layer[me]
    team = lay // 4
    near = [r for r in teams[team] if r != me]
    far = teams[1 - team]
    Q = {"v": g.vector, "s": g.scalar, "p": g.tensor, "g": g, "y": g.sync}
    ops, wr, rd, users, phys = [], {}, {}, {}, {}
    hold = []
    pools = {"b": [(T[x], 0) for x in ("PA", "PB", "PC", "PD")], "f": [(T.PF0, 0), (T.PF1, 0)],
             "G": [(T.GB, 1056 * i) for i in range(NG)], "m": [(T.MX, H * i) for i in range(NM)], "c": [(T.CT, 0), (T.CT, 384)],
             "r": [(T.RA, 0), (T.RB, 0)], "R": [(T.RS, 0)]}

    def new(pool):
        k = "%s#%d" % (pool, len(users)); users[k] = []
        return k

    def step(e, R, W, busy, late, issue, sem=None):
        deps = set(wr[k] for k in R + W if k in wr)
        for k in W:
            deps |= set(rd.get(k, []))
        i = len(ops)
        hard = set(deps)
        deps |= set(wr[k] for k in hold)
        del hold[:]
        ops.append(dict(e=e, tag=(W or [""])[-1], next=[], deps=deps, hard=hard, busy=busy, late=late, issue=issue, sem=sem, takes=[k for k in W if users.get(k) == []]))
        for k in R:
            rd.setdefault(k, []).append(i)
        for k in W:
            wr[k] = i; rd[k] = []
        for k in set(R + W):
            if k in users:
                users[k].append(i)

    def part(k, a, b, s=1, rows=128):
        return (k, a, b, s, rows)

    def ap(x):
        if isinstance(x, tuple):
            t, o = phys[x[0]]
            return t[0:x[4], o + x[1]:o + x[2]:x[3]] if x[3] > 1 else t[0:x[4], o + x[1]:o + x[2]]
        return x

    def do(e, R, W, n, call):
        step(e, R, W, max(64, n) * CYCLE, 0.0, lambda q: [call(q)])

    def dma(e, s, R, W, pairs, kb, rows):
        step(e, R, W, 0.1 * len(pairs), (kb, rows), lambda q: [Q[q].dma_start(o, i) for o, i in pairs], s)

    sent = [0]

    def send(R, W, items, busy=0.3):
        def issue(q):
            g.remote_dma_fused([RemoteDMATransfer(dst_ids=[dst(topo, c, core) for c in cs], dma_engine_mask=bits(en), remote_sem=T.sem[s],
                                                  src=src, dsts=[out for c in cs]) for cs, en, s, src, out in items], local_sem=T.sem.out)
            return []
        sent[0] += sum(len(it[1]) for it in items)
        step("g", R, W + ["gq"], busy, 0.0, issue, "out")

    def arrive(s, n, R, W, late):
        step("net", R, W, 0.0, late, n, s)

    vv, sc, pe = g.vector, g.scalar, g.tensor

    def ts(R, W, o, i, s1, s2, op0, op1=None, n=64):
        if op1 is None:
            do("v", R, W, n, lambda q: vv.tensor_scalar(ap(o), ap(i), ap(s1), None, op0))
        else:
            do("v", R, W, n, lambda q: vv.tensor_scalar(ap(o), ap(i), ap(s1), ap(s2), op0, op1))

    def tt(R, W, o, a, b, op, n=64):
        do("v", R, W, n, lambda q: vv.tensor_tensor(ap(o), ap(a), ap(b), op))

    def cp(R, W, o, i, e="v", n=64):
        do(e, R, W, n, lambda q: vv.tensor_copy(ap(o), ap(i)) if q == "v" else sc.activation(ap(o), ap(i), AF.Copy))

    def fill(W, o, n):
        do("v", [], W, n, lambda q: vv.memset(o, 0))

    def mm(R, W, items, n, beside=False):
        first = wr.get(W[0])
        step("p", R, W, n * CYCLE / 2, 0.0, lambda q: [pe.matmul(ap(o), ap(l), ap(r), a, z) for o, l, r, a, z in items])
        if beside:
            ops[-1]["hard"].discard(first)

    def group(out, terms):
        return [(out, l, r, j == 0, j == len(terms) - 1) for j, (l, r) in enumerate(terms)]

    def blk(t, i, n=1, w=128):
        return part(t, i * w, (i + n) * w) if isinstance(t, str) else t[:, i * w:(i + n) * w]

    def best_order():
        if "bias" not in MEMO:
            MEMO["bias"] = order
            MEMO["plan"] = plan_ = refine(dict(LONG["v"], **LONG["s"], **SENDS))
            MEMO["all"] = (ops, users, pools, body[0])
        _, seq, extra, where = order(None, MEMO["plan"][1])
        if "force" in MEMO:
            seq, extra, slots_ = MEMO["force"]
            where = {k: pools[k[0]][x] for k, x in slots_.items()}
        MEMO["seq"] = seq
        phys.update(where)
        for i, more in extra.items():
            ops[i]["hard"] = ops[i]["hard"] | more
        return seq

    def refine(starts):
        t = order(starts)[0]
        best, due = (t, MEMO["due"]), MEMO["latest"]
        for k in range(PASSES):
            t = order(None, due)[0]
            if t is None:
                break
            best = min(best, (t, due))
            due = [MIX * a + (1.0 - MIX) * b for a, b in zip(MEMO["latest"], due)]
        (now, due), seed = best, SEED
        sets = [[i] for i in range(body[0], len(ops)) if "name" not in ops[i]] + 3 * [list(range(named[k], last[k] + 1)) for k in last]
        for k in range(TRIES):
            new_ = list(due)
            for _ in range(2):
                seed = (seed * 1103515245 + 12345) % 2147483648
                for i in sets[(seed >> 3) % len(sets)]:
                    new_[i] += ((seed >> 14) % 1000) / 1000.0 * 2 * MOVE - MOVE
            t = order(None, new_)[0]
            if t is not None and t <= now + SLACK * (1.0 - k / TRIES):
                now, due = t, new_
                best = min(best, (t, due))
        return best

    def order(bias, given=None):
        n = len(ops); extra, where, since = {}, {}, {}
        after = [[] for _ in ops]
        for i, o in enumerate(ops):
            for d in o["deps"]:
                after[d].append(i)
        span = lambda o: o["busy"] + (2.0 + o["late"][0] / RATE if isinstance(o["late"], tuple) else o["late"]) + WAKE
        behind = {}
        for i, o in enumerate(ops):
            if "next" in o:
                behind.setdefault(o["next"], []).append(i)
        left = [len(o["deps"]) + ("next" in o) for o in ops]
        line = [i for i in range(n) if not left[i]]
        for i in line:
            for j in after[i] + behind.get(i, []):
                left[j] -= 1
                if not left[j]:
                    line.append(j)
        due = given or [bias[o["name"]] + o.get("into", 0.0) if "name" in o else bias.get(o["sem"], END) for o in ops]
        for again in (() if given else (0, 1)):
            for i in line[::-1]:
                due[i] = min([due[i]] + [due[j] - span(ops[i]) for j in after[i]] + [due[j] - ops[i]["busy"] for j in behind.get(i, [])])
            for k, v in users.items():
                for i in v[1:]:
                    due[i] = min(due[i], due[v[0]] + KEEP.get(k[0], END))
        rank = [-x for x in due]
        left = [len(o["deps"]) + ("next" in o) for o in ops]
        ready = [i for i in range(n) if not left[i]]
        end, free, pipe, seq, start = {}, {}, [0.0], [], {}
        slots = {p: [None] * len(v) for p, v in pools.items()}
        open_ = {k: len(v) for k, v in users.items()}
        uses = {}
        for k, v in users.items():
            for i in v:
                uses.setdefault(i, []).append(k)
        while ready:
            cand = []
            for i in ready:
                o = ops[i]; got = []
                if i not in since:
                    since[i] = max([end[d] + WAKE for d in o["deps"]] + [due[i] - SOON if o["e"] == "p" and o["takes"] and i >= body[0] else 0.0])
                t = since[i]
                for k in o["takes"]:
                    fr = [(max(end[u] for u in users[h]) if h else 0.0, x) for x, h in enumerate(slots[k[0]]) if h is None or not open_[h]]
                    if not fr:
                        break
                    got.append((k, min(fr)[1])); t = max(t, min(fr)[0] + WAKE)
                else:
                    for q in (o["e"] if o["e"] == "vs" else [o["e"]]):
                        cand.append((max(t, free.get(q, 0.0)) if q != "net" else t, q, i, got))
            if not cand:
                return None, None, None, None
            t0, q0 = min((c[0], c[1]) for c in cand)
            worth = lambda c: rank[c[2]] + (SMALL if ops[c[2]]["busy"] < 0.6 else 0.0) - IDLE * (c[0] - t0) - (SHY if c[1] == "v" and ops[c[2]]["e"] == "vs" else 0.0)
            t, q, i, got = max([c for c in cand if c[1] == q0 and c[0] <= t0 + LOOK], key=worth)
            o = ops[i]; ready.remove(i)
            for k, x in got:
                h = slots[k[0]][x]
                if h:
                    extra[i] = extra.get(i, set()) | set(users[h])
                slots[k[0]][x] = k; where[k] = pools[k[0]][x]
            free[q] = t + o["busy"]; start[i] = t
            if isinstance(o["late"], tuple):
                pipe[0] = max(pipe[0], t + 1.8) + o["late"][0] / RATE + o["late"][1] * 0.002
                end[i] = pipe[0]
            else:
                end[i] = free[q] + o["late"]
            for k in uses.get(i, []):
                open_[k] -= 1
            seq.append((i, q))
            for j in after[i] + behind.get(i, []):
                left[j] -= 1
                if not left[j]:
                    ready.append(j)
        MEMO["end"] = stop = max(end.values())
        latest, then, waits = [0.0] * n, {}, [list(a) for a in after]
        for i, more in extra.items():
            for j in more:
                waits[j].append(i)
        for i, q in seq[::-1]:
            took = end[i] - start[i] + WAKE
            latest[i] = min([stop - took] + [latest[j] - took for j in waits[i]] + [latest[j] for j in behind.get(i, [])]
                            + ([then[q] - ops[i]["busy"]] if q in then and q != "net" else []))
            then[q] = latest[i]
        MEMO["latest"], MEMO["due"] = latest, due
        MEMO["log"] = [(q, round(end[i], 1), ops[i].get("name") or ops[i]["sem"] or ops[i]["W"]) for i, q in seq]
        return max(end.values()) + EARLY * sum(end[i] for i in range(n) if ops[i]["e"] == "net"), seq, extra, where

    def arrange():
        n = len(ops); extra, since = {}, {}
        after, behind = [[] for _ in ops], [[] for _ in ops]
        for i, o in enumerate(ops):
            for d in o["deps"]:
                after[d].append(i)
            for d in o["next"]:
                behind[d].append(i)
        span = lambda o: o["busy"] + (2.0 + o["late"][0] / RATE if isinstance(o["late"], tuple) else o["late"]) + WAKE
        left = [len(o["deps"]) + len(o["next"]) for o in ops]
        line = [i for i in range(n) if not left[i]]
        for i in line:
            for j in after[i] + behind[i]:
                left[j] -= 1
                if not left[j]:
                    line.append(j)
        assert len(line) == n, [ops[i]["tag"] for i in range(n) if left[i]][:20]
        rank = [0.0] * n
        for i in line[::-1]:
            rank[i] = max([span(ops[i]) + rank[j] for j in after[i]] + [ops[i]["busy"] + rank[j] for j in behind[i]] + [span(ops[i])])
        left = [len(o["deps"]) + len(o["next"]) for o in ops]
        ready = [i for i in range(n) if not left[i]]
        end, free, pipe, seq = {}, {}, 0.0, []
        slots = {p: [None] * len(v) for p, v in pools.items()}
        open_ = {k: len(v) for k, v in users.items()}
        uses = {}
        for k, v in users.items():
            for i in v:
                uses.setdefault(i, []).append(k)
        while ready:
            cand = []
            for i in ready:
                o = ops[i]; got = []
                if i not in since:
                    since[i] = max([end[d] + WAKE for d in o["deps"]] + [0.0])
                t = since[i]
                for k in o["takes"]:
                    fr = [(max(end[u] for u in users[h]) if h else 0.0, x) for x, h in enumerate(slots[k[0]]) if h is None or not open_[h]]
                    if not fr:
                        break
                    got.append((k, min(fr)[1])); t = max(t, min(fr)[0] + WAKE)
                else:
                    cand.append((max(t, free.get(o["e"], 0.0)) if o["e"] != "net" else t, o["e"], i, got))
            assert cand, ([ops[i]["tag"] for i in ready], [[ops[u]["tag"] for u in users[h]] for h in slots["b"]], seq[-1])
            t0, q0 = min((c[0], c[1]) for c in cand)
            t, q, i, got = max([c for c in cand if c[1] == q0 and c[0] <= t0 + LOOK], key=lambda c: rank[c[2]] - IDLE * (c[0] - t0))
            o = ops[i]; ready.remove(i)
            for k, x in got:
                h = slots[k[0]][x]
                if h:
                    extra[i] = extra.get(i, set()) | set(users[h])
                slots[k[0]][x] = k; phys[k] = pools[k[0]][x]
            free[q] = t + o["busy"]
            if isinstance(o["late"], tuple):
                pipe = end[i] = max(pipe, t + 1.8) + o["late"][0] / RATE + o["late"][1] * 0.002
            else:
                end[i] = free[q] + o["late"]
            for k in uses.get(i, []):
                open_[k] -= 1
            seq.append((i, q))
            for j in after[i] + behind[i]:
                left[j] -= 1
                if not left[j]:
                    ready.append(j)
        MEMO.update(end=max(end.values()), all=(ops, users, pools, body[0]), seq=seq,
                    log=[(q, round(end[i], 1), ops[i]["sem"] or ops[i]["tag"]) for i, q in seq])
        if "force" in MEMO:
            seq, extra, slots_ = MEMO["force"]
            phys.update({k: pools[k[0]][x] for k, x in slots_.items()})
        for i, more in extra.items():
            ops[i]["hard"] = ops[i]["hard"] | more
        return seq

    def emit(seq):
        count, seen, tok = {}, {}, {}
        total = {}
        for o in ops:
            if isinstance(o["late"], tuple):
                total[o["sem"]] = total.get(o["sem"], 0) + 16 * int(round(o["busy"] * 10))
        for i, q in seq:
            o = ops[i]
            if q == "net":
                tok[i] = (o["sem"], o["issue"]); count[o["sem"]] = o["issue"]
                continue
            want = {}
            for d in o["hard"]:
                if tok[d]:
                    want[tok[d][0]] = max(want.get(tok[d][0], 0), tok[d][1])
            for s, k in want.items():
                if seen.get((q, s), 0) < k:
                    Q[q].wait_ge(T.sem[s], k); seen[q, s] = k
            s = o["sem"] or "c" + q
            for ins in o["issue"](q):
                ins.then_inc(T.sem[s], 16 if o["sem"] else 1); count[s] = count.get(s, 0) + (16 if o["sem"] else 1)
            tok[i] = None if s == "out" else (s, total.get(s, count[s]))
        count["out"] = sent[0]
        for s, k in count.items():
            g.wait_ge(T.sem[s], k)

    MAPS = {"A": (2, 3), "B": (1, 4, 5, 6), "C": (7, 0)}

    def rows(kind, d):
        m = [m for m in MAPS if d in MAPS[m]][0]
        k, n = MAPS[m].index(d), 128 // len(MAPS[m])
        return T[kind + m][:, n * k:n * k + n, :]

    half = lambda t, h: t[:, 64 * h:64 * h + 64, :]
    dma("y", "sA", [], ["sA"], [(rows("st", d), blk(T.mp, d - 1)) for d in MAPS["A"]], 128, 256)
    dma("y", "sF", [], ["sF"], [(half(T.stF, h), T.ft[:, H * h:H * h + H]) for h in (0, 1)], 512, 256)
    dma("y", "sB", [], ["sB"], [(rows("st", d), blk(T.mp, d - 1)) for d in MAPS["B"]], 256, 512)
    dma("y", "sC", [], ["sC"], [(rows("st", 7), blk(T.mp, 6))] + [(T.stC[k, 64, 0:7], T.lam[k // 4]) for k in range(N)]
        + [(T.stC[:, 64, 7:32], T.mp[0:8, 0:25]), (T.stC[:, 65:128, :], T.mp[0:32, 0:504])], 128, 200)
    do("g", [], ["pi0", "gq"], 130, lambda q: g.iota(T.CI[:, 0:1], [[0, 1]], 0, 1))
    do("g", [], ["IR"], 400, lambda q: g.iota(T.IR[:], [[1, 128]], 0, 0, allow_small_or_imprecise_dtypes=True))
    do("g", [], ["GM"], 400, lambda q: g.iota(T.GM[:], [[16, 8], [0, 16]], 0, 0, allow_small_or_imprecise_dtypes=True))
    off = topo.engines(core, cores[near[0]])
    on = [e for e in topo.engines(core, ports[me][0][0]) if e not in off]
    nof, q4 = len(off), len(off) // 4

    def spread(m, keys, slot, busy=0.3):
        st, ld = T["st" + m], T["ld" + m]
        of = (lambda x: x) if m in "OY" else (lambda x: layer[x])
        en, k = (on + off, 2 * q4) if m == "F" else (on, q4)
        out = [([ports[me][0][i]], en[k * i:k * i + k], "r" + m, st[of(x)], ld[0]) for i, x in enumerate(far)]
        inside = [([cores[x]], off[q4 * i:q4 * i + q4], "a" + m, st[of(x)], ld[slot]) for i, x in enumerate(near)]
        for items in ((out, inside) if m == "F" else (out + inside,)):
            send(keys, ["sent" + m], items, busy)
        dma("y", "own" + m, keys, ["own" + m], [(ld[slot], st[of(me)])], 48, 16)

    for m in "AFBC":
        spread(m, ["s" + m], me, 3.0 if m == "A" else 0.3)
        arrive("a" + m, 3 * q4 + 4 * nof, ["sent" + m], ["ld" + m], ARRIVE[m])
    dma("y", "ow", ["sC"], ["OWi"], [(blk(T.OWi, i), blk(T.mp, d - 1)) for i, d in enumerate(OD)], 192, 384)
    fill(["TC"], T.TC[:], V)
    fill(["TP"], T.TP[:], H)

    CF = T.CF
    IR, GM = T.IR, T.GM
    G8 = GM[:, 0:128:16]
    for j in range(3):
        ts(["pi0"], ["ci%d" % j], T.CI[:, 1 + j:2 + j], T.CI[:, 0:1], 4 + j, 1, A.logical_shift_right, A.bitwise_and)
    ts(["pi0"], ["ci3"], T.CI[:, 4:5], T.CI[:, 0:1], 15, None, A.bitwise_and)
    ts(["pi0"], ["ci4"], T.CI[:, 5:6], T.CI[:, 0:1], 1, 7, A.logical_shift_right, A.bitwise_and)
    ts(["pi0"], ["ci5"], T.CI[:, 6:7], T.CI[:, 0:1], 1, None, A.bitwise_and)
    cp(["pi0"] + ["ci%d" % j for j in range(6)], ["c0"], CF[:, 0:7], T.CI[:, 0:7])
    XO, PX, SC, GX, QM, IS, EX = 8, 16, 24, 32, 40, 56, 64
    col = lambda base, i: CF[:, base + i:base + i + 1]
    tb = {1: 0, 2: 1, 4: 2}
    isr = lambda d: col(IS, tb[top(d)])
    isj = lambda d: col(1, tb[top(d)])
    ts(["c0"], ["xo0"], col(XO, 0), col(0, 0), 0.0, None, A.mult)
    for j in range(3):
        ts(["c0"], ["xo%d" % (1 << j)], col(XO, 1 << j), col(1, j), -32.0 * (1 << j), 16.0 * (1 << j), A.mult, A.add)
    ts(["c0"], ["isr"], CF[:, IS:IS + 3], CF[:, 1:4], -1.0, 1.0, A.mult, A.add)
    ts(["c0", "IR"], ["qm"], CF[:, QM:QM + 16], T.IR[:, 0:16], col(0, 4), None, A.is_equal)
    tt(["xo1", "xo2"], ["xo3"], col(XO, 3), col(XO, 1), col(XO, 2), A.add)
    ts(["xo1", "xo2", "xo3", "xo4"], ["xo5"], CF[:, XO + 5:XO + 8], CF[:, XO + 1:XO + 4], col(XO, 4), None, A.add)
    xo = ["xo%d" % i for i in range(6)]
    ts(xo + ["c0"], ["px"], CF[:, PX:PX + 8], CF[:, XO:XO + 8], col(0, 0), None, A.add)
    ts(["px"], ["gx"], CF[:, GX:GX + 8], CF[:, PX:PX + 8], col(0, 4), None, A.subtract)
    for i, (src, k) in enumerate(((isr(1), 128.0), (isr(1), -2047.0), (isj(1), 128.0), (isj(1), -2047.0))):
        ts(["isr", "c0"], ["sc%d" % i], col(SC, i), src, k, None, A.mult)
    for i, (q_, side) in enumerate(((2, isr), (1, isj), (1, isr), (2, isj))):
        tt(["isr", "qm"], ["sc%d" % (4 + i)], col(SC, 4 + i), col(QM, q_), side(1), A.mult)
    ts(["c0"], ["ex0"], col(EX, 0), col(0, 0), 16.0, None, A.mult)
    ts(["c0"], ["ex1"], col(EX, 1), col(0, 6), -32.0, 16.0, A.mult, A.add)
    tt(["ex0"], ["ex1"], col(EX, 1), col(EX, 1), col(EX, 0), A.add)
    ts(["c0"], ["ex2"], col(EX, 2), col(0, 5), 1.0, None, A.add)
    ts(["c0"], ["ex3"], CF[:, EX + 3:EX + 5], CF[:, 2:4], 2.0, None, A.add)
    ts(["isr"], ["ex5"], CF[:, EX + 5:EX + 7], CF[:, IS + 1:IS + 3], 2.0, None, A.add)
    ts(["c0"], ["one"], col(EX, 7), col(0, 0), 0.0, 1.0, A.mult, A.add)
    mats, used = {}, {"MH": 0, "MB": 0, "CD": 0, "ZH": 0, "ZF": 0}
    cols = ["px", "gx", "qm", "isr", "IR", "GM", "ex0", "ex1", "ex2", "ex3", "ex5"] + ["sc%d" % i for i in range(8)]

    def mat(name, buf, row, s1, s2, op0=A.is_equal, op1=A.mult, parts=128):
        o = 128 * used[buf]; used[buf] += 1
        mats[name] = (buf, o)
        ts(cols, [name], T[buf][0:parts, o:o + 128], row[0:parts, :], s1, s2, op0, op1)

    def M(name, parts=128):
        buf, o = mats[name]
        return T[buf][0:parts, o:o + 128]

    def zmat(name, x, pick, buf="ZH"):
        o = 8 * used[buf]; used[buf] += 1
        mats[name] = (buf, o)
        ts(cols, [name], T[buf][:, o:o + 8], G8, col(GX, x), pick, A.is_equal, A.mult)

    for i, side in enumerate("rj"):
        for x in (2, 3):
            mat("A%d%s" % (x, side), "MH", IR, col(PX, x), col(SC, 2 * i))
            mat("B%d%s" % (x, side), "MH", IR, col(PX, x), col(SC, 2 * i + 1))
    zmat("Zr1", 2, col(SC, 4)); zmat("Zr2", 3, col(SC, 5)); zmat("Zj1", 3, col(SC, 6)); zmat("Zj2", 2, col(SC, 7))
    mat("I16", "MH", IR, col(PX, 0), 1.0)
    for t in (1, 2, 4):
        mat("D%d" % t, "MH", IR, col(PX, 0), isr(t))
    for d in range(1, 8):
        mat("P%d" % d, "MH", IR, col(PX, d), isr(d))
    mat("I", "MB", IR, col(PX, 0), 1.0)
    mat("nI", "MB", IR, col(PX, 0), -1.0)
    mat("bD", "MB", IR, col(PX, 0), isr(1)); mat("bP", "MB", IR, col(PX, 1), isr(1))
    G2, nG2 = T.MB[:, 512:520], T.MB[:, 520:528]
    ts(cols, ["G2"], G2, G8, col(GX, 0), 2.0, A.is_equal, A.mult)
    ts(cols, ["nG2"], nG2, G8, col(GX, 0), -2.0, A.is_equal, A.mult)
    ts(cols, ["G8"], T.G8[:], G8, col(GX, 0), None, A.is_equal)
    for x in range(8):
        ts(cols, ["zx%d" % x], blk(T.ZX, x, 1, 8), G8, col(GX, x), None, A.is_equal)
    ts(cols, ["zx8"], blk(T.ZX, 8, 1, 8), G8, col(GX, 0), col(QM, 0), A.is_equal, A.mult)
    zx = ["zx%d" % x for x in range(9)]
    ts(zx + cols, ["ZC"], T.ZC[:], T.ZX[:, 16:64], col(EX, 2), None, A.mult)
    for t in (1, 2, 4):
        for k, s in enumerate((1.0, isr(t), isj(t))):
            ts(zx + cols, ["g3%d%d" % (t, k)], blk(T.G3, 3 * tb[t] + k, 1, 8), T.ZX[:, 0:8], s, None, A.mult)
    b = new("b")
    mm(zx, [b], [x for d in range(1, 8) for x in group(part(b, 8 * d - 8, 8 * d, rows=8), [(blk(T.ZX, 8, 1, 8), blk(T.ZX, k, 1, 8)) for k in (0, d)])], 128)
    cp([], [b, "PR"], T.PR[0:8, 0:56], part(b, 0, 56, rows=8))
    for i, d in enumerate(OD):
        for t in (0, 1):
            o = 56 + 2 * (2 * i + t)
            ts(["PR", "IR"], ["own%d%d" % (d, t)], T.PR[0:8, o:o + 2], IR[0:8, 0:2], float(t), T.PR[0:8, 8 * d - 8 + me:8 * d - 7 + me], A.is_equal, A.mult)
    mat("B0", "MH", GM, CF[0:8, EX:EX + 1], 1.0, parts=8)
    mat("B1", "MH", GM, CF[0:8, EX + 1:EX + 2], 1.0, parts=8)
    mat("BT", "MH", GM, 64.0, CF[0:8, 0:1], A.is_ge, A.is_equal, parts=8)
    for x in range(1, 8):
        mat("A%d" % x, "MH", IR, col(PX, x), 128.0)
        mat("B%d" % (10 + x), "MH", IR, col(PX, x), -2047.0)
    for q in (2, 4, 6, 1, 3, 5, 7, 8, 9):
        zmat("Z%d" % q, 1, col(QM, q))
    for t, codes in ((1, (1.0, 2.0, 3.0)), (2, (1.0, col(EX, 3), col(EX, 5))), (4, (1.0, col(EX, 4), col(EX, 6)))):
        for k, s in enumerate(codes):
            mat("cd%d%d" % (t, k), "CD", IR, col(PX, 0), s)
    slot = {"X1": (T.X1, 4 * (lay % 4), 4), "X2": (T.X2, 12 * (lay % 4), 12), "X3": (T.X3, 12 * lay, 12)}
    for k, (buf, s, w) in slot.items():
        fill([k], buf[:, s:s + w], w)
    cp(["OWi"], ["OW"], T.OW[:], T.OWi[:], n=384)

    LA, LF, LB, LC = ([k + m for k in ("ld", "own")] for m in "AFBC")
    dma("y", "wa", LA, ["WallA"], [(blk(T.Wall, d - 1), rows("ld", d)) for d in (2, 3)], 128, 256)
    dma("y", "tc1", LA, ["TC"], [(T.TC[d - 1:128:16, :], rows("ld", d)) for d in (2, 3)], 128, 16)
    dma("y", "fall", LF, ["Fall"], [(T.Fall[:, H * h:H * h + H], half(T.ldF, h)) for h in (0, 1)], 512, 256)
    dma("y", "w1", LB, ["Wall1"], [(blk(T.Wall, 0), rows("ld", 1))], 64, 128)
    dma("y", "lm", LC, ["LMi"], [(T.LMi[0:8, 0:7], T.ldC[:, 64, 0:7])], 0, 16)
    dma("y", "wb", LB + LC, ["WallB"], [(blk(T.Wall, d - 1), rows("ld", d)) for d in (4, 5, 6, 7)], 256, 512)
    cp(["Fall"], ["Fw"], T.Fall[:, V:V + 16], T.Fall[:, 0:16], "s")

    def runs(src, same):
        out, a = [], 0
        while a < N:
            b = a + 1
            while b < N and src(b) == src(b - 1) + 1 and same(a, b):
                b += 1
            out.append((a, b)); a = b
        return out

    def load_features(d):
        at, t = V + 16 + V * POS[d], top(d)
        if POS[d] < 3:
            fill(["FT%d" % d], T.Fall[:, at:at + V], H)
        else:
            cp(["TP"], ["FT%d" % d], T.Fall[:, at:at + V], T.TP[:], "s", n=V)
        ts(["IR"], ["of%d" % d], blk(T.OF, POS[d], 1, 66), IR[:, 0:66], 0.0, float(at), A.mult, A.add)
        same = lambda a, b: a & t == b & t
        if d == 1:
            dma("y", "ft1", LF, ["FT1"], [(T.Fall[16 * a:16 * a + 16, at + H * h:at + H * h + H], T.ldF[a + 1, 64 * h:64 * h + 64, :])
                                          for a in range(0, N, 2) for h in (0, 1)], 256, 128)
            dma("y", "fh1", LF, ["FH1a"], [(T.FH[:, 0:H], T.ldF[0:N:2])], 256, 128)
            b = new("b")
            mm(["Fall", "bD", "bP"], [b], group(part(b, 0, 16), [(M("bD"), T.Fall[:, H:H + 16]), (M("bP"), T.Fall[:, 0:16])]), 128)
            cp(["FH1a"], [b, "FH1"], T.FH[:, H:H + 16], part(b, 0, 16), "s")
            return
        dma("y", "ft%d" % d, ["Fall"], ["FT%d" % d],
            [(T.Fall[16 * a:16 * b, at:at + V], T.Fall[16 * (a ^ d):16 * ((a ^ d) + b - a), 0:V]) for a, b in runs(lambda a: a ^ d, same) if not a & t], 256, 64)
        r = lambda a: a ^ d if a & t else a
        pairs = []
        for a, b in runs(r, same):
            h = H if a & t else 0
            pairs.append((T.FH[16 * a:16 * b, 1040 * POS[d]:1040 * (POS[d] + 1)], T.Fall[16 * r(a):16 * (r(a) + b - a), h:h + 1040]))
        dma("y", "fh%d" % d, ["Fall", "Fw"], ["FH%d" % d], pairs, 260, 128)

    for d in POS:
        load_features(d)

    place = {}
    body = [len(ops)]

    def lists(items):
        b = new("b"); its = []; R = []
        first = len(place)
        for i, (d, c, buf, k, key) in enumerate(items):
            o, s = i * 66, k * 128
            place[d, c] = first + i
            its += [(part(b, o, o + 66), M("D%d" % top(d)), blk(T.OF, POS[d], 1, 66), True, False),
                    (part(b, o, o + 66), M("D%d" % top(d)), buf[:, s:s + 66], False, False),
                    (part(b, o, o + 64), M("P%d" % d), buf[:, s + 64:s + 128], False, False),
                    (part(b, o + 64, o + 66), M("P%d" % d), buf[:, s:s + 2], False, True)]
            R += [key, "D%d" % top(d), "P%d" % d, "of%d" % d]
        n = len(items) * 66
        mm(R, [b], its, 4 * n)
        cp([], [b] + ["FL%d_%d" % it[:2] for it in items], T.FL[:, first * 66:first * 66 + n], part(b, 0, n), n=n)

    def stored(out, key, n, terms, R):
        b = new("b")
        mm(R, [b], [x for o, w, t in terms for x in group(part(b, o, o + w), t)], sum(w * len(t) for o, w, t in terms))
        ts([], [b] + key, out, part(b, 0, n), float(2047 * HB), None, A.add, n=n)

    named, last = {}, {}

    def long_step(name):
        ops[-1]["tag"] = name

    def gather(name, R, key, out, win, offs, o, n, less=None):
        k = (ORDER["v"] + ORDER["s"]).count(name)
        cuts = [n // k // 2 * 2 * j for j in range(k)] + [n]
        for a, b in zip(cuts, cuts[1:]):
            first = wr.get(key) if a else None
            src = win.indirect(offs[:, o + a:o + b])
            if less is None:
                cp(R, [key], out(16 * a, 16 * b), src, "vs", n=16 * (b - a) * GATHER + 60)
            else:
                tt(R, [key], out(16 * a, 16 * b), src, less(16 * a, 16 * b), A.subtract, n=16 * (b - a) * GATHER + 60)
            ops[-1]["hard"].discard(first)
            long_step(name)

    def compose(name, win, slot, keys, row, out=None):
        gather(name, keys + ["SL%d" % slot], row, out or (lambda a, b: part(row, a, b)), T[win][:, 0:V], T.SL, 128 * slot, 128)

    def turn(name, items):
        b = new("b"); o = 0
        for row, z, n, R in items:
            mm(R, [b], [(part(b, o + s, o + 128 * n, 16), row(s), z, True, True) for s in range(16)], 1024, o > 0)
            o += 128 * n
        c = new("c")
        cp([], [b, c, name], part(c, 0, o), part(b, 0, o), n=o)
        return c

    def back(c, n):
        b = new("b")
        mm([c, "I16"], [b], [(blk(b, i), blk(c, i), M("I16"), True, True) for i in range(n)], 128 * n)
        return b

    def extract(name, row, zs):
        buf, o = mats[zs[0]]
        return turn(name, [(lambda s: part(row, s, V, 16), T[buf][:, o:o + 8 * len(zs)], len(zs), [row] + list(zs))])

    def take(b, i, n, out, keys, e="v"):
        cp([], [b] + keys, out, blk(b, i, n), e, n=128 * n)

    def judge(d, c):
        G = new("G")
        o, e = place[d, c] * 66, 3 * POS[d] + c
        win = T.Fall[:, 0:2 * V + 16 + V * POS[d]]
        R = ["Fall", "Fw", "FL%d_%d" % (d, c)] + ["FT%d" % x for x in POS if POS[x] <= POS[d]]
        fh = 1040 * POS[d]
        if "J%d%d" % (d, c) in ORDER["s"]:
            gather("J%d%d" % (d, c), R, G, lambda a, b: part(G, a, b), win, T.FL, o, 65)
            pf = new("f")
            two = [group(part(pf, k, k + 512), [(M("I"), T.FH[:, fh + k:fh + k + 512]), (M("nI"), T.FH[:, fh + k + 1:fh + k + 513]),
                                                (M("nI"), part(G, k, k + 512)), (M("I"), part(G, k + 1, k + 513))]) for k in (0, 512)]
            for j, (k, n) in enumerate(((0, 0), (1, 0), (0, 2), (1, 2))):
                mm(["I", "nI", G if n else "FH%d" % d], [pf], two[k][n:n + 2], H, j > 0)
            acc = T.ACC[:, e:e + 1]; src = part(pf, 0, H)
            do("vs", [], [pf, G, "sum%d" % e], H + 150,
               lambda q: vv.tensor_reduce(acc, ap(src), AxisListType.X, A.add, apply_absolute_value=True) if q == "v"
               else sc.activation(ap(part(G, 0, H)), ap(src), AF.Abs, accum_out=acc))
            long_step("A%d%d" % (d, c))
        else:
            gather("J%d%d" % (d, c), R + ["FH%d" % d], G, lambda a, b: part(G, a, b), win, T.FL, o, 65, lambda a, b: T.FH[:, fh + a:fh + b])
            m = new("m")
            do("v", [G], [m, "m%d%d" % (d, c)], H // 2, lambda q: vv.tensor_tensor_scan(ap(part(m, 0, H)), ap(part(G, 0, H)), ap(part(G, 1, H + 1)), 64.0, A.min, A.max))
            b = new("b")
            mm([G, m, "G2", "nG2"], [b], group(part(b, 0, 8), [(blk(G, k), nG2) for k in range(8)] + [(blk(m, k), G2) for k in range(8)]), H)
            cp([], [b, "sum%d" % e, "s%d%d" % (d, c)], blk(T.P1, e, 1, 8), part(b, 0, 8), "vs")

    def differ(b, i, k, other, keys, n=1):
        tt(keys, [b] + ["ne%d" % (k + j) for j in range(n)], blk(T.NE, k, n), blk(b, i, n), other, A.not_equal, n=128 * n)

    def counts(ds, terms):
        b = new("b"); its, R = [], []
        for i, d in enumerate(ds):
            for c, t in enumerate(terms(i)):
                o = 8 * (3 * i + c)
                its += group(part(b, o, o + 8), [(blk(T.NE, k), blk(T.GW, 3 * POS[d] + s, 1, 8)) for k, s in t])
                R += ["ne%d" % k for k, s in t] + ["GW%d" % d]
        mm(R, [b], its, 64 * len(its))
        n = 24 * len(ds); o = 8 * (21 + 3 * POS[ds[0]])
        cp([], [b, "cnt%d" % ds[0]], T.P1[:, o:o + n], part(b, 0, n), "vs", n=n)

    def ways(k):
        return lambda i: ([(k + i, 0)], [(k + i, 1), (k + 3 + i, 1)], [(k + i, 2), (k + 3 + i, 1)])

    def partial(ds, key):
        buf, s, w = slot[key]
        b = new("b")
        line = sorted([(d, c) for d in ds for c in range(3)], key=lambda x: x in LAST)
        for k, some in enumerate((line[:-2], line[-2:])):
            its, R = [], ["cnt%d" % ds[0], "one", "G8"]
            for d, c in some:
                e, o = 3 * POS[d] + c, 3 * ds.index(d) + c
                its += group(part(b, o, o + 1, rows=8),
                             [(blk(T.P1, 21 + e, 1, 8), col(EX, 7)),
                              (T.G8[:], T.ACC[:, e:e + 1]) if "J%d%d" % (d, c) in ORDER["s"] else (blk(T.P1, e, 1, 8), col(EX, 7))])
                R.append("sum%d" % e)
            mm(R, [b], its, 32 * len(its), k > 0)
        cp([], [b, key], buf[0:8, s:s + 3 * len(ds)], part(b, 0, 3 * len(ds), rows=8))
        return buf[:, s:s + w]

    def team_send(ds, sem, key):
        x = partial(ds, key)
        send([key], [sem], [([cores[k] for k in near], off, sem, x, x)])
        arrive(sem, 3 * nof, [sem], [key + "in"], HOP)

    def decide(key, terms, spreads, r=8):
        n = len(terms); buf = slot[key][0]; SM = T.SM
        b = new("b")
        its = [x for i, t in enumerate(terms) for x in group(part(b, 3 * i, 3 * i + 3, rows=r), [(m, buf[0:8, o:o + 3]) for m, o in t])]
        mm([key, key + "in", "PR"] + ["own%d%d" % (d, t) for d in OD for t in (0, 1)], [b], its, 4 * max(r, 3) * len(its))
        cp([], [b, "sc"], SM[0:r, 0:3 * n], part(b, 0, 3 * n, rows=r))
        s = lambda c: SM[0:r, c:3 * n:3] if n > 1 else SM[0:r, c:c + 1]
        tt(["sc"], ["ma"], SM[0:r, 16:16 + n], s(1), s(2), A.min)
        tt(["sc"], ["mb"], SM[0:r, 24:24 + n], s(0), s(1), A.min)
        tt(["sc", "ma"], ["wa"], T.WH[0:r, 0:n], SM[0:r, 16:16 + n], s(0), A.is_lt)
        tt(["sc", "mb"], ["wb"], T.WH[0:r, 4:4 + n], s(2), SM[0:r, 24:24 + n], A.is_lt)
        b = new("b")
        mm(["wa", "wb"] + spreads, [b],
           [x for k, m in enumerate(spreads) for x in group(part(b, n * k, n * k + n), [(M(m, r), T.WH[0:r, o:o + n]) for o in (0, 4)])], 128 * len(spreads))
        return b

    def pair(d):
        return T.PR[0:8, 8 * d - 8:8 * d]

    def diag(wb, i, t, k):
        ts(["cd%d%d" % (t, j) for j in range(3)], [wb, "dg%d" % k], blk(T.DG, k, 1, 384), blk(T.CD, tb[t], 1, 384), part(wb, i, i + 1), 1.0,
           A.subtract, A.is_equal, n=192)

    def pick(sets):
        b = new("b")
        mm(["dg%d" % k for k, t in sets] + [key for k, t in sets for _, key in t], [b],
           [x for i, (k, t) in enumerate(sets) for x in group(blk(b, i), [(blk(T.DG, 3 * k + j), src) for j, (src, _) in enumerate(t)])], 384 * len(sets))
        return b

    W = lambda d: blk(T.W16, d - 1)
    WK = lambda d: "W1" if d == 1 else "WA" if d < 4 else "WB"
    Hh = lambda d: blk(T.H16, d - 1)
    UP = {2: 0, 4: 1, 6: 2, 3: 3, 5: 4, 7: 5}
    U = lambda d: blk(T.UW, UP[d])
    TT = lambda d: blk(T.TW, UP[d])
    floor16 = lambda R, Wk, o, i, n: ts(R, Wk, o, i, 0.0625, HB - 0.46875, A.mult, A.add, n=n)

    cp(["WallA"], ["WA"], blk(T.W16, 1, 2), blk(T.Wall, 1, 2), n=256)
    floor16(["WA"], ["HA"], blk(T.H16, 1, 2), blk(T.W16, 1, 2), 128)
    for k, side in enumerate("rj"):
        ms = [m + side for m in ("A2", "B2", "A3", "B3")]
        stored(blk(T.SL, k), ["SL%d" % k], 128, [(0, 128, [(M(m), src) for m, src in zip(ms, (W(2), Hh(2), W(3), Hh(3)))])], ["WA", "HA"] + ms)
    cp(["Wall1"], ["W1"], W(1), blk(T.Wall, 0), n=128)
    cp(["WallB"], ["WB"], blk(T.W16, 3, 4), blk(T.Wall, 3, 4), n=512)
    floor16(["WB"], ["HB"], blk(T.H16, 3, 4), blk(T.W16, 3, 4), 256)
    lists([(1, 0, T.W16, 0, "W1")])
    lists([(2, 0, T.W16, 1, "WA"), (3, 0, T.W16, 2, "WA")])
    lists([(d, 0, T.W16, d - 1, "WB") for d in (4, 5, 6, 7)])
    for xs in ((2, 3), (4, 5, 6, 7)):
        stored(blk(T.SL, xs[0], len(xs)), ["SL%d" % x for x in xs], 128 * len(xs),
               [(128 * i, 128, [(M("A%d" % x), W(x)), (M("B%d" % (10 + x)), Hh(x))]) for i, x in enumerate(xs)],
               [WK(xs[0]), "HA" if xs[0] == 2 else "HB"] + [k % x for x in xs for k in ("A%d", "B1%d")])
    cp(["LMi"], ["LMh"], T.LMh[0:8, 0:7], T.LMi[0:8, 0:7])
    bw = new("b")
    mm(["B0", "LMh"], [bw], [(part(bw, 0, 7), M("B0", 8), T.LMh[0:8, 0:7], True, True)], 64)
    cp([], [bw, "w"], T.SM[:, 32:39], part(bw, 0, 7), "vs")
    for d in POS:
        ts(["w"] + ["g3%d%d" % (top(d), k) for k in range(3)], ["GW%d" % d], blk(T.GW, POS[d], 1, 24), blk(T.G3, tb[top(d)], 1, 24), T.SM[:, 31 + d:32 + d], None, A.mult)
    row = new("r")
    compose("Cr", "TC", 0, ["TC"], row)
    b = back(extract("cr", row, ["Zr1", "Zr2"]), 2)
    take(b, 0, 2, T.PW[:], ["PW"])
    lists([(1, 1, T.PW, 0, "PW"), (1, 2, T.PW, 1, "PW")])
    differ(b, 0, 0, W(1), ["W1"])
    differ(b, 1, 1, W(1), ["W1"])
    differ(b, 1, 2, blk(T.PW, 0), ["PW"])
    counts([1], lambda i: ([(0, 1), (1, 1)], [(0, 1), (2, 1)], [(1, 1), (2, 1)]))
    for c in range(3):
        judge(1, c)
    team_send((1,), "a1", "X1")
    row = new("r")
    compose("Cj", "TC", 1, ["TC"], row)
    dma("y", "tc2", LB + LC, ["TC"], [(T.TC[d - 1:128:16, :], rows("ld", d)) for d in (4, 5, 6, 7)], 256, 32)
    c = extract("cj", row, ["Zj1", "Zj2"])
    b = new("b")
    mm([c, "I16", "W1", "PW"], [b], group(blk(b, 0), [(M("I16"), W(1))])
       + [x for i in (0, 1) for x in group(blk(b, 1 + i), [(blk(c, i), M("I16")), (M("I16"), blk(T.PW, i))])], 640)
    take(b, 0, 3, blk(T.HL, 0, 3), ["HI"], "vs")
    tt(["HI"], [b, "LO"], blk(T.HL, 3, 3), blk(b, 0, 3), blk(T.HL, 0, 3), A.subtract, n=384)
    dma("y", "tp", ["HI", "LO"], ["TP"], [(T.TP[2 * c_ + h:128:16, :], blk(T.HL, 3 * h + c_)) for c_ in range(3) for h in (0, 1)], 192, 768)
    take(b, 0, 3, T.PK[:], ["PK"])
    floor16(["PK"], ["PH"], T.PH[:], T.PK[:], 192)
    stored(T.SV[:], ["SV"], 384, [(0, 384, [(M("A1"), T.PK[:]), (M("B11"), T.PH[:])])], ["PK", "PH", "A1", "B11"])
    for d in EV + OD:
        x = d ^ 1
        compose("T%d" % d, "TP", x, ["TP"], "TR%d" % d, lambda a, b, o=V * (x - 2): T.TR[:, o + a:o + b])
    for d in EV + OD:
        judge(d, 0)
    wb = decide("X1", [[(pair(1), 4 * k) for k in range(4)]], ["B0"])
    diag(wb, 0, 1, 0)
    ts(["ZC"], [wb, "ZT"], T.ZT[:], T.ZC[:], part(wb, 0, 1), 1.0, A.subtract, A.is_equal)
    b = pick([(0, [(blk(T.SV, j), "SV") for j in range(3)])])
    take(b, 0, 1, blk(T.SL, 8), ["SL8"])
    take(pick([(0, [(blk(T.PK, j), "PK") for j in range(3)])]), 0, 1, blk(T.OY, 0), ["pi"], "vs")

    def by_far(ds):
        o = lambda d: V * ((d ^ 1) - 2)
        c = turn("c%d" % ds[-1], [(lambda s, d=d: T.TR[:, o(d) + s:o(d) + V:16], blk(T.ZT, (d ^ 1) - 2, 1, 8), 1, ["ZT", "TR%d" % d]) for d in ds])
        b = back(c, len(ds))
        take(b, 0, len(ds), blk(T.TW, UP[ds[0]], len(ds)), ["T%d" % d for d in ds] + ["t%d" % ds[-1]])
        return b

    row = new("r")
    compose("U", "TC", 8, ["TC"], row)
    b = bu = back(extract("cu", row, ["Z2", "Z4", "Z6"]), 3)
    take(b, 0, 3, blk(T.UW, 0, 3), ["UE"])
    lists([(d, 1, T.UW, UP[d], "UE") for d in EV])
    for i, d in enumerate(EV):
        differ(b, i, 3 + i, W(d), [WK(d)])
    take(back(extract("co", row, ["Z1", "Z3", "Z5"]), 3), 0, 3, blk(T.UW, 3, 3), ["UO"])
    for i, d in enumerate(EV):
        b = by_far([d])
        lists([(d, 2, T.TW, i, "T%d" % d)])
        cp(["T%d" % d], ["wi%d" % d], blk(T.WI, i), TT(d), n=128)
        dma("y", "tu%d" % d, ["wi%d" % d, "UE"], ["TE%d" % d], [(T.TC[7 + i:128:16, :], blk(T.WI, i))], 64, 128)
    differ(bu, 0, 6, blk(T.TW, 0, 2), ["T2", "T4"], 2)
    differ(b, 0, 8, U(6), ["UE"])
    counts(EV, ways(3))
    for c in (1, 2):
        for d in EV:
            judge(d, c)
    team_send(EV, "a2", "X2")
    row = new("r")
    compose("E", "TC", 8, ["TC", "TE2", "TE4", "TE6"], row)
    take(back(extract("ce", row, ["Z7", "Z8", "Z9"]), 3), 0, 3, T.EW[:], ["EW"])
    by_far(OD)
    wb = decide("X2", [[(pair(d), 12 * k + 3 * i) for k in range(4)] for i, d in enumerate(EV)], ["B0", "B1"])

    for i, d in enumerate(OD):
        diag(wb, 3 + i, top(d), i)
    for i, d in enumerate(OD):
        diag(wb, i, top(d), 3 + i)
    e = lambda i: (blk(T.EW, i), "EW")
    w = lambda d: (W(d), WK(d))
    b = pick([(i, [(U(d), "UO"), w(d), e(i)]) for i, d in enumerate(OD)])
    take(b, 0, 3, blk(T.OM, 0, 3), ["NU"])
    lists([(d, 1, T.OM, i, "NU") for i, d in enumerate(OD)])
    for i, d in enumerate(OD):
        differ(b, i, 9 + i, W(d), [WK(d)])
    b = pick([(3 + i, [(TT(d), "T%d" % d), e(i), w(d)]) for i, d in enumerate(OD)])
    take(b, 0, 3, blk(T.OM, 3, 3), ["NT"])
    lists([(d, 2, T.OM, 3 + i, "NT") for i, d in enumerate(OD)])
    differ(b, 0, 12, blk(T.OM, 0, 3), ["NU"], 3)
    b = pick([(3 + i, [w(d), (U(d), "UE"), (TT(d), "T%d" % d)]) for i, d in enumerate(EV)])
    take(b, 0, 3, blk(T.OY, 1, 3), ["fin"], "vs")
    dma("y", "sO", ["NU", "NT"], ["sO"], [(T.stO[:], T.OM[:])], 192, 128)
    dma("y", "sY", ["pi", "fin"], ["sY"], [(T.stY[:, 32 * k:32 * k + 32, :], blk(T.OY, k)) for k in range(4)], 256, 512)
    for m in "OY":
        spread(m, ["s" + m], lay)
        arrive("a" + m, 3 * q4 + 4 * nof, ["sent" + m], ["ld" + m], 1.75 * HOP)
    dma("y", "oi", ["ldO", "ownO"], ["OI"], [(T.OI[:], T.ldO[:])], 192, 128)
    dma("y", "y1", ["ldY", "ownY"], [], [(blk(T.ym, d - 1), T.ldY[:, 32 * k:32 * k + 32, :]) for k, d in enumerate((1,) + EV)], 256, 512)
    counts(OD, ways(9))
    for c in (1, 2):
        for d in OD:
            judge(d, c)
    x = partial(OD, "X3")
    send(["X3"], ["r3"], [(ports[me][1], on + off, "r3", x, T.X3[:, 0:12])])
    send(["X3"], ["r3"], [([cores[k] for k in near], off, "a3", x, x)])
    arrive("a3", 7 * nof, ["r3"], ["X3in"], 1.45 * HOP)

    wb = decide("X3", [[(T.PR[0:8, 56 + 2 * (2 * i + k // 4):58 + 2 * (2 * i + k // 4)], 12 * k + 3 * i) for k in range(N)] for i in range(3)], ["BT"], 2)
    for i, d in enumerate(OD):
        diag(wb, i, 1, i)
    for i, d in enumerate(OD):
        two = [(blk(T.OI, i), "OI"), (blk(T.OI, 3 + i), "OI")]
        b = pick([(i, [(blk(T.OW, i), "OW")] + (two if me < me ^ d else two[::-1]))])
        take(b, 0, 1, blk(T.YO, i), ["y%d" % d], "vs")
        dma("ys"[i % 2], "y%d" % d, ["y%d" % d], [], [(blk(T.ym, d - 1), blk(T.YO, i))], 64, 128)
    for o in ops:
        for k in GATE.get(o["sem"], ()):
            o["deps"].add(wr[k]); o["hard"].add(wr[k])
    lines = {"y": [[i for i, o in enumerate(ops) if o["sem"] == s][0] for s in LOADS]}
    tagged = {}
    for i in range(body[0], len(ops)):
        o = ops[i]
        if o["e"] == "p":
            o["tag"] = [ops[j]["tag"] for j in users[o["tag"]] if ops[j]["e"] != "p"][0]
        if o["e"] in ("v", "s", "vs", "p") and not o["sem"]:
            tagged.setdefault((o["e"] == "p", o["tag"]), []).append(i)
    for q in ORDER:
        lines[q] = [tagged[q == "p", k].pop(0) for k in ORDER[q]]
        for i in lines[q]:
            ops[i]["e"] = q
    for line in lines.values():
        for i, j in zip(line, line[1:]):
            ops[j]["next"].append(i)
    if "p" not in ORDER:
      for k, v in users.items():
        if k[0] in "bf" and v[0] >= body[0]:
            i = [i for i in v if ops[i]["e"] != "p"][0]
            line = lines[ops[i]["e"]]
            ops[v[0]]["next"].append(line[max(0, line.index(i) - LEAD[k[0]])])
    emit(arrange())
